import numpy as np, ml_dtypes
CORES = [48,51,52,55]
N = 4
BF = ml_dtypes.bfloat16
def f(rng, *shape):
    return (rng.standard_normal(shape, dtype=np.float32) * np.exp2(rng.integers(-2, 3, shape[:-1] + (1,)))).astype(BF)
def wide(rng, *shape):
    v = f(rng, *shape).astype(np.float32); k = shape[:-2] + (1, shape[-1])
    return (v * np.exp2(rng.integers(-6, 7, k)) * (rng.random(k) > 0.0625)).astype(BF)
E, EP, A, AP, TY = 512, 128, 32, 8, 64
TR, M, SH = 2048, 2, 5
CAPP, CAPO, L = 640, 320, 1280
def vals(rng, v):
    return v
def held(ent, att, g):
    h = np.zeros(E * A, bool); h[(ent[:, g].astype(np.int64) * A + att[:, g]).reshape(-1)] = True
    return h
def places(cls, form, g):
    fo = form[:, g].reshape(N, TY, A)[np.arange(N)[:, None], cls[:, g]].reshape(E, A)
    return [np.arange(E)[:, None] * A + ((fo >> (SH * i)) & (A - 1)) for i in range(M)]
def present(ent, att, cls, form, g):
    h = held(ent, att, g); ok = np.ones((E, A), bool)
    for p in places(cls, form, g):
        ok = ok & h[p]
    return ok
def deal(rng):
    mean = TR // N; m = np.zeros((8, N, N), np.int64)
    for g in range(8):
        for r in range(N):
            o = rng.permutation(N); x = rng.integers(0, CAPP - mean + 1, N // 2); m[g, r, o[0::2]] = mean + x; m[g, r, o[1::2]] = mean - x
    return m
def triples(rng, m, late):
    ent = np.zeros((N, 8, TR), np.int32); att = np.zeros((N, 8, TR), np.int32)
    for g in range(8):
        mine = [[] for r in range(N)]
        for q in range(N):
            pri = rng.random((EP, A)) + late[g, q * EP:(q + 1) * EP, None]; pri[:, 0] = 9
            cuts = np.add.accumulate(m[g, :, q])
            k = rng.permutation(np.argsort(pri, axis=None)[:cuts[-1]]) + q * EP * A
            for r, part in enumerate(np.split(k, cuts[:-1])):
                mine[r].append(part)
        for r in range(N):
            k = rng.permutation(np.concatenate(mine[r])); ent[r, g] = k >> SH; att[r, g] = k & (A - 1)
    return ent, att
def formulas(rng, same):
    fs = rng.integers(1, A, (M, N, 8, TY * A)); fs = np.where(rng.random(fs.shape[1:]) < same, fs[:1], fs)
    return np.where(rng.random(fs.shape) < 0.015625, 0, fs)
def pack(fs):
    v = fs[0]
    for i in range(1, M):
        v = v + (fs[i] << (SH * i))
    return v.astype(np.int32)
def trim(rng, d, full=False):
    for g in range(8):
        ok = present(d["ent"], d["att"], d["cls"], d["form"], g).reshape(N, EP, A)
        for q in range(N):
            n = np.zeros((TY, A), np.int64); np.add.at(n, d["cls"][q, g], ok[q].astype(np.int64))
            for c in range(N):
                w = n[:, c * AP:(c + 1) * AP].reshape(-1)
                if np.sum(w) <= CAPO:
                    continue
                o = rng.permutation(TY * AP)
                if full:
                    o = o[np.argsort(-w[o], kind="stable")]
                s = 0; w = w.tolist()
                for i in o.tolist():
                    if s + w[i] > CAPO:
                        d["form"][q, g, (i // AP) * A + c * AP + (i & (AP - 1))] = 0
                    else:
                        s += w[i]
    return d
def setup_inputs(rng):
    ent, att = triples(rng, deal(rng), np.zeros((8, E)))
    d = {"val": vals(rng, f(rng, N, 128, TR)), "ent": ent, "att": att, "cls": rng.integers(0, TY, (N, 8, EP)).astype(np.int32), "form": pack(formulas(rng, 0.0625))}
    return trim(rng, d)
def setup_inputs_full(rng):
    d = setup_inputs(rng); m = np.zeros((8, N, N), np.int64); crowd = int(rng.integers(8)); odd = int(rng.integers(N))
    for g in range(8):
        s = int(rng.integers(N))
        for r in range(N):
            rest = TR
            for i in range(N):
                o = r + s + i
                if g == crowd:
                    o = s - i if r == odd else s + i
                c = min(CAPP, rest); m[g, r, o % N] = c; rest -= c
    d["ent"], d["att"] = triples(rng, m, np.zeros((8, E)))
    d["cls"] = rng.permuted(np.tile(np.arange(EP) % TY, (N, 8, 1)), axis=2).astype(np.int32)
    fs = np.zeros((M, N, 8, TY * A), np.int64)
    for g in range(8):
        h = held(d["ent"], d["att"], g).reshape(N, EP, A)
        for q in range(N):
            o = np.argsort(np.sum(h[q], axis=1), kind="stable"); rep = np.zeros(TY, np.int64); rep[d["cls"][q, g][o]] = o
            fs[:, q, g] = np.argmax(rng.random((M, TY, A, A)) * h[q][rep][None, :, None, :], axis=3).reshape(M, -1)
    d["form"] = pack(fs); return trim(rng, d, True)
def setup_inputs_ragged(rng):
    d = setup_inputs(rng)
    late = np.stack([np.concatenate([rng.permutation(np.repeat(np.array([-1.0, 0.0, 0.0, 1.0]), EP // 4)) for q in range(N)]) for g in range(8)])
    d["ent"], d["att"] = triples(rng, deal(rng), late); fo = pack(formulas(rng, 0.0625)).reshape(N, 8, TY, A)
    for g in range(8):
        for c in range(N):
            fo[:, g, :, c * AP + int(rng.integers(AP))] = 0
        q, c = int(rng.integers(N)), int(rng.integers(N)); fo[q, g, :, c * AP:(c + 1) * AP] = 0
    d["form"] = np.ascontiguousarray(fo.reshape(N, 8, TY * A)); return trim(rng, d)
def setup_inputs_one(rng):
    d = setup_inputs(rng); d["cls"] = np.repeat(rng.integers(0, TY, (N, 8, 1)), EP, axis=2).astype(np.int32)
    k = np.sort(d["ent"] * A + d["att"], axis=2); k[1::2] = k[1::2, :, ::-1].copy()
    d["ent"] = (k >> SH).astype(np.int32); d["att"] = (k & (A - 1)).astype(np.int32)
    d["form"] = pack(formulas(rng, 0.5)); return trim(rng, d)
def setup_inputs_spread(rng):
    d = setup_inputs(rng); d["val"] = vals(rng, wide(rng, N, 128, TR)); return d
def check_inputs(d):
    bad = []
    for name, lo, hi in (("ent", 0, E), ("att", 1, A), ("cls", 0, TY), ("form", 0, A ** M)):
        if not ((d[name] >= lo) & (d[name] < hi)).all():
            bad.append("range of " + name)
    if not (np.abs(d["val"].astype(np.float32)) < 2.0 ** 100).all():
        bad.append("finite")
    if bad:
        return bad
    ent, att = d["ent"], d["att"]
    for g in range(8):
        if np.count_nonzero(held(ent, att, g)) != N * TR:
            bad.append("distinct triples")
        if max(int(np.bincount(ent[r, g] // EP, minlength=N).max()) for r in range(N)) > CAPP:
            bad.append("triples of a rank for an owner")
        if np.sum(present(ent, att, d["cls"], d["form"], g).reshape(N, EP, N, AP), axis=(1, 3)).max() > CAPO:
            bad.append("derived cells of a pair of owners")
    return sorted(set(bad))
def reference(val, ent, att, cls, form):
    y = np.zeros((N, 128, L), BF); who = np.full((N, 8, L), -1, np.float32); cnt = np.zeros((N, 8, AP), np.float32)
    for g in range(8):
        cell = np.zeros((E * A, 16), np.float32)
        for r in range(N):
            cell[ent[r, g].astype(np.int64) * A + att[r, g]] = val[r, 16 * g:16 * g + 16].T.astype(np.float32)
        ps = places(cls, form, g); ok = present(ent, att, cls, form, g)
        new = cell[ps[0]] - cell[ps[1]]
        for p in ps[2:]:
            new = new + cell[p]
        for c in range(N):
            o = np.ascontiguousarray(ok[:, c * AP:(c + 1) * AP].T); a, e = np.nonzero(o); n = len(e)
            y[c, 16 * g:16 * g + 16, :n] = new[e, c * AP + a].T.astype(BF); who[c, g, :n] = e; cnt[c, g] = np.sum(o, axis=1)
    return {"y": y, "who": who, "cnt": cnt}

@@ -1,0 +1,390 @@
+import math
+from concourse.bass import DstId, RemoteDMATransfer
+from concourse.mybir import AluOpType, AxisListType, ActivationFunctionType
+
+A_ = AluOpType
+F_ = ActivationFunctionType
+SH = 12288
+NV1, NG, NB1 = 1536, 4096, 8192
+LSPLIT = 112
+LN2 = math.log(2.0)
+
+SCRATCH = {"vl": ("dram", [4, 128, 512], "bfloat16")}
+for _d, _l in (
+        ("bfloat16", "win:28672 vw:8192 vs:2048 ph:256 tt:256 tl:256 pw:16 pay:2048 one:128 zt:128 c128:128 one8:64 N1:128 cn:256 "
+                     "FS:528 I1:128 I99:128 I2k:128 MW:144 NW:128 RW:128 Hm:144 FW:512 FG:512 Fe:512 sg:512 W:1024 PC:512 pt:1024 "
+                     "ht:1024 lt:1024 mg:512 pres:256 junk:1280 LK:2560 t2:1280 Y:1280 YL:1280"),
+        ("int32", "ei:128 ai:128 fi:128 ct:32 k0:128 f12:256 h12:256 pi:8 pb:16 n1:512 n2:512 s1:256 s2:256 v1:256 v2:256 u1:80 u2:400"),
+        ("float32", "cf:32 cT:32 k2:128 k3:128 k4:128 k5:128 hx:256 pf:16 pc:16 J:224 iA:128 iB:128 iX:32 iC:144 CZ:128 wS:128 "
+                    "iE:256 iS:80 i4:8 m3:4 lm:4 dm:8 q1:128 q2:128 Q:128 b1:16 b2:16 bb:16 Z:224 S128:80 TB:16 ab:512 P:1024 Ts:512 "
+                    "o32:256 GW:520 v0:256 keep:256 X:256 acc:8 Gt:240 g1:560 zp:320 c8:16 cd:4 zc:4 u3:400 wt:128 wT:128 wL:128"),
+        ("float16", "Ep:144 E:144 z:512 U:8192"),
+        ("uint16", "ks:160 kl:160 gl:16 ll:160 lo:160")):
+    for _e in _l.split():
+        SCRATCH[_e.split(":")[0]] = ("sbuf", [128, int(_e.split(":")[1])], _d)
+for _j in range(7):
+    SCRATCH["B%d" % _j] = ("psum", [128, 512], "float32")
+SEMAPHORES = ("pv ps pe pg lkey lcls lform zero lval lown wrp wrh unw lwin akey aform aval awho ay0 ay1 ay2 ay3 "
+              "skey sform sval swho sy0 sy1 sy2 sy3 who1 who2 st0 st1 st2 st3").split()
+
+
+def rank_program(g, core, T, topo):
+    k = T.rank_of(core)
+    if k is None:
+        return
+    cores = T.cores
+    others = [(k + 1) % 4, (k + 2) % 4, (k + 3) % 4]
+    Q = {"v": g.vector, "s": g.scalar, "t": g.tensor, "g": g, "y": g.sync}
+    count, wrote, read = {}, {}, {}
+    seen = {q: {} for q in Q}
+
+    def wait(q, s, n):
+        if seen[q].get(s, 0) < n:
+            Q[q].wait_ge(T.sem[s], n)
+            seen[q][s] = n
+
+    def deps(q, r, w, own):
+        toks = []
+        for key in r:
+            toks += wrote.get(key, [])
+            if key[0] == "B":
+                toks += [t for t in read.get(key, []) if t[0] != own]
+        for key in w:
+            toks += [t for t in wrote.get(key, []) + read.get(key, []) if t[0] != own]
+        for s in sorted(set(t[0] for t in toks)):
+            wait(q, s, max(t[1] for t in toks if t[0] == s))
+
+    def note(s, r, w):
+        for key in r:
+            read.setdefault(key, []).append((s, count[s]))
+        for key in w:
+            wrote.setdefault(key, []).append((s, count[s]))
+
+    def op(q, r, w, f, *a, **kw):
+        s = {"v": "pv", "s": "ps", "t": "pe", "g": "pg"}[q]
+        deps(q, r.split(), w.split(), s)
+        count[s] = count.get(s, 0) + 1
+        f(*a, **kw).then_inc(T.sem[s], 1)
+        note(s, r.split(), w.split())
+
+    def dmas(s, r, w, items):
+        for q in sorted(set(it[0] for it in items)):
+            deps(q, r.split(), w.split(), None)
+        for q, o, i in items:
+            Q[q].dma_start(o, i).then_inc(T.sem[s], 16)
+        count[s] = 16 * len(items)
+        note(s, r.split(), w.split())
+
+    def send(s, rsem, r, items):
+        deps("g", [r], [], None)
+        trs = []
+        for d, src, dst, lo, hi in items:
+            rid, pid, _ = topo.addr(cores[d])
+            m = sum(1 << e for e in topo.engines(core, cores[d])[lo:hi])
+            trs.append(RemoteDMATransfer(dst_ids=[DstId(rid=rid, pnc=pid)], dma_engine_mask=m, remote_sem=T.sem[rsem], src=src, dst=dst))
+            count[s] = count.get(s, 0) + hi - lo
+        g.remote_dma_fused(trs, local_sem=T.sem[s])
+        note(s, [r], [])
+
+    def arrives(s, n, w):
+        count[s] = n
+        note(s, [], [w])
+
+    V, S = g.vector, g.scalar
+
+    def ts1(r, w, o, i, s, o0):
+        op("v", r, w, V.tensor_scalar, o, i, s, None, o0)
+
+    def ts2(r, w, *a):
+        op("v", r, w, V.tensor_scalar, *a)
+
+    def tt(r, w, *a):
+        op("v", r, w, V.tensor_tensor, *a)
+
+    def cp(r, w, *a):
+        op("v", r, w, V.tensor_copy, *a)
+
+    def tr(r, w, *a):
+        op("v", r, w, V.transpose, *a)
+
+    def act(r, w, o, i, f=F_.Copy, **kw):
+        op("s", r, w, S.activation, o, i, f, **kw)
+
+    def mm(r, w, *a):
+        op("t", r, w, g.tensor.matmul, *a)
+
+    def iota(w, o, pat, base=0):
+        op("g", "", w, g.iota, o, pat, base, 0, allow_small_or_imprecise_dtypes=True)
+
+    def sel(r, w, *a):
+        op("g", r, w, g.affine_select, *a)
+
+    def c_(name, a, n):
+        return T[name][:, a:a + n]
+
+    def clear(a, b):
+        for a0 in range(a, b, 2048):
+            act("pay", "bots", c_("win", a0, 2048), T.pay[:], F_.Identity, scale=0.0)
+
+    win = T.win
+    AND, SHR, MUL, ADD, SUB, EQ, MAX, GT, GE = (A_.bitwise_and, A_.logical_shift_right, A_.mult, A_.add, A_.subtract, A_.is_equal,
+                                                A_.max, A_.is_gt, A_.is_ge)
+    dmas("lkey", "", "ei ai", [it for kk in range(4) for it in (("y", c_("ei", kk * 32, 32), T.ent[2 * kk:2 * kk + 2, :]),
+                                                               ("s", c_("ai", kk * 32, 32), T.att[2 * kk:2 * kk + 2, :]))])
+    dmas("lcls", "", "ct", [("ys"[j & 1], T.ct[(j >> 1) * 32 + (j & 1):(j >> 1) * 32 + 32:2, :], T.cls[(j >> 2)::2, :]) for j in range(8)])
+    dmas("lform", "", "fi", [("ys"[kk & 1], c_("fi", kk * 32, 32), T.form[2 * kk:2 * kk + 2, :]) for kk in range(4)])
+
+    p0 = c_("pi", 0, 1)
+    op("g", "", "pi", g.iota, p0, [[0, 1]], 0, 1)
+    iota("iX", c_("iX", 0, 16), [[1, 4], [0, 4]])
+    iota("iX", c_("iX", 16, 16), [[0, 4], [32, 4]])
+    iota("iB", T.iB[:], [[0, 4], [1, 32]])
+    iota("iA", T.iA[:], [[16, 4], [0, 32]])
+    iota("one8", T.one8[:], [[0, 4], [-1, 2], [0, 8]], 1)
+    iota("FS", c_("FS", 0, 16), [[0, 16]])
+    for j in range(8):
+        sel("one8", "FS", c_("FS", 16 + j * 64, 64), T.one8[:], [[-16, 2], [0, 2], [-1, 16]], EQ, 0.0,
+            -64 * (j & 1) - 32 * (j >> 2) - 8 * ((j >> 1) & 1), 1)
+    op("v", "", "wz1", V.memset, c_("win", SH, NV1), 0.0)
+    dmas("zero", "wz1", "wrow", [("y", win[x::16, 16384:16384 + SH], c_("win", SH + x * 384, SH // 16)) for x in range(3)])
+    act("wz1", "wz3", c_("win", SH + NV1, NV1), c_("win", SH, NV1))
+    act("wz1", "wz3", win[:, SH + 2 * NV1:16384], win[:, SH:16384 - 2 * NV1])
+    pb = [c_("pb", j, 1) for j in range(7)]
+    pf = [c_("pf", j, 1) for j in range(7)]
+    pc = [c_("pc", j, 1) for j in range(10)]
+    for j, (sh, m) in enumerate(((0, 15), (4, 3), (0, 1), (0, 64), (0, 3), (2, 3), (0, 0x70))):
+        ts2("pi", "pb", pb[j], p0, sh, m, SHR, AND)
+    cp("pb", "pf", c_("pf", 0, 7), c_("pb", 0, 7))
+    ts1("iB pf", "m3", c_("m3", 0, 3), c_("iB", 0, 3), pf[0], EQ)
+    ts1("pf", "pc0", pc[0], pf[1], 4.0, MUL)
+    ts2("pf", "pc1", pc[1], pf[2], 256.0, 64.0 * k, MUL, ADD)
+    m0, m1, m2 = c_("m3", 0, 1), c_("m3", 1, 1), c_("m3", 2, 1)
+    ts1("iA m3", "q1", T.q1[:], T.iA[:], m0, MUL)
+    ts1("iB m3", "q2", T.q2[:], T.iB[:], m1, MUL)
+    ts2("iX m3 pc0", "b1", T.b1[:], c_("iX", 0, 16), pc[0], m0, ADD, MUL)
+    ts2("iX m3", "b2", T.b2[:], c_("iX", 16, 16), m1, m2, MUL, ADD)
+    tt("q1 q2", "Q", T.Q[:], T.q1[:], T.q2[:], ADD)
+    tt("b1 b2", "bb", T.bb[:], T.b1[:], T.b2[:], ADD)
+    for x in range(16):
+        act("Q bb", "pay", T.pay[:, x::16], T.Q[:], F_.Identity, bias=c_("bb", x, 1))
+    clear(NG, NG + 2048)
+
+    ts1("ei", "k0", T.k0[:], T.ei[:], 2, SHR)
+    ts1("ei", "k2", T.k2[:], T.ei[:], 32.0, MUL)
+    ts1("k0", "k3", T.k3[:], T.k0[:], -16383.0 / 128, MUL)
+    tt("k2 ai", "k4", T.k4[:], T.k2[:], T.ai[:], ADD)
+    ts1("ct pc1", "cf", T.cf[:], T.ct[:], pc[1], ADD)
+    tt("k3 k4", "k5", T.k5[:], T.k4[:], T.k3[:], ADD)
+    tr("cf", "cT", T.cT[:], T.cf[:])
+    for nm, key, ks in (("ks", "ks", others), ("kl", "klown", [k])):
+        for kk in ks:
+            ts1("k5", key, c_(nm, kk * 40, 32), c_("k5", kk * 32, 32), 128.0, MUL)
+        for kk in ks:
+            cp("cT", key, c_(nm, kk * 40 + 32, 8), c_("cT", kk * 8, 8))
+    send("skey", "akey", "ks", [(d, c_("ks", d * 40, 40), c_("kl", k * 40, 40), 4 * j, 4 * j + 4) for j, d in enumerate(others)])
+    arrives("akey", 12, "klrem")
+    ts1("fi", "h12", c_("h12", 0, 128), T.fi[:], 1, AND)
+    ts2("fi", "h12", c_("h12", 128, 128), T.fi[:], 5, 1, SHR, AND)
+    ts1("fi", "f12", c_("f12", 0, 128), T.fi[:], 31, AND)
+    ts1("h12", "hx", T.hx[:], T.h12[:], 199.0, MUL)
+    ts1("fi", "f12", c_("f12", 128, 128), T.fi[:], 5, SHR)
+    tt("hx f12", "ph", T.ph[:], T.hx[:], T.f12[:], ADD)
+    tr("ph", "tt", T.tt[:], T.ph[:])
+    send("sform", "aform", "tt", [(d, c_("tt", f * 128 + d * 32, 32), c_("tl", (k * 2 + f) * 32, 32), 4 * j + 2 * f, 4 * j + 2 * f + 2)
+                                  for j, d in enumerate(others) for f in range(2)])
+    arrives("aform", 12, "tlrem")
+    for f in range(2):
+        act("tt", "tlown", c_("tl", (k * 2 + f) * 32, 32), c_("tt", f * 128 + k * 32, 32))
+    clear(NG + 2048, NB1)
+    iota("J", T.J[:], [[1, 224]])
+    iota("iC", c_("iC", 0, 16), [[0, 16]], 999)
+    iota("iC", c_("iC", 16, 128), [[64, 2], [0, 4], [1, 16]])
+    iota("zt", T.zt[:], [[0, 128]])
+    iota("one", T.one[:], [[0, 128]], 1)
+    dmas("lval", "ks", "vs", [("y", c_("vs", d * 512, 512), T.val[32 * d:32 * d + 32, :]) for d in others])
+    send("sval", "aval", "vs", [(d, c_("vs", d * 512, 512), T.vl[k], (0, 4, 8)[j], (4, 8, 16)[j]) for j, d in enumerate(others)])
+    arrives("aval", 16, "vl")
+
+    def windows(s, r, rs):
+        dmas(s, r, s, [("y", T.vw[c * 32:c * 32 + 32, q * 2048:q * 2048 + 2048], T.val[32 * k:32 * k + 32, :] if q == k else T.vl[q])
+                       for q in rs for c in range(4)])
+    for nm, c in (("I1", 1.0), ("I99", -99.5), ("I2k", 2048.0)):
+        sel("zt", nm, T[nm][:], T.zt[:], [[-1, 128]], A_.not_equal, c, 0, 1)
+    iota("c128", T.c128[:], [[0, 128]], 128)
+    iota("cn", T.cn[:], [[0, 256]], -2048)
+    sel("c128", "N1", T.N1[:], T.c128[:], [[-16, 8], [0, 16]], GE, 0.0, 0, 1)
+    iota("o32", T.o32[:], [[0, 256]], 1)
+    sel("N1", "NW", T.NW[:], T.N1[:], [[16, 8], [0, 16]], GE, 0.0, 15, -1)
+    iota("GWp", c_("GW", 0, 1), [[0, 1]])
+    iota("GWp", c_("GW", 257, 1), [[0, 1]])
+    sel("NW", "RW", T.RW[:], T.NW[:], [[-1, 128]], GE, 0.0, 0, 1)
+    iota("i4", T.i4[:], [[4, 8]], 1)
+    iota("iS", T.iS[:], [[16, 20], [320, 4]])
+    iota("iE", T.iE[:], [[0, 8], [128, 32]])
+    for a in range(0, NG, 2048):
+        iota("botg", c_("win", a, 2048), [[0, 2048]])
+    iota("wt", T.wt[:], [[0, 128]])
+    sel("o32", "CZ", c_("CZ", 0, 80), c_("o32", 0, 80), [[-32, 4], [-1, 20]], EQ, 0.0, 0, 1)
+    sel("o32", "CZ", c_("CZ", 80, 48), c_("o32", 0, 48), [[-1000, 48]], EQ, 0.0, -20, 1)
+    act("pf", "pw", c_("pw", 0, 1), pf[0], F_.Exp, scale=LN2, bias=LN2)
+    act("pw", "pc9", pc[9], c_("pw", 0, 1))
+
+    for r in [k] + others:
+        op("v", "tab pay " + ("klown" if r == k else "klrem"), "wz1 wz3 wrow tab", V.tensor_copy,
+           c_("win", SH, 16384).indirect(c_("kl", r * 40, 32)), c_("pay", r * 512, 512))
+    dmas("wrp", "tab", "pt", [("y", c_("pt", u * 256, 256), win[u * 16 + 2::64, SH:SH + 16384]) for u in range(4)])
+
+    for j in range(16):
+        y, q, t5 = j >> 3, (j >> 1) & 3, j & 1
+        for f in range(2):
+            mm("FS tlown tlrem", "B5", c_("B5", j * 32, 32), c_("FS", (t5 * 2 + y) * 128 + 16 - 8 * f, 128), c_("tl", (q * 2 + f) * 32, 32),
+               f == 0, f == 1)
+    act("B5", "FW", T.FW[:], T.B5[:])
+    for q in range(4):
+        act("FW klown klrem", "FG", c_("FG", q * 128, 128), T.FW[:].indirect(c_("kl", q * 40 + 32, 8)))
+    tr("FG", "Fe", T.Fe[:], T.FG[:])
+    act("Fe", "W0", c_("W", 0, 512), T.Fe[:], F_.Exp, scale=-LN2 / 2, bias=-LN2)
+    act("Fe", "ab", T.ab[:], T.Fe[:], F_.Abs, bias=-200.0)
+    act("ab", "W1", c_("W", 512, 512), T.ab[:], F_.Exp, scale=-LN2 / 2, bias=-LN2)
+    act("Fe", "sg", T.sg[:], T.Fe[:], F_.Sign, bias=-100.0)
+    tt("pf", "pc2", pc[2], pf[3], pf[1], ADD)
+    ts2("pf", "pc6", pc[6], pf[5], 32.0, -99.5, MUL, ADD)
+    ts2("iC pc2 pc9", "MW", T.MW[:], T.iC[:], pc[2], pc[9], EQ, MUL)
+    ts2("pf", "pc6", pc[7], pf[4], 32.0, -99.5, MUL, ADD)
+    ts1("pf", "pc3", pc[3], pf[6], 15.0, ADD)
+    ts2("pf", "pc4", pc[4], pf[3], 0.25, pf[0], MUL, ADD)
+    ts2("pf", "pc8", pc[8], pf[4], 20.0, pf[5], MUL, ADD)
+    ts1("J pc3", "Ep", T.Ep[:], c_("J", 0, 144), pc[3], EQ)
+    ts2("J pc4", "Z", T.Z[:], T.J[:], -96.0, pc[4], ADD, EQ)
+    tt("Ep", "E", c_("E", 0, 143), c_("Ep", 0, 143), c_("Ep", 1, 143), SUB)
+    ts2("m3", "pc5", pc[5], m0, 128.0, m1, MUL, ADD)
+    ts1("J pf", "lm", T.lm[:], c_("J", 0, 4), pf[1], EQ)
+    ts2("J pc3 pc5", "Hm", T.Hm[:], c_("J", 0, 144), pc[3], pc[5], EQ, MUL)
+
+    M = c_("B0", 0, 64)
+    mm("one", "B0", M, T.one[0:1, :], T.one[0:1, 0:64], True, False)
+    for j in range(16):
+        u, xb = j >> 2, j & 3
+        mm("MW pt", "B0", M, c_("MW", 16 - 4 * xb, 128), T.pt[:, u * 256 + xb:u * 256 + 256:4], False, j == 15)
+    dmas("wrh", "tab pt", "ht", [("y", c_(("ht", "lt")[h], u * 256, 256), win[u * 16 + h::64, SH:SH + 16384]) for h in range(2) for u in range(4)])
+    for j in range(16):
+        mm("I1 Fe", "B5", c_("B5", j * 32, 32), T.I1[:], T.Fe[:, j::16], True, False)
+        mm("I99 sg", "B5", c_("B5", j * 32, 32), T.I99[:], T.sg[:, j::16], False, True)
+    for f in range(2):
+        act("B5 pc6", "PC", c_("PC", f * 256, 256), c_("B5", f * 256, 256), F_.Identity, bias=pc[6 + f])
+    for j in range(16):
+        tt("W0 W1 B0", "P", T.P[:, j::16], T.W[:, j::16], M, MUL)
+    tt("P", "Ts", T.Ts[:], c_("P", 0, 512), c_("P", 512, 512), ADD)
+    ts1("Ts", "n1", T.n1[:], T.Ts[:], -0.5, ADD)
+    ts1("n1", "n2", T.n2[:], T.n1[:], 1, AND)
+    for al in range(8):
+        tt("n2", "pres", c_("pres", al * 32, 32), T.n2[:, al::16], T.n2[:, 8 + al::16], MUL)
+    mm("NW pres", "B1", c_("B1", 0, 256), T.NW[:], T.pres[:], True, True)
+    mm("RW pres", "B1", c_("B1", 256, 256), T.RW[:], T.pres[:], True, True)
+    for f in range(2):
+        o = c_("B2", f * 256, 256)
+        mm("I1 PC", "B2", o, T.I1[:], c_("PC", f * 256, 256), True, False)
+        mm("one cn", "B2", o, T.one[0:1, :], T.cn[0:1, :], False, False)
+        mm("I2k pres", "B2", o, T.I2k[:], T.pres[:], False, True)
+    for j in range(8):
+        mm("I1 ht", "B6", c_("B6", (j >> 2) * 256, 256), T.I1[:], c_(("ht", "lt")[j >> 2], (j & 3) * 256, 256), j & 3 == 0, j & 3 == 3)
+    clear(NB1, SH)
+    act("B6", "mg", T.mg[:], T.B6[:])
+    act("iE", "B4", c_("B4", 0, 256), T.iE[:])
+    windows("lown", "ht", [k])
+    dmas("unw", "mg", "tab botg bots lk", [("y", win[c * 32 + h:c * 32 + 32:16, 0:16384], c_("mg", h * 256, 256))
+                                           for c in range(4) for h in range(2)])
+    windows("lwin", "vl", others)
+    ts2("i4 pc8", "TB0", c_("TB", 8, 8), T.i4[:], pc[8], 2048.0, ADD, MUL)
+    ts2("iS pf", "S128", T.S128[:], T.iS[:], pf[0], 128.0, ADD, MUL)
+    ts1("TB0", "TB", c_("TB", 0, 8), c_("TB", 8, 8), -64.0, ADD)
+    incl = c_("GW", 258, 256)
+    op("v", "o32 B1", "GWi", V.tensor_tensor_scan, incl, T.o32[:], c_("B1", 0, 256), 0.0, MUL, ADD)
+    tt("GWi B1", "s1", T.s1[:], incl, c_("B1", 256, 256), SUB)
+    for j in range(5):
+        act("GWi TB", "acc", c_("junk", j * 256, 255), c_("GW", 258, 255), F_.Sign, scale=-1.0, bias=c_("TB", j, 1), accum_out=c_("acc", j, 1))
+    ts1("s1", "s2", T.s2[:], T.s1[:], 0x780, AND)
+    for f in range(2):
+        tt("s2 B2", "z", c_("z", f * 256, 256), T.s2[:], c_("B2", f * 256, 256), ADD)
+    for j in range(16):
+        ts2("z", "U%d" % j, c_("U", j * 512, 512), T.z[:], -128.0 * j, 0.0, ADD, MAX)
+        mm("Ep E U%d" % j, "B3", T.B3[:], c_("Ep" if j == 0 else "E", 15 - j, 128), c_("U", j * 512, 512), j == 0, j == 15)
+    for j, c in enumerate((128.5, 127.5, 385.5)):
+        ts2("acc", "gl", c_("gl", 5 * j, 5), c_("acc", 0, 5), 0.5, c, MUL, ADD)
+    ts1("B3", "v0", T.v0[:], c_("B3", 256, 256), 4096.0, MUL)
+    tt("B3 v0", "v1", T.v1[:], T.v0[:], c_("B3", 0, 256), ADD)
+    ts1("v1", "v2", T.v2[:], T.v1[:], 0x7F07F, AND)
+    ts1("v2", "keep", T.keep[:], T.v2[:], 0.0, EQ)
+    tt("v2 B4", "X", T.X[:], T.v2[:], c_("B4", 0, 256), ADD)
+    op("v", "keep X", "GWf", V.tensor_tensor_scan, c_("GW", 1, 256), T.keep[:], T.X[:], 0.0, MUL, MAX)
+    cp("GWf GWi GWp gl", "Gt", T.Gt[:], c_("GW", 0, 514).indirect(c_("gl", 0, 15)))
+    g1 = [c_("g1", j * 80, 80) for j in range(7)]
+    tt("Gt S128", "g0", g1[0], c_("Gt", 160, 80), T.S128[:], SUB)
+    tt("Gt", "g1", g1[1], c_("Gt", 80, 80), c_("Gt", 0, 80), SUB)
+    ts1("g0", "g2", g1[2], g1[0], 2048.0, GT)
+    ts1("g0", "g3", g1[3], g1[0], 0.0, GT)
+    tt("g1 g2", "g4", g1[4], g1[1], g1[2], MUL)
+    tt("Gt g3", "g5", g1[5], c_("Gt", 0, 80), g1[3], MUL)
+    tt("g4 g5", "g6", g1[6], g1[4], g1[5], ADD)
+    for d in range(4):
+        ts1("g6 lm", "zp", c_("zp", d * 80, 80), g1[6], c_("lm", d, 1), MUL)
+    for c in range(4):
+        mm("Z zp", "B0", c_("B0", 0, 80), c_("Z", 96 - 32 * c, 128), T.zp[:, c::4], c == 0, c == 3)
+    ts2("J pf", "dm", T.dm[:], c_("J", 0, 8), pf[0], 1.0 / 128, EQ, MUL)
+    tt("GWi GWp", "c8", c_("c8", 0, 8), T.GW[:, 289:514:32], T.GW[:, 257:482:32], SUB)
+    tt("c8 dm", "c9", c_("c8", 8, 8), c_("c8", 0, 8), T.dm[:], MUL)
+    op("v", "c9", "cd", V.tensor_reduce, c_("cd", 0, 1), c_("c8", 8, 8), AxisListType.X, ADD)
+    ts1("cd lm", "zc", T.zc[:], T.lm[:], c_("cd", 0, 1), MUL)
+    u1 = T.u1[:]
+    u2 = [c_("u2", j * 80, 80) for j in range(5)]
+    u3 = [c_("u3", j * 80, 80) for j in range(5)]
+    lw = c_("win", 0, 16384)
+    cp("B0", "u1", u1, c_("B0", 0, 80))
+    ts1("u1", "a0", u2[0], u1, 5, SHR)
+    ts1("u1", "a1", u2[1], u1, 31, AND)
+    cp("a0", "ll2", c_("ll", 0, 80), u2[0])
+    act("ll2 lk", "LKa", c_("LK", 0, 1280), lw.indirect(c_("ll", 0, 80)))
+    ts2("u1", "a2", u2[2], u1, 5, 0x307F, SHR, AND)
+    ts1("a1", "c0", u3[0], u2[1], 128.0, MUL)
+    ts2("u1", "a3", u2[3], u1, 5, 127, SHR, AND)
+    tt("c0 a2", "c1", u3[1], u3[0], u2[2], ADD)
+    mm("Z zc", "B1", c_("B1", 0, 4), c_("Z", 96, 128), T.zc[:], True, True)
+    ts1("u1", "a4", u2[4], u1, 17, SHR)
+    cp("c1", "ll1", c_("ll", 80, 80), u3[1])
+    act("ll1 lk", "LKb", T.LK[:, 1280:16 * LSPLIT], lw.indirect(T.ll[:, 80:LSPLIT]))
+    ts1("u1", "c2", u3[2], u1, 0.0, EQ)
+    ts1("a3", "c3", u3[3], u2[3], 4.0, MUL)
+    tt("a4 c2", "c4", u3[4], u2[4], u3[2], SUB)
+    cp("B1", "wt", T.wt[:, 20::32], c_("B1", 0, 4))
+    for d in range(4):
+        tt("c3 c4", "wt", c_("wt", d * 32, 20), c_("u3", 240 + d * 20, 20), c_("u3", 320 + d * 20, 20), ADD)
+    tr("wt", "wT", T.wT[:], T.wt[:])
+    cp("ll1 lk", "LKc", T.LK[:, 16 * LSPLIT:2560], lw.indirect(T.ll[:, LSPLIT:160]))
+    for x in range(16):
+        mm("Hm LKa", "B6", c_("B6", 0, 80), c_("Hm", 15 - x, 128), T.LK[:, x:1280:16], x == 0, x == 15)
+    mm("CZ wT", "B2", c_("B2", 0, 128), T.CZ[:], T.wT[:], True, True)
+    act("B2", "wS", T.wS[:], c_("B2", 0, 128))
+    send("swho", "awho", "wS", [(d, c_("wS", d * 32, 32), c_("wL", k * 32, 32), 4 * j, 4 * j + 4) for j, d in enumerate(others)])
+    arrives("awho", 12, "wL")
+    for s, nm, ks in (("who1", "wS", [k]), ("who2", "wL", others)):
+        dmas(s, nm, "", [it for kk in ks for g_ in (2 * kk, 2 * kk + 1)
+                         for it in (("y", T.who[g_:g_ + 1, :], T[nm][0:80, g_ * 16:g_ * 16 + 16]),
+                                    ("y", T.cnt[g_:g_ + 1, :], T[nm][80:81, g_ * 16:g_ * 16 + 8]))])
+    for x in range(16):
+        mm("Hm LKb LKc", "B3", c_("B3", 0, 80), c_("Hm", 15 - x, 128), T.LK[:, 1280 + x::16], x == 0, x == 15)
+    cp("B6", "lo2", c_("lo", 0, 80), c_("B6", 0, 80))
+    cp("B3", "lo1", c_("lo", 80, 80), c_("B3", 0, 80))
+    for d in others + [k]:
+        act("lo2 lown lwin", "t2%d" % d, c_("t2", d * 320, 320), T.vw[:].indirect(c_("lo", d * 20, 20)))
+        tt("lo1 lown lwin t2%d" % d, "Y%d" % d, c_("Y", d * 320, 320), T.vw[:].indirect(c_("lo", 80 + d * 20, 20)),
+           c_("t2", d * 320, 320), SUB)
+        if d != k:
+            send("sy%d" % d, "ay%d" % k, "Y%d" % d, [(d, c_("Y", d * 320, 320), c_("YL", k * 320, 320), 0, 16)])
+    for r in others:
+        arrives("ay%d" % r, 16, "YL%d" % r)
+    for r in [k] + others[::-1]:
+        nm = "Y" if r == k else "YL"
+        dmas("st%d" % r, nm + str(r), "", [("ys"[c & 1], T.y[32 * r:32 * r + 32, c * 320:c * 320 + 320],
+                                            T[nm][c * 32:c * 32 + 32, r * 320:r * 320 + 320]) for c in range(4)])
+    for s in count:
+        wait("g", s, count[s])

@@ -4,28 +4,27 @@ from concourse.mybir import AluOpType, AxisListType, ActivationFunctionType
 
 A_ = AluOpType
 F_ = ActivationFunctionType
-SH = 12288
+SH = 13312
 NV1, NG, NB1 = 1536, 4096, 8192
-LSPLIT = 112
 LN2 = math.log(2.0)
 
 SCRATCH = {"vl": ("dram", [4, 128, 512], "bfloat16")}
 for _d, _l in (
-        ("bfloat16", "win:28672 vw:8192 vs:2048 ph:256 tt:256 tl:256 pw:16 pay:2048 one:128 zt:128 c128:128 one8:64 N1:128 cn:256 "
+        ("bfloat16", "win:29696 vw:8192 vs:2048 ph:256 tt:256 tl:256 pw:16 pay:2048 one:128 zt:128 c128:128 one8:64 N1:128 cn:256 "
                      "FS:528 I1:128 I99:128 I2k:128 MW:144 NW:128 RW:128 Hm:144 FW:512 FG:512 Fe:512 sg:512 W:1024 PC:512 pt:1024 "
-                     "ht:1024 lt:1024 mg:512 pres:256 junk:1280 LK:2560 t2:1280 Y:1280 YL:1280"),
+                     "ht:1024 lt:1024 mg:512 pres:256 junk:1280 LK:2560 t2:1280 Y:1280 YL:1280 ub:160"),
         ("int32", "ei:128 ai:128 fi:128 ct:32 k0:128 f12:256 h12:256 pi:8 pb:16 n1:512 n2:512 s1:256 s2:256 v1:256 v2:256 u1:80 u2:400"),
         ("float32", "cf:32 cT:32 k2:128 k3:128 k4:128 k5:128 hx:256 pf:16 pc:16 J:224 iA:128 iB:128 iX:32 iC:144 CZ:128 wS:128 "
                     "iE:256 iS:80 i4:8 m3:4 lm:4 dm:8 q1:128 q2:128 Q:128 b1:16 b2:16 bb:16 Z:224 S128:80 TB:16 ab:512 P:1024 Ts:512 "
-                    "o32:256 GW:520 v0:256 keep:256 X:256 acc:8 Gt:240 g1:560 zp:320 c8:16 cd:4 zc:4 u3:400 wt:128 wT:128 wL:128"),
+                    "o32:256 GW:520 v0:256 keep:256 X:256 acc:8 Gt:240 g1:320 zp:320 c8:16 cd:4 zc:48 u3:240 wT:128 wL:128"),
         ("float16", "Ep:144 E:144 z:512 U:8192"),
-        ("uint16", "ks:160 kl:160 gl:16 ll:160 lo:160")):
+        ("uint16", "ks:128 kl:96 ls:32 lr:32 gl:16 ll:160 lo:160")):
     for _e in _l.split():
         SCRATCH[_e.split(":")[0]] = ("sbuf", [128, int(_e.split(":")[1])], _d)
 for _j in range(7):
     SCRATCH["B%d" % _j] = ("psum", [128, 512], "float32")
-SEMAPHORES = ("pv ps pe pg lkey lcls lform zero lval lown wrp wrh unw lwin akey aform aval awho ay0 ay1 ay2 ay3 "
-              "skey sform sval swho sy0 sy1 sy2 sy3 who1 who2 st0 st1 st2 st3").split()
+SEMAPHORES = ("pv ps pe pg lkey lcls lform zero lval lown wrp0 wrp1 wrh unw lwin alist akey aform aval awho ay0 ay1 ay2 ay3 "
+              "slist skey sform sval swho sy0 sy1 sy2 sy3 who1 who2 st0 st1 st2 st3").split()
 
 
 def rank_program(g, core, T, topo):
@@ -34,6 +33,8 @@ def rank_program(g, core, T, topo):
         return
     cores = T.cores
     others = [(k + 1) % 4, (k + 2) % 4, (k + 3) % 4]
+    far_first = sorted(others, key=lambda d: topo.die(cores[d]) == topo.die(core))
+    order = far_first + [k]
     Q = {"v": g.vector, "s": g.scalar, "t": g.tensor, "g": g, "y": g.sync}
     count, wrote, read = {}, {}, {}
     seen = {q: {} for q in Q}
@@ -124,7 +125,7 @@ def rank_program(g, core, T, topo):
 
     def clear(a, b):
         for a0 in range(a, b, 2048):
-            act("pay", "bots", c_("win", a0, 2048), T.pay[:], F_.Identity, scale=0.0)
+            act("pay", "bots", c_("win", a0, min(2048, b - a0)), c_("pay", 0, min(2048, b - a0)), F_.Identity, scale=0.0)
 
     win = T.win
     AND, SHR, MUL, ADD, SUB, EQ, MAX, GT, GE = (A_.bitwise_and, A_.logical_shift_right, A_.mult, A_.add, A_.subtract, A_.is_equal,
@@ -136,31 +137,36 @@ def rank_program(g, core, T, topo):
 
     p0 = c_("pi", 0, 1)
     op("g", "", "pi", g.iota, p0, [[0, 1]], 0, 1)
-    iota("iX", c_("iX", 0, 16), [[1, 4], [0, 4]])
-    iota("iX", c_("iX", 16, 16), [[0, 4], [32, 4]])
     iota("iB", T.iB[:], [[0, 4], [1, 32]])
     iota("iA", T.iA[:], [[16, 4], [0, 32]])
+    iota("iX", c_("iX", 0, 16), [[1, 4], [0, 4]])
+    iota("iX", c_("iX", 16, 16), [[0, 4], [32, 4]])
     iota("one8", T.one8[:], [[0, 4], [-1, 2], [0, 8]], 1)
     iota("FS", c_("FS", 0, 16), [[0, 16]])
-    for j in range(8):
-        sel("one8", "FS", c_("FS", 16 + j * 64, 64), T.one8[:], [[-16, 2], [0, 2], [-1, 16]], EQ, 0.0,
-            -64 * (j & 1) - 32 * (j >> 2) - 8 * ((j >> 1) & 1), 1)
+
+    def formula_matrices(js):
+        for j in js:
+            sel("one8", "FS", c_("FS", 16 + j * 64, 64), T.one8[:], [[-16, 2], [0, 2], [-1, 16]], EQ, 0.0,
+                -64 * (j & 1) - 32 * (j >> 2) - 8 * ((j >> 1) & 1), 1)
+    formula_matrices(range(5))
     op("v", "", "wz1", V.memset, c_("win", SH, NV1), 0.0)
-    dmas("zero", "wz1", "wrow", [("y", win[x::16, 16384:16384 + SH], c_("win", SH + x * 384, SH // 16)) for x in range(3)])
+    dmas("zero", "wz1", "wrow", [("y", win[x::16, 16384:16384 + SH], c_("win", SH + x * 352, SH // 16)) for x in range(3)])
     act("wz1", "wz3", c_("win", SH + NV1, NV1), c_("win", SH, NV1))
-    act("wz1", "wz3", win[:, SH + 2 * NV1:16384], win[:, SH:16384 - 2 * NV1])
     pb = [c_("pb", j, 1) for j in range(7)]
     pf = [c_("pf", j, 1) for j in range(7)]
     pc = [c_("pc", j, 1) for j in range(10)]
-    for j, (sh, m) in enumerate(((0, 15), (4, 3), (0, 1), (0, 64), (0, 3), (2, 3), (0, 0x70))):
-        ts2("pi", "pb", pb[j], p0, sh, m, SHR, AND)
-    cp("pb", "pf", c_("pf", 0, 7), c_("pb", 0, 7))
+
+    def bits(a, fields):
+        for j, (sh, m) in enumerate(fields):
+            ts2("pi", "pb", pb[a + j], p0, sh, m, SHR, AND)
+        cp("pb", "pf", c_("pf", a, len(fields)), c_("pb", a, len(fields)))
+    bits(0, ((0, 15), (4, 3), (0, 1)))
     ts1("iB pf", "m3", c_("m3", 0, 3), c_("iB", 0, 3), pf[0], EQ)
     ts1("pf", "pc0", pc[0], pf[1], 4.0, MUL)
     ts2("pf", "pc1", pc[1], pf[2], 256.0, 64.0 * k, MUL, ADD)
     m0, m1, m2 = c_("m3", 0, 1), c_("m3", 1, 1), c_("m3", 2, 1)
-    ts1("iA m3", "q1", T.q1[:], T.iA[:], m0, MUL)
     ts1("iB m3", "q2", T.q2[:], T.iB[:], m1, MUL)
+    ts1("iA m3", "q1", T.q1[:], T.iA[:], m0, MUL)
     ts2("iX m3 pc0", "b1", T.b1[:], c_("iX", 0, 16), pc[0], m0, ADD, MUL)
     ts2("iX m3", "b2", T.b2[:], c_("iX", 16, 16), m1, m2, MUL, ADD)
     tt("q1 q2", "Q", T.Q[:], T.q1[:], T.q2[:], ADD)
@@ -169,20 +175,20 @@ def rank_program(g, core, T, topo):
         act("Q bb", "pay", T.pay[:, x::16], T.Q[:], F_.Identity, bias=c_("bb", x, 1))
     clear(NG, NG + 2048)
 
+    ts1("ct pc1", "cf", T.cf[:], T.ct[:], pc[1], ADD)
     ts1("ei", "k0", T.k0[:], T.ei[:], 2, SHR)
+    tr("cf", "cT", T.cT[:], T.cf[:])
     ts1("ei", "k2", T.k2[:], T.ei[:], 32.0, MUL)
+    cp("cT", "ls", T.ls[:], T.cT[:])
     ts1("k0", "k3", T.k3[:], T.k0[:], -16383.0 / 128, MUL)
     tt("k2 ai", "k4", T.k4[:], T.k2[:], T.ai[:], ADD)
-    ts1("ct pc1", "cf", T.cf[:], T.ct[:], pc[1], ADD)
     tt("k3 k4", "k5", T.k5[:], T.k4[:], T.k3[:], ADD)
-    tr("cf", "cT", T.cT[:], T.cf[:])
-    for nm, key, ks in (("ks", "ks", others), ("kl", "klown", [k])):
-        for kk in ks:
-            ts1("k5", key, c_(nm, kk * 40, 32), c_("k5", kk * 32, 32), 128.0, MUL)
-        for kk in ks:
-            cp("cT", key, c_(nm, kk * 40 + 32, 8), c_("cT", kk * 8, 8))
-    send("skey", "akey", "ks", [(d, c_("ks", d * 40, 40), c_("kl", k * 40, 40), 4 * j, 4 * j + 4) for j, d in enumerate(others)])
-    arrives("akey", 12, "klrem")
+    ts1("k5", "ks", T.ks[:], T.k5[:], 128.0, MUL)
+    send("slist", "alist", "ls", [(d, c_("ls", d * 8, 8), c_("lr", k * 8, 8), 4 * j, 4 * j + 4) for j, d in enumerate(others)])
+    arrives("alist", 12, "lr")
+    send("skey", "akey", "ks", [(d, c_("ks", d * 32, 32), c_("kl", j * 32, 32), 4 * j, 4 * j + 4) for j, d in enumerate(others)])
+    arrives("akey", 12, "kl")
+    formula_matrices(range(5, 8))
     ts1("fi", "h12", c_("h12", 0, 128), T.fi[:], 1, AND)
     ts2("fi", "h12", c_("h12", 128, 128), T.fi[:], 5, 1, SHR, AND)
     ts1("fi", "f12", c_("f12", 0, 128), T.fi[:], 31, AND)
@@ -206,8 +212,8 @@ def rank_program(g, core, T, topo):
     arrives("aval", 16, "vl")
 
     def windows(s, r, rs):
-        dmas(s, r, s, [("y", T.vw[c * 32:c * 32 + 32, q * 2048:q * 2048 + 2048], T.val[32 * k:32 * k + 32, :] if q == k else T.vl[q])
-                       for q in rs for c in range(4)])
+        dmas(s, r, s, [("y", T.vw[c * 32:c * 32 + 32, (k - q) % 4 * 2048:(k - q) % 4 * 2048 + 2048],
+                        T.val[32 * k:32 * k + 32, :] if q == k else T.vl[q]) for q in rs for c in range(4)])
     for nm, c in (("I1", 1.0), ("I99", -99.5), ("I2k", 2048.0)):
         sel("zt", nm, T[nm][:], T.zt[:], [[-1, 128]], A_.not_equal, c, 0, 1)
     iota("c128", T.c128[:], [[0, 128]], 128)
@@ -219,20 +225,18 @@ def rank_program(g, core, T, topo):
     iota("GWp", c_("GW", 257, 1), [[0, 1]])
     sel("NW", "RW", T.RW[:], T.NW[:], [[-1, 128]], GE, 0.0, 0, 1)
     iota("i4", T.i4[:], [[4, 8]], 1)
-    iota("iS", T.iS[:], [[16, 20], [320, 4]])
+    iota("iS", T.iS[:], [[16, 20], [320, 4]], 16)
     iota("iE", T.iE[:], [[0, 8], [128, 32]])
     for a in range(0, NG, 2048):
         iota("botg", c_("win", a, 2048), [[0, 2048]])
-    iota("wt", T.wt[:], [[0, 128]])
+    iota("zc0", T.zc[:], [[0, 48]])
     sel("o32", "CZ", c_("CZ", 0, 80), c_("o32", 0, 80), [[-32, 4], [-1, 20]], EQ, 0.0, 0, 1)
     sel("o32", "CZ", c_("CZ", 80, 48), c_("o32", 0, 48), [[-1000, 48]], EQ, 0.0, -20, 1)
     act("pf", "pw", c_("pw", 0, 1), pf[0], F_.Exp, scale=LN2, bias=LN2)
     act("pw", "pc9", pc[9], c_("pw", 0, 1))
 
-    for r in [k] + others:
-        op("v", "tab pay " + ("klown" if r == k else "klrem"), "wz1 wz3 wrow tab", V.tensor_copy,
-           c_("win", SH, 16384).indirect(c_("kl", r * 40, 32)), c_("pay", r * 512, 512))
-    dmas("wrp", "tab", "pt", [("y", c_("pt", u * 256, 256), win[u * 16 + 2::64, SH:SH + 16384]) for u in range(4)])
+    for key, off, a, n in (("ks", c_("ks", k * 32, 32), 0, 512), ("kl", T.kl[:], 512, 1536)):
+        op("v", "tab pay " + key, "wz1 wz3 wrow tab", V.tensor_copy, c_("win", SH, 16384).indirect(off), c_("pay", a, n))
 
     for j in range(16):
         y, q, t5 = j >> 3, (j >> 1) & 3, j & 1
@@ -241,12 +245,16 @@ def rank_program(g, core, T, topo):
                f == 0, f == 1)
     act("B5", "FW", T.FW[:], T.B5[:])
     for q in range(4):
-        act("FW klown klrem", "FG", c_("FG", q * 128, 128), T.FW[:].indirect(c_("kl", q * 40 + 32, 8)))
+        act("FW ls lr", "FG", c_("FG", q * 128, 128), T.FW[:].indirect(c_("ls" if q == k else "lr", q * 8, 8)))
+    for j in range(2):
+        dmas("wrp%d" % j, "tab", "pt%d" % j, [("ys"[u & 1], c_("pt", u * 256, 256), win[u * 16 + 2::64, SH:SH + 16384])
+                                             for u in (2 * j, 2 * j + 1)])
     tr("FG", "Fe", T.Fe[:], T.FG[:])
     act("Fe", "W0", c_("W", 0, 512), T.Fe[:], F_.Exp, scale=-LN2 / 2, bias=-LN2)
     act("Fe", "ab", T.ab[:], T.Fe[:], F_.Abs, bias=-200.0)
     act("ab", "W1", c_("W", 512, 512), T.ab[:], F_.Exp, scale=-LN2 / 2, bias=-LN2)
     act("Fe", "sg", T.sg[:], T.Fe[:], F_.Sign, bias=-100.0)
+    bits(3, ((0, 64), (0, 3), (2, 3), (0, 0x70)))
     tt("pf", "pc2", pc[2], pf[3], pf[1], ADD)
     ts2("pf", "pc6", pc[6], pf[5], 32.0, -99.5, MUL, ADD)
     ts2("iC pc2 pc9", "MW", T.MW[:], T.iC[:], pc[2], pc[9], EQ, MUL)
@@ -257,16 +265,15 @@ def rank_program(g, core, T, topo):
     ts1("J pc3", "Ep", T.Ep[:], c_("J", 0, 144), pc[3], EQ)
     ts2("J pc4", "Z", T.Z[:], T.J[:], -96.0, pc[4], ADD, EQ)
     tt("Ep", "E", c_("E", 0, 143), c_("Ep", 0, 143), c_("Ep", 1, 143), SUB)
-    ts2("m3", "pc5", pc[5], m0, 128.0, m1, MUL, ADD)
     ts1("J pf", "lm", T.lm[:], c_("J", 0, 4), pf[1], EQ)
-    ts2("J pc3 pc5", "Hm", T.Hm[:], c_("J", 0, 144), pc[3], pc[5], EQ, MUL)
 
     M = c_("B0", 0, 64)
     mm("one", "B0", M, T.one[0:1, :], T.one[0:1, 0:64], True, False)
     for j in range(16):
         u, xb = j >> 2, j & 3
-        mm("MW pt", "B0", M, c_("MW", 16 - 4 * xb, 128), T.pt[:, u * 256 + xb:u * 256 + 256:4], False, j == 15)
-    dmas("wrh", "tab pt", "ht", [("y", c_(("ht", "lt")[h], u * 256, 256), win[u * 16 + h::64, SH:SH + 16384]) for h in range(2) for u in range(4)])
+        mm("MW pt%d" % (u >> 1), "B0", M, c_("MW", 16 - 4 * xb, 128), T.pt[:, u * 256 + xb:u * 256 + 256:4], False, j == 15)
+    dmas("wrh", "tab pt0 pt1", "ht", [("y", c_(("ht", "lt")[h], u * 256, 256), win[u * 16 + h::64, SH:SH + 16384])
+                                      for h in range(2) for u in range(4)])
     for j in range(16):
         mm("I1 Fe", "B5", c_("B5", j * 32, 32), T.I1[:], T.Fe[:, j::16], True, False)
         mm("I99 sg", "B5", c_("B5", j * 32, 32), T.I99[:], T.sg[:, j::16], False, True)
@@ -302,89 +309,114 @@ def rank_program(g, core, T, topo):
     op("v", "o32 B1", "GWi", V.tensor_tensor_scan, incl, T.o32[:], c_("B1", 0, 256), 0.0, MUL, ADD)
     tt("GWi B1", "s1", T.s1[:], incl, c_("B1", 256, 256), SUB)
     for j in range(5):
-        act("GWi TB", "acc", c_("junk", j * 256, 255), c_("GW", 258, 255), F_.Sign, scale=-1.0, bias=c_("TB", j, 1), accum_out=c_("acc", j, 1))
+        act("GWi TB", "acc", c_("junk", j * 256, 256), incl, F_.Sign, scale=-1.0, bias=c_("TB", j, 1), accum_out=c_("acc", j, 1))
     ts1("s1", "s2", T.s2[:], T.s1[:], 0x780, AND)
     for f in range(2):
         tt("s2 B2", "z", c_("z", f * 256, 256), T.s2[:], c_("B2", f * 256, 256), ADD)
     for j in range(16):
         ts2("z", "U%d" % j, c_("U", j * 512, 512), T.z[:], -128.0 * j, 0.0, ADD, MAX)
         mm("Ep E U%d" % j, "B3", T.B3[:], c_("Ep" if j == 0 else "E", 15 - j, 128), c_("U", j * 512, 512), j == 0, j == 15)
-    for j, c in enumerate((128.5, 127.5, 385.5)):
+    for j, c in enumerate((129.0, 128.0, 386.0)):
         ts2("acc", "gl", c_("gl", 5 * j, 5), c_("acc", 0, 5), 0.5, c, MUL, ADD)
+    ts1("GWi", "GWe", c_("GW", 514, 1), c_("GW", 513, 1), 2048.0, ADD)
     ts1("B3", "v0", T.v0[:], c_("B3", 256, 256), 4096.0, MUL)
     tt("B3 v0", "v1", T.v1[:], T.v0[:], c_("B3", 0, 256), ADD)
     ts1("v1", "v2", T.v2[:], T.v1[:], 0x7F07F, AND)
     ts1("v2", "keep", T.keep[:], T.v2[:], 0.0, EQ)
     tt("v2 B4", "X", T.X[:], T.v2[:], c_("B4", 0, 256), ADD)
     op("v", "keep X", "GWf", V.tensor_tensor_scan, c_("GW", 1, 256), T.keep[:], T.X[:], 0.0, MUL, MAX)
-    cp("GWf GWi GWp gl", "Gt", T.Gt[:], c_("GW", 0, 514).indirect(c_("gl", 0, 15)))
-    g1 = [c_("g1", j * 80, 80) for j in range(7)]
-    tt("Gt S128", "g0", g1[0], c_("Gt", 160, 80), T.S128[:], SUB)
+    cp("GWf GWi GWp GWe gl", "Gt", T.Gt[:], c_("GW", 0, 515).indirect(c_("gl", 0, 15)))
+    g1 = [c_("g1", j * 80, 80) for j in range(4)]
+    tt("Gt S128", "g0", g1[0], c_("Gt", 160, 80), T.S128[:], GT)
     tt("Gt", "g1", g1[1], c_("Gt", 80, 80), c_("Gt", 0, 80), SUB)
-    ts1("g0", "g2", g1[2], g1[0], 2048.0, GT)
-    ts1("g0", "g3", g1[3], g1[0], 0.0, GT)
-    tt("g1 g2", "g4", g1[4], g1[1], g1[2], MUL)
-    tt("Gt g3", "g5", g1[5], c_("Gt", 0, 80), g1[3], MUL)
-    tt("g4 g5", "g6", g1[6], g1[4], g1[5], ADD)
-    for d in range(4):
-        ts1("g6 lm", "zp", c_("zp", d * 80, 80), g1[6], c_("lm", d, 1), MUL)
+    tt("g0 g1", "g2", g1[2], g1[1], g1[0], MUL)
+    tt("Gt g2", "g3", g1[3], c_("Gt", 0, 80), g1[2], ADD)
+    for j, d in enumerate(order):
+        ts1("g3 lm", "zp", c_("zp", j * 80, 80), g1[3], c_("lm", d, 1), MUL)
     for c in range(4):
         mm("Z zp", "B0", c_("B0", 0, 80), c_("Z", 96 - 32 * c, 128), T.zp[:, c::4], c == 0, c == 3)
     ts2("J pf", "dm", T.dm[:], c_("J", 0, 8), pf[0], 1.0 / 128, EQ, MUL)
     tt("GWi GWp", "c8", c_("c8", 0, 8), T.GW[:, 289:514:32], T.GW[:, 257:482:32], SUB)
+    ts2("m3", "pc5", pc[5], m0, 128.0, m1, MUL, ADD)
     tt("c8 dm", "c9", c_("c8", 8, 8), c_("c8", 0, 8), T.dm[:], MUL)
+    ts2("J pc3 pc5", "Hm", T.Hm[:], c_("J", 0, 144), pc[3], pc[5], EQ, MUL)
     op("v", "c9", "cd", V.tensor_reduce, c_("cd", 0, 1), c_("c8", 8, 8), AxisListType.X, ADD)
-    ts1("cd lm", "zc", T.zc[:], T.lm[:], c_("cd", 0, 1), MUL)
     u1 = T.u1[:]
     u2 = [c_("u2", j * 80, 80) for j in range(5)]
-    u3 = [c_("u3", j * 80, 80) for j in range(5)]
+    u3 = [c_("u3", j * 80, 80) for j in range(3)]
     lw = c_("win", 0, 16384)
+
+    def look(f, a, b):
+        f("ll%d lk" % (2 - a // 80), "LK%d" % a, T.LK[:, 16 * a:16 * b], lw.indirect(T.ll[:, a:b]))
+
+    def wrap(bank, a, r):
+        for x in range(16):
+            mm("Hm " + r, bank, c_(bank, 0, 40), c_("Hm", 15 - x, 128), T.LK[:, 16 * a + x:16 * a + 640:16], x == 0, x == 15)
+
+    def lst(bank, a):
+        cp(bank, "lo%d" % a, c_("lo", a, 40), c_(bank, 0, 40))
+
+    def second(j):
+        act("lo%d lown lwin" % (j // 2 * 40), "t2%d" % j, c_("t2", j * 320, 320), T.vw[:].indirect(c_("lo", j * 20, 20)))
+
+    def first(j):
+        d = order[j]
+        tt("lo%d lown lwin t2%d" % (80 + j // 2 * 40, j), "Y%d" % d, c_("Y", j * 320, 320), T.vw[:].indirect(c_("lo", 80 + j * 20, 20)),
+           c_("t2", j * 320, 320), SUB)
+        if d != k:
+            send("sy%d" % d, "ay%d" % k, "Y%d" % d, [(d, c_("Y", j * 320, 320), c_("YL", k * 320, 320), 0, 16)])
+    ts2("B0", "a0", u2[0], c_("B0", 0, 80), 1.0 / 32, -0.484375, MUL, ADD)
     cp("B0", "u1", u1, c_("B0", 0, 80))
-    ts1("u1", "a0", u2[0], u1, 5, SHR)
-    ts1("u1", "a1", u2[1], u1, 31, AND)
     cp("a0", "ll2", c_("ll", 0, 80), u2[0])
-    act("ll2 lk", "LKa", c_("LK", 0, 1280), lw.indirect(c_("ll", 0, 80)))
-    ts2("u1", "a2", u2[2], u1, 5, 0x307F, SHR, AND)
+    look(act, 0, 40)
+    look(act, 40, 80)
+    ts1("u1", "a1", u2[1], u1, 31, AND)
+    ts1("a0", "a2", u2[2], u2[0], 0x307F, AND)
     ts1("a1", "c0", u3[0], u2[1], 128.0, MUL)
-    ts2("u1", "a3", u2[3], u1, 5, 127, SHR, AND)
+    ts1("cd lm zc0", "zc", T.zc[:, 0::12], T.lm[:], c_("cd", 0, 1), MUL)
     tt("c0 a2", "c1", u3[1], u3[0], u2[2], ADD)
-    mm("Z zc", "B1", c_("B1", 0, 4), c_("Z", 96, 128), T.zc[:], True, True)
-    ts1("u1", "a4", u2[4], u1, 17, SHR)
+    for j, d in enumerate(order):
+        mm("Z zc zc0", "B1", c_("B1", j * 32 + 20, 12), c_("Z", 96, 128), c_("zc", d * 12, 12), True, True)
+    ts1("a0", "a3", u2[3], u2[0], 127, AND)
     cp("c1", "ll1", c_("ll", 80, 80), u3[1])
-    act("ll1 lk", "LKb", T.LK[:, 1280:16 * LSPLIT], lw.indirect(T.ll[:, 80:LSPLIT]))
+    look(act, 140, 160)
+    ts1("u1", "a4", u2[4], u1, 17, SHR)
     ts1("u1", "c2", u3[2], u1, 0.0, EQ)
-    ts1("a3", "c3", u3[3], u2[3], 4.0, MUL)
-    tt("a4 c2", "c4", u3[4], u2[4], u3[2], SUB)
-    cp("B1", "wt", T.wt[:, 20::32], c_("B1", 0, 4))
-    for d in range(4):
-        tt("c3 c4", "wt", c_("wt", d * 32, 20), c_("u3", 240 + d * 20, 20), c_("u3", 320 + d * 20, 20), ADD)
-    tr("wt", "wT", T.wT[:], T.wt[:])
-    cp("ll1 lk", "LKc", T.LK[:, 16 * LSPLIT:2560], lw.indirect(T.ll[:, LSPLIT:160]))
-    for x in range(16):
-        mm("Hm LKa", "B6", c_("B6", 0, 80), c_("Hm", 15 - x, 128), T.LK[:, x:1280:16], x == 0, x == 15)
+    ts1("a3", "c3", c_("ub", 0, 80), u2[3], 4.0, MUL)
+    tt("a4 c2", "c4", c_("ub", 80, 80), u2[4], u3[2], SUB)
+    wrap("B6", 0, "LK0")
+    for j in range(8):
+        mm("I1 c3 c4", "B1", c_("B1", (j >> 1) * 32, 20), T.I1[:], c_("ub", (j & 1) * 80 + (j >> 1) * 20, 20), j & 1 == 0, j & 1 == 1)
+    look(cp, 80, 120)
+    tr("B1", "wT", T.wT[:], c_("B1", 0, 128))
+    lst("B6", 0)
+    wrap("B3", 80, "LK80")
     mm("CZ wT", "B2", c_("B2", 0, 128), T.CZ[:], T.wT[:], True, True)
+    wrap("B5", 40, "LK40")
+    look(cp, 120, 140)
+    wrap("B4", 120, "LK120 LK140")
+    second(0)
     act("B2", "wS", T.wS[:], c_("B2", 0, 128))
-    send("swho", "awho", "wS", [(d, c_("wS", d * 32, 32), c_("wL", k * 32, 32), 4 * j, 4 * j + 4) for j, d in enumerate(others)])
+    send("swho", "awho", "wS", [(d, c_("wS", j * 32, 32), c_("wL", k * 32, 32), 4 * j, 4 * j + 4) for j, d in enumerate(far_first)])
     arrives("awho", 12, "wL")
     for s, nm, ks in (("who1", "wS", [k]), ("who2", "wL", others)):
-        dmas(s, nm, "", [it for kk in ks for g_ in (2 * kk, 2 * kk + 1)
-                         for it in (("y", T.who[g_:g_ + 1, :], T[nm][0:80, g_ * 16:g_ * 16 + 16]),
-                                    ("y", T.cnt[g_:g_ + 1, :], T[nm][80:81, g_ * 16:g_ * 16 + 8]))])
-    for x in range(16):
-        mm("Hm LKb LKc", "B3", c_("B3", 0, 80), c_("Hm", 15 - x, 128), T.LK[:, 1280 + x::16], x == 0, x == 15)
-    cp("B6", "lo2", c_("lo", 0, 80), c_("B6", 0, 80))
-    cp("B3", "lo1", c_("lo", 80, 80), c_("B3", 0, 80))
-    for d in others + [k]:
-        act("lo2 lown lwin", "t2%d" % d, c_("t2", d * 320, 320), T.vw[:].indirect(c_("lo", d * 20, 20)))
-        tt("lo1 lown lwin t2%d" % d, "Y%d" % d, c_("Y", d * 320, 320), T.vw[:].indirect(c_("lo", 80 + d * 20, 20)),
-           c_("t2", d * 320, 320), SUB)
-        if d != k:
-            send("sy%d" % d, "ay%d" % k, "Y%d" % d, [(d, c_("Y", d * 320, 320), c_("YL", k * 320, 320), 0, 16)])
+        dmas(s, nm, "", [it for kk in ks for h in range(2) for g_, c0 in [(2 * kk + h, (96 if kk == k else kk * 32) + 16 * h)]
+                         for it in (("y", T.who[g_:g_ + 1, :], T[nm][0:80, c0:c0 + 16]), ("y", T.cnt[g_:g_ + 1, :], T[nm][80:81, c0:c0 + 8]))])
+    second(1)
+    lst("B3", 80)
+    first(0)
+    lst("B5", 40)
+    second(2)
+    second(3)
+    first(1)
+    lst("B4", 120)
+    first(2)
+    first(3)
     for r in others:
         arrives("ay%d" % r, 16, "YL%d" % r)
-    for r in [k] + others[::-1]:
-        nm = "Y" if r == k else "YL"
+    for r in [k] + far_first:
+        nm, c0 = ("Y", 960) if r == k else ("YL", r * 320)
         dmas("st%d" % r, nm + str(r), "", [("ys"[c & 1], T.y[32 * r:32 * r + 32, c * 320:c * 320 + 320],
-                                            T[nm][c * 32:c * 32 + 32, r * 320:r * 320 + 320]) for c in range(4)])
+                                            T[nm][c * 32:c * 32 + 32, c0:c0 + 320]) for c in range(4)])
     for s in count:
         wait("g", s, count[s])

@@ -1,29 +1,33 @@
 import math
 from concourse.bass import DstId, RemoteDMATransfer
-from concourse.mybir import AluOpType, AxisListType, ActivationFunctionType
+from concourse.mybir import AluOpType, ActivationFunctionType
 
 A_ = AluOpType
 F_ = ActivationFunctionType
-SH = 13312
-NV1, NG, NB1 = 1536, 4096, 8192
+SH = 15360
+SPENT = ("pay:2048 vs:1536 pt:1024 ht:1024 lt:1024 SG:1024 W:512 FW:512 FG:512 Fe:512 fb:512 FS:528 FN:528 MW:144 ME:176 one8:64 "
+         "N1:128 c4:128 GT:128 NW:128 LT:128 RW:128 I4k:128 I512:128 I32:128 I480:128 Rb:128 rest:2272")
+AT = {}
+for _e in SPENT.split():
+    AT[_e.split(":")[0]] = (sum(n for _, n in AT.values()), int(_e.split(":")[1]))
 LN2 = math.log(2.0)
+Z0 = 480.0 * 6144 + 32.0 * 24576 - 4096
 
 SCRATCH = {"vl": ("dram", [4, 128, 512], "bfloat16")}
 for _d, _l in (
-        ("bfloat16", "win:29696 vw:8192 vs:2048 ph:256 tt:256 tl:256 pw:16 pay:2048 one:128 zt:128 c128:128 one8:64 N1:128 cn:256 "
-                     "FS:528 I1:128 I99:128 I2k:128 MW:144 NW:128 RW:128 Hm:144 FW:512 FG:512 Fe:512 sg:512 W:1024 PC:512 pt:1024 "
-                     "ht:1024 lt:1024 mg:512 pres:256 junk:1280 LK:2560 t2:1280 Y:1280 YL:1280 ub:160"),
-        ("int32", "ei:128 ai:128 fi:128 ct:32 k0:128 f12:256 h12:256 pi:8 pb:16 n1:512 n2:512 s1:256 s2:256 v1:256 v2:256 u1:80 u2:400"),
-        ("float32", "cf:32 cT:32 k2:128 k3:128 k4:128 k5:128 hx:256 pf:16 pc:16 J:224 iA:128 iB:128 iX:32 iC:144 CZ:128 wS:128 "
-                    "iE:256 iS:80 i4:8 m3:4 lm:4 dm:8 q1:128 q2:128 Q:128 b1:16 b2:16 bb:16 Z:224 S128:80 TB:16 ab:512 P:1024 Ts:512 "
-                    "o32:256 GW:520 v0:256 keep:256 X:256 acc:8 Gt:240 g1:320 zp:320 c8:16 cd:4 zc:48 u3:240 wT:128 wL:128"),
-        ("float16", "Ep:144 E:144 z:512 U:8192"),
+        ("bfloat16", "win:31744 vw:8192 pw:16 one:256 I1:128 In:128 Hm:144 P1:144 E1:144 P2:144 E2:144 P2k:144 E2k:144 Ta:128 Tb:128 "
+                     "nA:128 nB:128 Cp:144 Cn:144 mg:512 pres:272 Gs:768 Gb:272 Fg:80 keep:256 iE:256 rA:160 junk:1280 LK:2560 "
+                     "t2:1280 Y:1280 YL:1280 ub:176"),
+        ("int32", "ei:128 ai:128 fi:128 ct:32 pi:8 pb:16 u2:480"),
+        ("float32", "cf:96 cT:32 k5:128 pf:16 pc:32 J:224 iA:128 iB:128 iX:16 iC:144 i3:128 CZ:128 wS:160 i4:8 m3:4 lm:4 q1:128 "
+                    "q2:128 Q:128 bb:16 Z:224 TB:16 rr:512 bt:256 Jb:256 o32:264 GW:264 acc:16 om:160 g1:240 zp:320 u3:160 wT:128 wL:160"),
+        ("float16", "ph:256 tt:256 tl:256 s1:272 r4:256 r16:256 U:2048 V:2048"),
         ("uint16", "ks:128 kl:96 ls:32 lr:32 gl:16 ll:160 lo:160")):
     for _e in _l.split():
         SCRATCH[_e.split(":")[0]] = ("sbuf", [128, int(_e.split(":")[1])], _d)
-for _j in range(7):
+for _j in range(8):
     SCRATCH["B%d" % _j] = ("psum", [128, 512], "float32")
-SEMAPHORES = ("pv ps pe pg lkey lcls lform zero lval lown wrp0 wrp1 wrh unw lwin alist akey aform aval awho ay0 ay1 ay2 ay3 "
+SEMAPHORES = ("pv ps pe pg lkey lcls lform zero lval lown wrp wrh unw lwin alist akey aform aval awho ay0 ay1 ay2 ay3 "
               "slist skey sform sval swho sy0 sy1 sy2 sy3 who1 who2 st0 st1 st2 st3").split()
 
 
@@ -108,11 +112,24 @@ def rank_program(g, core, T, topo):
     def tr(r, w, *a):
         op("v", r, w, V.transpose, *a)
 
+    def scan(r, w, *a):
+        op("v", r, w, V.tensor_tensor_scan, *a)
+
+    def fill(w, o, c=0.0):
+        op("v", "", w, V.memset, o, c)
+
     def act(r, w, o, i, f=F_.Copy, **kw):
         op("s", r, w, S.activation, o, i, f, **kw)
 
+    def scaled(r, w, c):
+        act(r, w, c_(w), c_(r), F_.Identity, scale=c)
+
     def mm(r, w, *a):
         op("t", r, w, g.tensor.matmul, *a)
+
+    def mms(w, o, terms):
+        for j, (r, a, b) in enumerate(terms):
+            mm(r, w, o, a, b, j == 0, j == len(terms) - 1)
 
     def iota(w, o, pat, base=0):
         op("g", "", w, g.iota, o, pat, base, 0, allow_small_or_imprecise_dtypes=True)
@@ -120,301 +137,337 @@ def rank_program(g, core, T, topo):
     def sel(r, w, *a):
         op("g", r, w, g.affine_select, *a)
 
-    def c_(name, a, n):
-        return T[name][:, a:a + n]
-
-    def clear(a, b):
-        for a0 in range(a, b, 2048):
-            act("pay", "bots", c_("win", a0, min(2048, b - a0)), c_("pay", 0, min(2048, b - a0)), F_.Identity, scale=0.0)
+    def c_(name, a=0, n=None, step=1):
+        a0, width = AT[name] if name in AT else (0, SCRATCH[name][1][1])
+        return T["win" if name in AT else name][:, a0 + a:a0 + (width if n is None else a + n):step]
 
     win = T.win
-    AND, SHR, MUL, ADD, SUB, EQ, MAX, GT, GE = (A_.bitwise_and, A_.logical_shift_right, A_.mult, A_.add, A_.subtract, A_.is_equal,
-                                                A_.max, A_.is_gt, A_.is_ge)
+    AND, SHR, MUL, ADD, SUB, EQ, MAX, LT_, GE = (A_.bitwise_and, A_.logical_shift_right, A_.mult, A_.add, A_.subtract, A_.is_equal,
+                                                 A_.max, A_.is_lt, A_.is_ge)
+    E3 = ((0, 4), (4, 8), (8, 16))
+    dmas("lcls", "", "ct", [("ys"[j & 1], T.ct[(j >> 1) * 32 + (j & 1):(j >> 1) * 32 + 32:2, :], T.cls[(j >> 2)::2, :]) for j in range(8)])
     dmas("lkey", "", "ei ai", [it for kk in range(4) for it in (("y", c_("ei", kk * 32, 32), T.ent[2 * kk:2 * kk + 2, :]),
                                                                ("s", c_("ai", kk * 32, 32), T.att[2 * kk:2 * kk + 2, :]))])
-    dmas("lcls", "", "ct", [("ys"[j & 1], T.ct[(j >> 1) * 32 + (j & 1):(j >> 1) * 32 + 32:2, :], T.cls[(j >> 2)::2, :]) for j in range(8)])
     dmas("lform", "", "fi", [("ys"[kk & 1], c_("fi", kk * 32, 32), T.form[2 * kk:2 * kk + 2, :]) for kk in range(4)])
 
     p0 = c_("pi", 0, 1)
     op("g", "", "pi", g.iota, p0, [[0, 1]], 0, 1)
     iota("iB", T.iB[:], [[0, 4], [1, 32]])
-    iota("iA", T.iA[:], [[16, 4], [0, 32]])
-    iota("iX", c_("iX", 0, 16), [[1, 4], [0, 4]])
-    iota("iX", c_("iX", 16, 16), [[0, 4], [32, 4]])
-    iota("one8", T.one8[:], [[0, 4], [-1, 2], [0, 8]], 1)
+    iota("iA", T.iA[:], [[2048, 4], [0, 32]])
+    iota("iX", T.iX[:], [[32, 16]])
+    iota("one8", c_("one8"), [[0, 4], [-1, 2], [0, 8]], 1)
     iota("FS", c_("FS", 0, 16), [[0, 16]])
 
     def formula_matrices(js):
         for j in js:
-            sel("one8", "FS", c_("FS", 16 + j * 64, 64), T.one8[:], [[-16, 2], [0, 2], [-1, 16]], EQ, 0.0,
+            sel("one8", "FS", c_("FS", 16 + j * 64, 64), c_("one8"), [[-16, 2], [0, 2], [-1, 16]], EQ, 0.0,
                 -64 * (j & 1) - 32 * (j >> 2) - 8 * ((j >> 1) & 1), 1)
-    formula_matrices(range(5))
-    op("v", "", "wz1", V.memset, c_("win", SH, NV1), 0.0)
-    dmas("zero", "wz1", "wrow", [("y", win[x::16, 16384:16384 + SH], c_("win", SH + x * 352, SH // 16)) for x in range(3)])
-    act("wz1", "wz3", c_("win", SH + NV1, NV1), c_("win", SH, NV1))
-    pb = [c_("pb", j, 1) for j in range(7)]
-    pf = [c_("pf", j, 1) for j in range(7)]
-    pc = [c_("pc", j, 1) for j in range(10)]
+    formula_matrices(range(2))
+    fill("wz0", c_("win", SH, 1024))
+    dmas("zero", "wz0", "wrow", [("y", win[x::16, 16384:16384 + SH], c_("win", SH, SH // 16)) for x in range(3)])
+    pb = [c_("pb", j, 1) for j in range(9)]
+    pf = [c_("pf", j, 1) for j in range(9)]
+    pc = [c_("pc", j, 1) for j in range(24)]
 
     def bits(a, fields):
         for j, (sh, m) in enumerate(fields):
-            ts2("pi", "pb", pb[a + j], p0, sh, m, SHR, AND)
-        cp("pb", "pf", c_("pf", a, len(fields)), c_("pb", a, len(fields)))
+            ts2("pi", "pb%d" % a, pb[a + j], p0, sh, m, SHR, AND)
+        cp("pb%d" % a, "pf%d" % a, c_("pf", a, len(fields)), c_("pb", a, len(fields)))
     bits(0, ((0, 15), (4, 3), (0, 1)))
-    ts1("iB pf", "m3", c_("m3", 0, 3), c_("iB", 0, 3), pf[0], EQ)
-    ts1("pf", "pc0", pc[0], pf[1], 4.0, MUL)
-    ts2("pf", "pc1", pc[1], pf[2], 256.0, 64.0 * k, MUL, ADD)
+    ts1("iB pf0", "m3", c_("m3", 0, 3), c_("iB", 0, 3), pf[0], EQ)
+    ts1("pf0", "pc0", pc[0], pf[1], 512.0, MUL)
+    ts2("pf0", "pc1", pc[1], pf[2], 256.0, 32.0 * k, MUL, ADD)
     m0, m1, m2 = c_("m3", 0, 1), c_("m3", 1, 1), c_("m3", 2, 1)
-    ts1("iB m3", "q2", T.q2[:], T.iB[:], m1, MUL)
-    ts1("iA m3", "q1", T.q1[:], T.iA[:], m0, MUL)
-    ts2("iX m3 pc0", "b1", T.b1[:], c_("iX", 0, 16), pc[0], m0, ADD, MUL)
-    ts2("iX m3", "b2", T.b2[:], c_("iX", 16, 16), m1, m2, MUL, ADD)
+    ts2("iB m3", "q2", T.q2[:], T.iB[:], m1, m2, MUL, ADD)
+    ts2("iA m3 pc0", "q1", T.q1[:], T.iA[:], pc[0], m0, ADD, MUL)
+    ts1("iX m3", "bb", T.bb[:], T.iX[:], m0, MUL)
     tt("q1 q2", "Q", T.Q[:], T.q1[:], T.q2[:], ADD)
-    tt("b1 b2", "bb", T.bb[:], T.b1[:], T.b2[:], ADD)
     for x in range(16):
-        act("Q bb", "pay", T.pay[:, x::16], T.Q[:], F_.Identity, bias=c_("bb", x, 1))
-    clear(NG, NG + 2048)
+        act("Q bb", "pay", c_("pay", x, None, 16), T.Q[:], F_.Identity, bias=c_("bb", x, 1))
 
-    ts1("ct pc1", "cf", T.cf[:], T.ct[:], pc[1], ADD)
-    ts1("ei", "k0", T.k0[:], T.ei[:], 2, SHR)
-    tr("cf", "cT", T.cT[:], T.cf[:])
-    ts1("ei", "k2", T.k2[:], T.ei[:], 32.0, MUL)
+    ts2("ct", "cf0", c_("cf", 0, 32), T.ct[:], 32.0, 96.0, GE, MUL)
+    ts1("ct pc1", "cf1", c_("cf", 32, 32), T.ct[:], pc[1], ADD)
+    tt("cf0 cf1", "cf2", c_("cf", 64, 32), c_("cf", 0, 32), c_("cf", 32, 32), ADD)
+    tr("cf2", "cT", T.cT[:], c_("cf", 64, 32))
     cp("cT", "ls", T.ls[:], T.cT[:])
-    ts1("k0", "k3", T.k3[:], T.k0[:], -16383.0 / 128, MUL)
-    tt("k2 ai", "k4", T.k4[:], T.k2[:], T.ai[:], ADD)
-    tt("k3 k4", "k5", T.k5[:], T.k4[:], T.k3[:], ADD)
-    ts1("k5", "ks", T.ks[:], T.k5[:], 128.0, MUL)
-    send("slist", "alist", "ls", [(d, c_("ls", d * 8, 8), c_("lr", k * 8, 8), 4 * j, 4 * j + 4) for j, d in enumerate(others)])
-    arrives("alist", 12, "lr")
-    send("skey", "akey", "ks", [(d, c_("ks", d * 32, 32), c_("kl", j * 32, 32), 4 * j, 4 * j + 4) for j, d in enumerate(others)])
-    arrives("akey", 12, "kl")
-    formula_matrices(range(5, 8))
-    ts1("fi", "h12", c_("h12", 0, 128), T.fi[:], 1, AND)
-    ts2("fi", "h12", c_("h12", 128, 128), T.fi[:], 5, 1, SHR, AND)
-    ts1("fi", "f12", c_("f12", 0, 128), T.fi[:], 31, AND)
-    ts1("h12", "hx", T.hx[:], T.h12[:], 199.0, MUL)
-    ts1("fi", "f12", c_("f12", 128, 128), T.fi[:], 5, SHR)
-    tt("hx f12", "ph", T.ph[:], T.hx[:], T.f12[:], ADD)
+    send("slist", "alist", "ls", [(d, c_("ls", d * 8, 8), c_("lr", k * 8, 8)) + E3[j] for j, d in enumerate(others)])
+    arrives("alist", 16, "lr")
+    ts1("ai", "B7", c_("B7", 0, 128), T.ai[:], 512.0, MUL)
+    tt("B7 ei", "k5", T.k5[:], c_("B7", 0, 128), T.ei[:], ADD)
+    cp("k5", "ks", T.ks[:], T.k5[:])
+    send("skey", "akey", "ks", [(d, c_("ks", d * 32, 32), c_("kl", j * 32, 32)) + E3[j] for j, d in enumerate(others)])
+    arrives("akey", 16, "kl")
+    cp("fi", "ph", c_("ph", 0, 128), T.fi[:])
+    ts2("fi", "ph", c_("ph", 128, 128), T.fi[:], 1.0 / 32, 1536 - 0.484375, MUL, ADD)
     tr("ph", "tt", T.tt[:], T.ph[:])
-    send("sform", "aform", "tt", [(d, c_("tt", f * 128 + d * 32, 32), c_("tl", (k * 2 + f) * 32, 32), 4 * j + 2 * f, 4 * j + 2 * f + 2)
+    send("sform", "aform", "tt", [(d, c_("tt", f * 128 + d * 32, 32), c_("tl", f * 128 + k * 32, 32), 4 * j + 2 * f, 4 * j + 2 * f + 2)
                                   for j, d in enumerate(others) for f in range(2)])
     arrives("aform", 12, "tlrem")
     for f in range(2):
-        act("tt", "tlown", c_("tl", (k * 2 + f) * 32, 32), c_("tt", f * 128 + k * 32, 32))
-    clear(NG + 2048, NB1)
+        cp("tt", "tlown", c_("tl", f * 128 + k * 32, 32), c_("tt", f * 128 + k * 32, 32))
+    bits(3, ((3, 1), (0, 64), (0, 3), (2, 3), (0, 0x70), (0, 0x7C)))
+    formula_matrices(range(2, 8))
+    act("pf0", "pw", c_("pw", 0, 1), pf[0], F_.Exp, scale=LN2, bias=LN2)
+    act("pf3", "pc10", pc[10], pf[3], F_.Identity, scale=-49152.0 - 1536.0, bias=49152.0)
+    act("pw", "pc9", pc[9], c_("pw", 0, 1))
+    for j, (a, sc, b) in enumerate((
+            (6, 32.0, Z0), (5, 32.0, Z0),
+            (8, 1.0, 3.0), (7, 1.0, pf[5]),
+            (4, 1.0, pf[0]), (7, 1.0, 15.0),
+            (4, 0.25, pf[0]), (5, 20.0, pf[6]),
+            (0, -1.0 / 16, 160 + 15.0 / 16 - 0.46875), (5, 1.0, -2.0), (4, 1.0 / 128, pf[1]))):
+        act("pf0 pf3", "pcs", pc[11 + j], pf[a], F_.Relu if j == 9 else F_.Identity, scale=sc, bias=b)
+    act("pcs", "pc20", pc[20], pc[20], F_.Identity, scale=-1024.0, bias=1024.0)
+    act("pcs", "pc22", pc[22], pc[21], F_.Identity, scale=2.0, bias=1.0)
+    for j in range(3):
+        act("pcs", "th", c_("q1", j, 1), pc[11], F_.Identity, bias=0.5 - 512.0 * (j + 1))
+    act("m3", "pc5", pc[5], m0, F_.Identity, bias=m1)
+    act("pc22 m3", "pc23", pc[23], pc[22], F_.Identity, scale=m0, bias=-1.0)
+    scaled("FS", "FN", -32.0)
+    wait("y", "skey", count["skey"])
+    dmas("lval", "", "vs", [("y", c_("vs", j * 512, 512), T.val[32 * d:32 * d + 32, :]) for j, d in enumerate(others)])
     iota("J", T.J[:], [[1, 224]])
     iota("iC", c_("iC", 0, 16), [[0, 16]], 999)
     iota("iC", c_("iC", 16, 128), [[64, 2], [0, 4], [1, 16]])
-    iota("zt", T.zt[:], [[0, 128]])
-    iota("one", T.one[:], [[0, 128]], 1)
-    dmas("lval", "ks", "vs", [("y", c_("vs", d * 512, 512), T.val[32 * d:32 * d + 32, :]) for d in others])
-    send("sval", "aval", "vs", [(d, c_("vs", d * 512, 512), T.vl[k], (0, 4, 8)[j], (4, 8, 16)[j]) for j, d in enumerate(others)])
+    iota("one", T.one[:], [[0, 256]], 1)
+    send("sval", "aval", "vs", [(d, c_("vs", j * 512, 512), T.vl[k]) + E3[j] for j, d in enumerate(others)])
     arrives("aval", 16, "vl")
+    one = c_("one", 0, 128)
+    sel("one", "I1", T.I1[:], one, [[-1, 128]], EQ, 0.0, 0, 1)
+    sel("one", "N1", c_("N1"), one, [[-16, 8], [0, 16]], GE, 0.0, 0, 1)
+    iota("i3", T.i3[:], [[0, 32], [1, 4]])
+    sel("N1", "NW", c_("NW"), c_("N1"), [[16, 8], [0, 16]], GE, 0.0, 15, -1)
+    iota("i4", T.i4[:], [[4, 8]], 1)
+    sel("NW", "GT", c_("GT"), c_("NW"), [[-1, 128]], GE, 0.0, -1, 1)
+    sel("NW", "RW", c_("RW"), c_("NW"), [[-1, 128]], GE, 0.0, 0, 1)
+    sel("NW", "LT", c_("LT"), c_("NW"), [[1, 128]], GE, 0.0, -1, -1)
+    iota("nA", T.nA[:], [[0, 8], [128, 4], [0, 4]], -384)
+    iota("rest", c_("rest"), [[0, AT["rest"][1]]])
+    iota("iE", T.iE[:], [[0, 8], [128, 32]])
+    iota("rA", c_("rA", 0, 80), [[-1, 20], [-20, 4]], -161)
+    iota("rA", c_("rA", 80, 80), [[1, 20], [20, 4]], 162)
 
     def windows(s, r, rs):
         dmas(s, r, s, [("y", T.vw[c * 32:c * 32 + 32, (k - q) % 4 * 2048:(k - q) % 4 * 2048 + 2048],
                         T.val[32 * k:32 * k + 32, :] if q == k else T.vl[q]) for q in rs for c in range(4)])
-    for nm, c in (("I1", 1.0), ("I99", -99.5), ("I2k", 2048.0)):
-        sel("zt", nm, T[nm][:], T.zt[:], [[-1, 128]], A_.not_equal, c, 0, 1)
-    iota("c128", T.c128[:], [[0, 128]], 128)
-    iota("cn", T.cn[:], [[0, 256]], -2048)
-    sel("c128", "N1", T.N1[:], T.c128[:], [[-16, 8], [0, 16]], GE, 0.0, 0, 1)
-    iota("o32", T.o32[:], [[0, 256]], 1)
-    sel("N1", "NW", T.NW[:], T.N1[:], [[16, 8], [0, 16]], GE, 0.0, 15, -1)
-    iota("GWp", c_("GW", 0, 1), [[0, 1]])
-    iota("GWp", c_("GW", 257, 1), [[0, 1]])
-    sel("NW", "RW", T.RW[:], T.NW[:], [[-1, 128]], GE, 0.0, 0, 1)
-    iota("i4", T.i4[:], [[4, 8]], 1)
-    iota("iS", T.iS[:], [[16, 20], [320, 4]], 16)
-    iota("iE", T.iE[:], [[0, 8], [128, 32]])
-    for a in range(0, NG, 2048):
-        iota("botg", c_("win", a, 2048), [[0, 2048]])
-    iota("zc0", T.zc[:], [[0, 48]])
-    sel("o32", "CZ", c_("CZ", 0, 80), c_("o32", 0, 80), [[-32, 4], [-1, 20]], EQ, 0.0, 0, 1)
-    sel("o32", "CZ", c_("CZ", 80, 48), c_("o32", 0, 48), [[-1000, 48]], EQ, 0.0, -20, 1)
-    act("pf", "pw", c_("pw", 0, 1), pf[0], F_.Exp, scale=LN2, bias=LN2)
-    act("pw", "pc9", pc[9], c_("pw", 0, 1))
 
     for key, off, a, n in (("ks", c_("ks", k * 32, 32), 0, 512), ("kl", T.kl[:], 512, 1536)):
-        op("v", "tab pay " + key, "wz1 wz3 wrow tab", V.tensor_copy, c_("win", SH, 16384).indirect(off), c_("pay", a, n))
+        op("v", "tab pay " + key, "wz0 wrow tab", V.tensor_copy, c_("win", SH, 16384).indirect(off), c_("pay", a, n))
 
-    for j in range(16):
-        y, q, t5 = j >> 3, (j >> 1) & 3, j & 1
-        for f in range(2):
-            mm("FS tlown tlrem", "B5", c_("B5", j * 32, 32), c_("FS", (t5 * 2 + y) * 128 + 16 - 8 * f, 128), c_("tl", (q * 2 + f) * 32, 32),
-               f == 0, f == 1)
-    act("B5", "FW", T.FW[:], T.B5[:])
+    for j in range(4):
+        a = ((j & 1) * 2 + (j >> 1)) * 128
+        r = "FS FN tlown tlrem"
+        mms("B5", c_("B5", j * 128, 128), [(r, c_("FS", a + 16, 128), c_("tl", 0, 128)), (r, c_("FS", a + 8, 128), c_("tl", 128, 128)),
+                                           (r, c_("FN", a + 16, 128), c_("tl", 128, 128))])
+    act("B5 pc10", "FW", c_("FW"), T.B5[:], F_.Identity, bias=pc[10])
     for q in range(4):
-        act("FW ls lr", "FG", c_("FG", q * 128, 128), T.FW[:].indirect(c_("ls" if q == k else "lr", q * 8, 8)))
-    for j in range(2):
-        dmas("wrp%d" % j, "tab", "pt%d" % j, [("ys"[u & 1], c_("pt", u * 256, 256), win[u * 16 + 2::64, SH:SH + 16384])
-                                             for u in (2 * j, 2 * j + 1)])
-    tr("FG", "Fe", T.Fe[:], T.FG[:])
-    act("Fe", "W0", c_("W", 0, 512), T.Fe[:], F_.Exp, scale=-LN2 / 2, bias=-LN2)
-    act("Fe", "ab", T.ab[:], T.Fe[:], F_.Abs, bias=-200.0)
-    act("ab", "W1", c_("W", 512, 512), T.ab[:], F_.Exp, scale=-LN2 / 2, bias=-LN2)
-    act("Fe", "sg", T.sg[:], T.Fe[:], F_.Sign, bias=-100.0)
-    bits(3, ((0, 64), (0, 3), (2, 3), (0, 0x70)))
-    tt("pf", "pc2", pc[2], pf[3], pf[1], ADD)
-    ts2("pf", "pc6", pc[6], pf[5], 32.0, -99.5, MUL, ADD)
-    ts2("iC pc2 pc9", "MW", T.MW[:], T.iC[:], pc[2], pc[9], EQ, MUL)
-    ts2("pf", "pc6", pc[7], pf[4], 32.0, -99.5, MUL, ADD)
-    ts1("pf", "pc3", pc[3], pf[6], 15.0, ADD)
-    ts2("pf", "pc4", pc[4], pf[3], 0.25, pf[0], MUL, ADD)
-    ts2("pf", "pc8", pc[8], pf[4], 20.0, pf[5], MUL, ADD)
-    ts1("J pc3", "Ep", T.Ep[:], c_("J", 0, 144), pc[3], EQ)
-    ts2("J pc4", "Z", T.Z[:], T.J[:], -96.0, pc[4], ADD, EQ)
-    tt("Ep", "E", c_("E", 0, 143), c_("Ep", 0, 143), c_("Ep", 1, 143), SUB)
-    ts1("J pf", "lm", T.lm[:], c_("J", 0, 4), pf[1], EQ)
-
-    M = c_("B0", 0, 64)
-    mm("one", "B0", M, T.one[0:1, :], T.one[0:1, 0:64], True, False)
-    for j in range(16):
-        u, xb = j >> 2, j & 3
-        mm("MW pt%d" % (u >> 1), "B0", M, c_("MW", 16 - 4 * xb, 128), T.pt[:, u * 256 + xb:u * 256 + 256:4], False, j == 15)
-    dmas("wrh", "tab pt0 pt1", "ht", [("y", c_(("ht", "lt")[h], u * 256, 256), win[u * 16 + h::64, SH:SH + 16384])
-                                      for h in range(2) for u in range(4)])
-    for j in range(16):
-        mm("I1 Fe", "B5", c_("B5", j * 32, 32), T.I1[:], T.Fe[:, j::16], True, False)
-        mm("I99 sg", "B5", c_("B5", j * 32, 32), T.I99[:], T.sg[:, j::16], False, True)
-    for f in range(2):
-        act("B5 pc6", "PC", c_("PC", f * 256, 256), c_("B5", f * 256, 256), F_.Identity, bias=pc[6 + f])
-    for j in range(16):
-        tt("W0 W1 B0", "P", T.P[:, j::16], T.W[:, j::16], M, MUL)
-    tt("P", "Ts", T.Ts[:], c_("P", 0, 512), c_("P", 512, 512), ADD)
-    ts1("Ts", "n1", T.n1[:], T.Ts[:], -0.5, ADD)
-    ts1("n1", "n2", T.n2[:], T.n1[:], 1, AND)
-    for al in range(8):
-        tt("n2", "pres", c_("pres", al * 32, 32), T.n2[:, al::16], T.n2[:, 8 + al::16], MUL)
-    mm("NW pres", "B1", c_("B1", 0, 256), T.NW[:], T.pres[:], True, True)
-    mm("RW pres", "B1", c_("B1", 256, 256), T.RW[:], T.pres[:], True, True)
-    for f in range(2):
-        o = c_("B2", f * 256, 256)
-        mm("I1 PC", "B2", o, T.I1[:], c_("PC", f * 256, 256), True, False)
-        mm("one cn", "B2", o, T.one[0:1, :], T.cn[0:1, :], False, False)
-        mm("I2k pres", "B2", o, T.I2k[:], T.pres[:], False, True)
-    for j in range(8):
-        mm("I1 ht", "B6", c_("B6", (j >> 2) * 256, 256), T.I1[:], c_(("ht", "lt")[j >> 2], (j & 3) * 256, 256), j & 3 == 0, j & 3 == 3)
-    clear(NB1, SH)
-    act("B6", "mg", T.mg[:], T.B6[:])
-    act("iE", "B4", c_("B4", 0, 256), T.iE[:])
-    windows("lown", "ht", [k])
-    dmas("unw", "mg", "tab botg bots lk", [("y", win[c * 32 + h:c * 32 + 32:16, 0:16384], c_("mg", h * 256, 256))
-                                           for c in range(4) for h in range(2)])
+        act("FW ls lr", "FG", c_("FG", q * 128, 128), c_("FW").indirect(c_("ls" if q == k else "lr", q * 8, 8)))
+    dmas("wrp", "tab", "pt", [("y", c_("pt", w * 512, 512), win[2::16, SH + w * 8192:SH + w * 8192 + 8192]) for w in range(2)])
+    dmas("wrh", "tab pt", "ht lt", [("y", c_(("ht", "lt")[h]), win[h::16, SH:SH + 16384]) for h in range(2)])
+    windows("lown", "", [k])
     windows("lwin", "vl", others)
-    ts2("i4 pc8", "TB0", c_("TB", 8, 8), T.i4[:], pc[8], 2048.0, ADD, MUL)
-    ts2("iS pf", "S128", T.S128[:], T.iS[:], pf[0], 128.0, ADD, MUL)
-    ts1("TB0", "TB", c_("TB", 0, 8), c_("TB", 8, 8), -64.0, ADD)
-    incl = c_("GW", 258, 256)
-    op("v", "o32 B1", "GWi", V.tensor_tensor_scan, incl, T.o32[:], c_("B1", 0, 256), 0.0, MUL, ADD)
-    tt("GWi B1", "s1", T.s1[:], incl, c_("B1", 256, 256), SUB)
-    for j in range(5):
-        act("GWi TB", "acc", c_("junk", j * 256, 256), incl, F_.Sign, scale=-1.0, bias=c_("TB", j, 1), accum_out=c_("acc", j, 1))
-    ts1("s1", "s2", T.s2[:], T.s1[:], 0x780, AND)
-    for f in range(2):
-        tt("s2 B2", "z", c_("z", f * 256, 256), T.s2[:], c_("B2", f * 256, 256), ADD)
+    for nm, c in (("I4k", 4096.0), ("I512", 512.0), ("I32", -32.0), ("I480", -480.0), ("In", -1.0)):
+        scaled("I1", nm, c)
+    tr("FG", "Fe", c_("Fe"), c_("FG"))
     for j in range(16):
-        ts2("z", "U%d" % j, c_("U", j * 512, 512), T.z[:], -128.0 * j, 0.0, ADD, MAX)
-        mm("Ep E U%d" % j, "B3", T.B3[:], c_("Ep" if j == 0 else "E", 15 - j, 128), c_("U", j * 512, 512), j == 0, j == 15)
-    for j, c in enumerate((129.0, 128.0, 386.0)):
-        ts2("acc", "gl", c_("gl", 5 * j, 5), c_("acc", 0, 5), 0.5, c, MUL, ADD)
-    ts1("GWi", "GWe", c_("GW", 514, 1), c_("GW", 513, 1), 2048.0, ADD)
-    ts1("B3", "v0", T.v0[:], c_("B3", 256, 256), 4096.0, MUL)
-    tt("B3 v0", "v1", T.v1[:], T.v0[:], c_("B3", 0, 256), ADD)
-    ts1("v1", "v2", T.v2[:], T.v1[:], 0x7F07F, AND)
-    ts1("v2", "keep", T.keep[:], T.v2[:], 0.0, EQ)
-    tt("v2 B4", "X", T.X[:], T.v2[:], c_("B4", 0, 256), ADD)
-    op("v", "keep X", "GWf", V.tensor_tensor_scan, c_("GW", 1, 256), T.keep[:], T.X[:], 0.0, MUL, MAX)
-    cp("GWf GWi GWp GWe gl", "Gt", T.Gt[:], c_("GW", 0, 515).indirect(c_("gl", 0, 15)))
-    g1 = [c_("g1", j * 80, 80) for j in range(4)]
-    tt("Gt S128", "g0", g1[0], c_("Gt", 160, 80), T.S128[:], GT)
-    tt("Gt", "g1", g1[1], c_("Gt", 80, 80), c_("Gt", 0, 80), SUB)
-    tt("g0 g1", "g2", g1[2], g1[1], g1[0], MUL)
-    tt("Gt g2", "g3", g1[3], c_("Gt", 0, 80), g1[2], ADD)
+        mm("I1 Fe", "B5", c_("B5", j * 32, 32), T.I1[:], c_("Fe", j, None, 16), True, True)
+    act("B5", "SG1", c_("SG", 1, None, 2), T.B5[:], F_.Sign, bias=-15.5)
+    act("B5", "W", c_("W"), T.B5[:], F_.Exp, scale=-LN2, bias=-LN2)
+    act("B5", "fb", c_("fb"), T.B5[:])
+    ts2("iC pf3 pc9", "MW", c_("MW"), T.iC[:], pf[4], pc[9], EQ, MUL)
+    fill("SG0", c_("SG", 0, None, 2))
+    fill("pres0", T.pres[:, 0:258:257])
+    fill("o32", T.o32[:], 1.0)
+    ts2("J pcs", "ME", c_("ME"), c_("J", 0, 176), -48.0, pc[15], ADD, EQ)
+    ts1("J pcs", "P1", T.P1[:], c_("J", 0, 144), pc[13], EQ)
+    ts2("J pcs", "P2", T.P2[:], c_("J", 0, 144), -12.0, pc[14], ADD, EQ)
+    ts2("i3 pf3", "c4", c_("c4"), T.i3[:], pf[5], 128.0, EQ, MUL)
+    tt("P1", "E1", c_("E1", 0, 143), c_("P1", 0, 143), c_("P1", 1, 143), SUB)
+    tt("P2", "E2", c_("E2", 0, 140), c_("P2", 0, 140), c_("P2", 4, 140), SUB)
+    tt("c4 GT", "Ta", T.Ta[:], c_("c4"), c_("GT"), MUL)
+    ts2("i4 pcs", "TB0", c_("TB", 8, 8), T.i4[:], pc[18], 16.0, ADD, MUL)
+    ts2("J pcs", "Z", T.Z[:], T.J[:], -96.0, pc[17], ADD, EQ)
+    ts1("TB0", "TB", c_("TB", 0, 8), c_("TB", 8, 8), -0.5, ADD)
+    ts1("J pf0", "lm", T.lm[:], c_("J", 0, 4), pf[1], EQ)
+    fill("GWp", T.GW[:, 0:258:257])
+    sel("o32", "CZ", c_("CZ", 0, 80), c_("o32", 0, 80), [[-32, 4], [-1, 20]], EQ, 0.0, 0, 1)
+    iota("CZ", c_("CZ", 80, 48), [[0, 48]])
+
+    mms("B0", T.B0[:, 1:128:2], [("one", T.one[0:1, 0:128], T.one[0:1, 0:64])] +
+        [("MW pt", c_("MW", 16 - x, 128), c_("pt", x, None, 16)) for x in range(16)])
+    for f in range(2):
+        mm("I1 fb", "B%d" % (4 + 2 * f), c_("B%d" % (4 + 2 * f), 0, 256), T.I1[:], c_("fb", f * 256, 256), True, False)
+    for h in range(2):
+        for x in range(4):
+            mms("B7", T.B7[:, h * 256 + x:h * 256 + 256:4],
+                [("ME ht lt", c_("ME", 48 - 16 * b, 128), c_(("ht", "lt")[h], 4 * x + b, None, 16)) for b in range(4)])
+    act("NW m3", "Rb", c_("Rb"), c_("NW"), F_.Identity, scale=m0)
+    scaled("P2", "P2k", 4096.0)
+    act("E2", "E2k", c_("E2k", 0, 140), c_("E2", 0, 140), F_.Identity, scale=4096.0)
+    scaled("nA", "nB", 4096.0)
+    scaled("Ta", "Tb", 4096.0)
+    act("B7", "mg", T.mg[:], T.B7[:])
+    ts2("B0", "B0", T.B0[:, 0:64:2], T.B0[:, 65:128:2], 131072.0, 65536.0, ADD, MUL)
+    for j in range(16):
+        b = "B%d" % (1 + (j >> 3))
+        scan("SG0 SG1 B0", b, c_(b, (j & 7) * 64, 64), c_("SG", j * 64, 64), c_("B0", 0, 64), 0.0, MUL, MAX)
+    for f in range(2):
+        tt("W B%d" % (1 + f), "B3", c_("B3", f * 256, 256), T["B%d" % (1 + f)][:, 1::2], c_("W", f * 256, 256), MUL)
+    ts2("B3", "rr", T.rr[:], T.B3[:], 1.5 * 2 ** 24, -1.5 * 2 ** 24, ADD, ADD)
+    tt("B3 rr", "B1", c_("B1", 0, 256), c_("B3", 0, 256), c_("rr", 0, 256), LT_)
+    tt("B3 rr", "bt", T.bt[:], c_("B3", 256, 256), c_("rr", 256, 256), LT_)
+    pres = c_("pres", 1, 256)
+    tt("B1 bt", "pres", pres, c_("B1", 0, 256), T.bt[:], MUL)
+    mms("B2", c_("B2", 0, 257), [("LT pres pres0", c_("LT"), c_("pres", 1, 257)), ("RW pres pres0", c_("RW"), c_("pres", 0, 257))])
+    for b in ("B4", "B6"):
+        mm("I4k pres", b, c_(b, 0, 256), c_("I4k"), pres, False, False)
+    ts2("J pcs pc5", "Hm", T.Hm[:], c_("J", 0, 144), pc[16], pc[5], EQ, MUL)
+    ts1("J pc23", "Cp", T.Cp[:], c_("J", 0, 144), pc[23], EQ)
+    s1 = c_("s1", 0, 256)
+    scan("o32 B2", "s1", c_("s1", 0, 257), c_("o32", 0, 257), c_("B2", 0, 257), 0.0, MUL, ADD)
+    ts1("s1", "r16", T.r16[:], s1, 24576 - 7.5, ADD)
+    ts1("s1", "r4", T.r4[:], s1, 6144 - 1.5, ADD)
+    fill("ub0", c_("ub", 160, 16))
+    scaled("Cp", "Cn", -1.0)
+    for b in ("B4", "B6"):
+        for nm, r in (("I512", "s1"), ("I32", "r16"), ("I480", "r4")):
+            mm(nm + " " + r, b, c_(b, 0, 256), c_(nm), c_(r, 0, 256), False, r == "r4")
+        if b == "B4":
+            mm("Rb s1", "B0", c_("B0", 0, 257), c_("Rb"), c_("s1", 0, 257), True, True)
+    dmas("unw", "mg", "tab lk SG0 SG1 " + " ".join(AT), [("y", win[c * 32 + h:c * 32 + 32:16, 0:16384], c_("mg", h * 256, 256))
+                                                         for c in range(4) for h in range(2)])
+    for f in range(2):
+        ts2("B%d pcs" % (4 + 2 * f), "U0", c_("U", f * 256, 256), c_("B%d" % (4 + 2 * f), 0, 256), pc[11 + f], 0.0, ADD, MAX)
+    act("B0 pcs", "Gb", c_("Gb", 0, 257), c_("B0", 0, 257), F_.Identity, scale=1.0 / 16, bias=pc[19])
+    for j in range(3):
+        act("B4 th", "Gs%d" % j, c_("Gs", j * 256, 256), c_("B4", 0, 256), F_.Sign, bias=c_("q1", j, 1))
+    for j in range(1, 4):
+        ts2("U0", "U%d" % j, c_("U", j * 512, 512), c_("U", 0, 512), -512.0 * j, 0.0, ADD, MAX)
+
+    def stage1(j):
+        mm("P1 E1 U%d" % j, "B1", T.B1[:], c_("E1" if j else "P1", 3 - j, 128), c_("U", j * 512, 512), j == 0, j == 3)
+
+    def excess(j):
+        mm("P1 Gs%d" % j, "B7", c_("B7", 0, 256), c_("P1", 3 - j, 128), c_("Gs", j * 256, 256), j == 0, j == 2)
+
+    def columns(j):
+        act("B0 TB", "acc", c_("junk", j * 256, 256), c_("B0", 1, 256), F_.Sign, scale=-1.0, bias=c_("TB", j, 1), accum_out=c_("acc", j, 1))
+    for f, j in ((stage1, 0), (excess, 0), (stage1, 1), (excess, 1), (excess, 2), (stage1, 2), (stage1, 3)):
+        f(j)
+    mms("B3", c_("B3", 0, 256), [("I1 Gb", T.I1[:], c_("Gb", 1, 256)), ("In Gb", T.In[:], c_("Gb", 0, 256))])
+    act("Gb", "Gb1", c_("Gb", 257, 1), c_("Gb", 256, 1), F_.Identity, bias=1.0)
+    ts2("B7 pc20", "Jb", T.Jb[:], c_("B7", 0, 256), 256.0, pc[20], MUL, ADD)
+    for j in range(4):
+        columns(j)
+    act("B3", "keep", T.keep[:], c_("B3", 0, 256), F_.Identity, scale=-1.0, bias=1.0)
+    columns(4)
+    X = c_("B5", 0, 256)
+    mm("one iE", "B5", X, T.one[0:1, 0:128], T.iE[0:1, :], True, False)
+    for nm in ("nA", "nB"):
+        mm("one " + nm, "B5", X, T[nm][0:1, :], T.one[0:1, :], False, False)
+    for f in range(2):
+        tt("B1 Jb", "V0%d" % f, c_("V", f * 256, 256), c_("B1", f * 256, 256), T.Jb[:], SUB)
+        mm("P2 P2k V0%d" % f, "B5", X, c_(("P2", "P2k")[f], 12, 128), c_("V", f * 256, 256), False, False)
+    for nm in ("Ta", "Tb"):
+        mm("keep " + nm, "B5", X, T[nm][:], T.keep[:], False, False)
+    for j in range(1, 4):
+        ts2("V00 V01", "V%d" % j, c_("V", j * 512, 512), c_("V", 0, 512), -128.0 * j, 0.0, ADD, MAX)
+        for f in range(2):
+            mm("E2 E2k V%d" % j, "B5", X, c_(("E2", "E2k")[f], 12 - 4 * j, 128), c_("V", j * 512 + f * 256, 256), False, j + f == 4)
+        if j == 1:
+            ts2("acc", "gl1", c_("gl", 6, 5), c_("acc", 0, 5), 0.5, 129.0, MUL, ADD)
+        if j == 2:
+            act("Gb Gb1 gl1", "Fg", T.Fg[:], T.Gb[:].indirect(c_("gl", 6, 5)))
+            for h, nm in enumerate(("I1", "In")):
+                mms("B4", c_("B4", h * 80, 80), [("one rA", T.one[0:1, 0:128], T.rA[0:1, h * 80:h * 80 + 80]), (nm + " Fg", T[nm][:], T.Fg[:])])
+            act("B4", "om", T.om[:], c_("B4", 0, 160), F_.Relu)
+    ts2("acc", "gl0", c_("gl", 0, 5), c_("acc", 0, 5), 0.5, 128.0, MUL, ADD)
+    scan("keep B5", "GWf", c_("GW", 1, 256), T.keep[:], X, 0.0, MUL, MAX)
+    g1 = [c_("g1", j * 80, 80) for j in range(3)]
+    for j in range(2):
+        tt("GWf GWp gl%d om" % j, "g%d" % j, g1[j], T.GW[:].indirect(c_("gl", 6 * j, 5)), c_("om", j * 80, 80), MUL)
+    tt("g0 g1", "g2", g1[2], g1[0], g1[1], ADD)
     for j, d in enumerate(order):
-        ts1("g3 lm", "zp", c_("zp", j * 80, 80), g1[3], c_("lm", d, 1), MUL)
-    for c in range(4):
-        mm("Z zp", "B0", c_("B0", 0, 80), c_("Z", 96 - 32 * c, 128), T.zp[:, c::4], c == 0, c == 3)
-    ts2("J pf", "dm", T.dm[:], c_("J", 0, 8), pf[0], 1.0 / 128, EQ, MUL)
-    tt("GWi GWp", "c8", c_("c8", 0, 8), T.GW[:, 289:514:32], T.GW[:, 257:482:32], SUB)
-    ts2("m3", "pc5", pc[5], m0, 128.0, m1, MUL, ADD)
-    tt("c8 dm", "c9", c_("c8", 8, 8), c_("c8", 0, 8), T.dm[:], MUL)
-    ts2("J pc3 pc5", "Hm", T.Hm[:], c_("J", 0, 144), pc[3], pc[5], EQ, MUL)
-    op("v", "c9", "cd", V.tensor_reduce, c_("cd", 0, 1), c_("c8", 8, 8), AxisListType.X, ADD)
-    u1 = T.u1[:]
-    u2 = [c_("u2", j * 80, 80) for j in range(5)]
-    u3 = [c_("u3", j * 80, 80) for j in range(3)]
+        ts1("g2 lm", "zp", c_("zp", j * 80, 80), g1[2], c_("lm", d, 1), MUL)
+    mms("B0", c_("B0", 0, 80), [("Z zp", c_("Z", 96 - 32 * c, 128), T.zp[:, c::4]) for c in range(4)])
+    u2 = [c_("u2", j * 80, 80) for j in range(6)]
+    u3 = [c_("u3", j * 80, 80) for j in range(2)]
     lw = c_("win", 0, 16384)
+    word = c_("B0", 0, 80)
 
-    def look(f, a, b):
-        f("ll%d lk" % (2 - a // 80), "LK%d" % a, T.LK[:, 16 * a:16 * b], lw.indirect(T.ll[:, a:b]))
+    def look(f, j, h):
+        f("ll%d lk" % h, "LK%d%d" % (j, h), c_("LK", j * 640 + h * 320, 320), lw.indirect(c_("ll", h * 80 + j * 20, 20)))
 
-    def wrap(bank, a, r):
-        for x in range(16):
-            mm("Hm " + r, bank, c_(bank, 0, 40), c_("Hm", 15 - x, 128), T.LK[:, 16 * a + x:16 * a + 640:16], x == 0, x == 15)
+    def wrap(j):
+        b = "B%d" % (3 + j)
+        mms(b, c_(b, 0, 40), [("Hm LK%d0 LK%d1" % (j, j), c_("Hm", 15 - x, 128), c_("LK", j * 640 + x, 640 - x, 16)) for x in range(16)])
 
-    def lst(bank, a):
-        cp(bank, "lo%d" % a, c_("lo", a, 40), c_(bank, 0, 40))
+    def lst(j):
+        cp("B%d" % (3 + j), "lo%d" % j, c_("lo", j * 40, 40), c_("B%d" % (3 + j), 0, 40))
 
     def second(j):
-        act("lo%d lown lwin" % (j // 2 * 40), "t2%d" % j, c_("t2", j * 320, 320), T.vw[:].indirect(c_("lo", j * 20, 20)))
+        act("lo%d lown lwin" % j, "t2%d" % j, c_("t2", j * 320, 320), T.vw[:].indirect(c_("lo", j * 40, 20)))
 
     def first(j):
         d = order[j]
-        tt("lo%d lown lwin t2%d" % (80 + j // 2 * 40, j), "Y%d" % d, c_("Y", j * 320, 320), T.vw[:].indirect(c_("lo", 80 + j * 20, 20)),
+        tt("lo%d lown lwin t2%d" % (j, j), "Y%d" % d, c_("Y", j * 320, 320), T.vw[:].indirect(c_("lo", j * 40 + 20, 20)),
            c_("t2", j * 320, 320), SUB)
         if d != k:
             send("sy%d" % d, "ay%d" % k, "Y%d" % d, [(d, c_("Y", j * 320, 320), c_("YL", k * 320, 320), 0, 16)])
-    ts2("B0", "a0", u2[0], c_("B0", 0, 80), 1.0 / 32, -0.484375, MUL, ADD)
-    cp("B0", "u1", u1, c_("B0", 0, 80))
-    cp("a0", "ll2", c_("ll", 0, 80), u2[0])
-    look(act, 0, 40)
-    look(act, 40, 80)
-    ts1("u1", "a1", u2[1], u1, 31, AND)
+    ts2("B0", "ll0", c_("ll", 0, 80), word, 1.0 / 32, -0.484375, MUL, ADD)
+    ts2("B0", "a0", u2[0], word, 1.0 / 32, -0.484375, MUL, ADD)
+    ts1("B0", "u1", u2[1], word, 128.0, MUL)
+    look(act, 0, 0)
+    look(act, 1, 0)
     ts1("a0", "a2", u2[2], u2[0], 0x307F, AND)
-    ts1("a1", "c0", u3[0], u2[1], 128.0, MUL)
-    ts1("cd lm zc0", "zc", T.zc[:, 0::12], T.lm[:], c_("cd", 0, 1), MUL)
-    tt("c0 a2", "c1", u3[1], u3[0], u2[2], ADD)
+    ts1("u1", "a1", u2[3], u2[1], 0xF80, AND)
+    ts1("a0", "a3", u2[4], u2[0], 127, AND)
+    tt("a1 a2", "c1", u3[0], u2[2], u2[3], ADD)
+    ts1("a0", "a4", u2[5], u2[0], 12, SHR)
+    cp("c1", "ll1", c_("ll", 80, 80), u3[0])
+    ts1("a0", "c2", u3[1], u2[0], 0.0, EQ)
+    look(cp, 0, 1)
+    look(act, 1, 1)
+    look(act, 2, 0)
     for j, d in enumerate(order):
-        mm("Z zc zc0", "B1", c_("B1", j * 32 + 20, 12), c_("Z", 96, 128), c_("zc", d * 12, 12), True, True)
-    ts1("a0", "a3", u2[3], u2[0], 127, AND)
-    cp("c1", "ll1", c_("ll", 80, 80), u3[1])
-    look(act, 140, 160)
-    ts1("u1", "a4", u2[4], u1, 17, SHR)
-    ts1("u1", "c2", u3[2], u1, 0.0, EQ)
-    ts1("a3", "c3", c_("ub", 0, 80), u2[3], 4.0, MUL)
-    tt("a4 c2", "c4", c_("ub", 80, 80), u2[4], u3[2], SUB)
-    wrap("B6", 0, "LK0")
-    for j in range(8):
-        mm("I1 c3 c4", "B1", c_("B1", (j >> 1) * 32, 20), T.I1[:], c_("ub", (j & 1) * 80 + (j >> 1) * 20, 20), j & 1 == 0, j & 1 == 1)
-    look(cp, 80, 120)
-    tr("B1", "wT", T.wT[:], c_("B1", 0, 128))
-    lst("B6", 0)
-    wrap("B3", 80, "LK80")
-    mm("CZ wT", "B2", c_("B2", 0, 128), T.CZ[:], T.wT[:], True, True)
-    wrap("B5", 40, "LK40")
-    look(cp, 120, 140)
-    wrap("B4", 120, "LK120 LK140")
+        mms("B2", c_("B2", j * 40 + 32, 8), [("Cp s1", c_("Cp", 2 * d, 128), T.s1[:, 32:257:32]), ("Cn s1", c_("Cn", 2 * d, 128), T.s1[:, 0:256:32])])
+    wrap(0)
+    ts1("a3", "c3", c_("ub", 0, 80), u2[4], 4.0, MUL)
+    tt("a4 c2", "c4b", c_("ub", 80, 80), u2[5], u3[1], SUB)
+    for j in range(4):
+        mms("B1", c_("B1", j * 32, 32), [("I1 c3 c4b ub0", T.I1[:], c_("ub", h * 80 + j * 20, 32)) for h in range(2)])
+    wrap(1)
+    lst(0)
+    look(act, 3, 0)
     second(0)
-    act("B2", "wS", T.wS[:], c_("B2", 0, 128))
-    send("swho", "awho", "wS", [(d, c_("wS", j * 32, 32), c_("wL", k * 32, 32), 4 * j, 4 * j + 4) for j, d in enumerate(far_first)])
+    tr("B1", "wT", T.wT[:], c_("B1", 0, 128))
+    look(cp, 2, 1)
+    for j in range(4):
+        mm("CZ wT", "B2", c_("B2", j * 40, 32), T.CZ[:], c_("wT", j * 32, 32), True, True)
+    wrap(2)
+    lst(1)
+    act("B2", "wS", T.wS[:], c_("B2", 0, 160))
+    send("swho", "awho", "wS", [(d, c_("wS", j * 40, 40), c_("wL", k * 40, 40), 4 * j, 4 * j + 4) for j, d in enumerate(far_first)])
     arrives("awho", 12, "wL")
     for s, nm, ks in (("who1", "wS", [k]), ("who2", "wL", others)):
-        dmas(s, nm, "", [it for kk in ks for h in range(2) for g_, c0 in [(2 * kk + h, (96 if kk == k else kk * 32) + 16 * h)]
-                         for it in (("y", T.who[g_:g_ + 1, :], T[nm][0:80, c0:c0 + 16]), ("y", T.cnt[g_:g_ + 1, :], T[nm][80:81, c0:c0 + 8]))])
+        dmas(s, nm, "", [it for kk in ks for c0 in [120 if kk == k else kk * 40]
+                         for it in (("y", T.who[2 * kk:2 * kk + 1, :], T[nm][0:80, c0:c0 + 16]),
+                                    ("y", T.who[2 * kk + 1:2 * kk + 2, :], T[nm][0:80, c0 + 16:c0 + 32]),
+                                    ("y", T.cnt[2 * kk:2 * kk + 2, :], T[nm][0:2, c0 + 32:c0 + 40]))])
     second(1)
-    lst("B3", 80)
     first(0)
-    lst("B5", 40)
+    lst(2)
     second(2)
-    second(3)
     first(1)
-    lst("B4", 120)
+    look(act, 3, 1)
     first(2)
+    wrap(3)
+    lst(3)
+    second(3)
     first(3)
     for r in others:
         arrives("ay%d" % r, 16, "YL%d" % r)
-    for r in [k] + far_first:
+    for r in far_first[:2] + [k] + far_first[2:]:
         nm, c0 = ("Y", 960) if r == k else ("YL", r * 320)
         dmas("st%d" % r, nm + str(r), "", [("ys"[c & 1], T.y[32 * r:32 * r + 32, c * 320:c * 320 + 320],
                                             T[nm][c * 32:c * 32 + 32, c0:c0 + 320]) for c in range(4)])

@@ -5,24 +5,30 @@ from concourse.mybir import AluOpType, ActivationFunctionType
 A_ = AluOpType
 F_ = ActivationFunctionType
 SH = 15360
-SPENT = ("pay:2048 vs:1536 pt:1024 ht:1024 lt:1024 SG:1024 W:512 FW:512 FG:512 Fe:512 fb:512 FS:528 FN:528 MW:144 ME:176 one8:64 "
-         "N1:128 c4:128 GT:128 NW:128 LT:128 RW:128 I4k:128 I512:128 I32:128 I480:128 Rb:128 rest:2272")
+SPENT = ("pay:2048 vs:1536 pt:1024 ht:1024 lt:1024 clr:2048 sg:512 W:512 FW:512 FG:512 Fe:512 fb:512 FS:528 MW:144 "
+         "ME:176 c4:128 GT:128 NW:128 LT:128 RW:128 I4k:128 I512:128 I32:128 I15:128 I480:128 N1:128 one8:64 zt:128 Rb:128")
 AT = {}
 for _e in SPENT.split():
     AT[_e.split(":")[0]] = (sum(n for _, n in AT.values()), int(_e.split(":")[1]))
+AT["rest"] = (sum(n for _, n in AT.values()), SH - sum(n for _, n in AT.values()))
 LN2 = math.log(2.0)
-Z0 = 480.0 * 6144 + 32.0 * 24576 - 4096
+Z0 = 480.0 * 6144 + 32.0 * 24576 - 4096 - 15.5
+EVEN = 1.5 * 2 ** 24
+MIDDLE = ("merge0 merge1 merge2 merge3 pick1 pick0 shift1 shift0 open1 round0 scale0 round1 test0 test1 open0 both0 scale1 both1 "
+          "number0 rows0 floor0 evac0 tally0 held0 number1 floor1 kept0 step0 rows1 signs0 count0 held1 junk0 steps0 step1 table0 kept1 "
+          "excess0 keep0 signs1 keep1 steps1 junk1 count1 again0 tally1 anew0 again1 spread0 excess1 anew1 lists0 spread1 over0 carry0 carry1")
+TAIL = "S00 w00 S10 V01 S20 S21 V11 w01 l00 V30 w101 l01 s0 W w201 l101 s1 f0 l201 f1 s2 S31 w301 f2 l301 s3 f3"
 
-SCRATCH = {"vl": ("dram", [4, 128, 512], "bfloat16")}
+SCRATCH = {"vl": ("dram", [4, 128, 512], "bfloat16"), "zp": ("sbuf", [128, 4, 80], "float32"), "SG": ("sbuf", [128, 64, 16], "bfloat16")}
 for _d, _l in (
-        ("bfloat16", "win:31744 vw:8192 pw:16 one:256 I1:128 In:128 Hm:144 P1:144 E1:144 P2:144 E2:144 P2k:144 E2k:144 Ta:128 Tb:128 "
-                     "nA:128 nB:128 Cp:144 Cn:144 mg:512 pres:272 Gs:768 Gb:272 Fg:80 keep:256 iE:256 rA:160 junk:1280 LK:2560 "
-                     "t2:1280 Y:1280 YL:1280 ub:176"),
-        ("int32", "ei:128 ai:128 fi:128 ct:32 pi:8 pb:16 u2:480"),
-        ("float32", "cf:96 cT:32 k5:128 pf:16 pc:32 J:224 iA:128 iB:128 iX:16 iC:144 i3:128 CZ:128 wS:160 i4:8 m3:4 lm:4 q1:128 "
-                    "q2:128 Q:128 bb:16 Z:224 TB:16 rr:512 bt:256 Jb:256 o32:264 GW:264 acc:16 om:160 g1:240 zp:320 u3:160 wT:128 wL:160"),
+        ("bfloat16", "win:31744 vw:8192 one:256 I1:128 In:128 pw:16 Hm:144 P1:144 E1:144 P2:144 E2:144 P2k:144 E2k:144 Ta:128 Tb:128 "
+                     "nA:128 nB:128 Cp:144 Cn:144 mg:512 pres:272 Gs:768 Gb:272 Fg:80 keep:256 iE:128 rA:160 junk:1280 LK:2560 "
+                     "t2:1280 Y:1280 YL:1280 ub:208 Pm:128"),
+        ("int32", "ei:128 ai:128 fi:128 ct:32 pi:8 pb:16 u2:560"),
+        ("float32", "cf:32 cT:32 k5:32 pf:16 pc:32 J:224 iA:128 iB:128 iX:16 iC:144 i3:128 wS:160 i4:8 m3:4 lm:4 q1:128 q2:128 Q:128 "
+                    "bb:16 Z:224 TB:16 rr:768 bt:256 Jb:256 GW:264 acc:24 om:160 g1:240 u3:160 wL:160"),
         ("float16", "ph:256 tt:256 tl:256 s1:272 r4:256 r16:256 U:2048 V:2048"),
-        ("uint16", "ks:128 kl:96 ls:32 lr:32 gl:16 ll:160 lo:160")):
+        ("uint16", "ks:32 ka:128 ke:128 kl:96 ls:32 lr:32 gl:16 ll:160 lo:160")):
     for _e in _l.split():
         SCRATCH[_e.split(":")[0]] = ("sbuf", [128, int(_e.split(":")[1])], _d)
 for _j in range(8):
@@ -81,15 +87,16 @@ def rank_program(g, core, T, topo):
         note(s, r.split(), w.split())
 
     def send(s, rsem, r, items):
-        deps("g", [r], [], None)
+        deps("g", r.split(), [], None)
         trs = []
         for d, src, dst, lo, hi in items:
             rid, pid, _ = topo.addr(cores[d])
             m = sum(1 << e for e in topo.engines(core, cores[d])[lo:hi])
-            trs.append(RemoteDMATransfer(dst_ids=[DstId(rid=rid, pnc=pid)], dma_engine_mask=m, remote_sem=T.sem[rsem], src=src, dst=dst))
+            sides = dict(srcs=src, dsts=[dst], alu_op=1) if isinstance(src, list) else dict(src=src, dst=dst)
+            trs.append(RemoteDMATransfer(dst_ids=[DstId(rid=rid, pnc=pid)], dma_engine_mask=m, remote_sem=T.sem[rsem], **sides))
             count[s] = count.get(s, 0) + hi - lo
         g.remote_dma_fused(trs, local_sem=T.sem[s])
-        note(s, [r], [])
+        note(s, r.split(), [])
 
     def arrives(s, n, w):
         count[s] = n
@@ -127,9 +134,9 @@ def rank_program(g, core, T, topo):
     def mm(r, w, *a):
         op("t", r, w, g.tensor.matmul, *a)
 
-    def mms(w, o, terms):
+    def mms(w, o, terms, start=True, stop=True):
         for j, (r, a, b) in enumerate(terms):
-            mm(r, w, o, a, b, j == 0, j == len(terms) - 1)
+            mm(r, w, o, a, b, start and j == 0, stop and j == len(terms) - 1)
 
     def iota(w, o, pat, base=0):
         op("g", "", w, g.iota, o, pat, base, 0, allow_small_or_imprecise_dtypes=True)
@@ -145,15 +152,15 @@ def rank_program(g, core, T, topo):
     AND, SHR, MUL, ADD, SUB, EQ, MAX, LT_, GE = (A_.bitwise_and, A_.logical_shift_right, A_.mult, A_.add, A_.subtract, A_.is_equal,
                                                  A_.max, A_.is_lt, A_.is_ge)
     E3 = ((0, 4), (4, 8), (8, 16))
-    dmas("lcls", "", "ct", [("ys"[j & 1], T.ct[(j >> 1) * 32 + (j & 1):(j >> 1) * 32 + 32:2, :], T.cls[(j >> 2)::2, :]) for j in range(8)])
     dmas("lkey", "", "ei ai", [it for kk in range(4) for it in (("y", c_("ei", kk * 32, 32), T.ent[2 * kk:2 * kk + 2, :]),
                                                                ("s", c_("ai", kk * 32, 32), T.att[2 * kk:2 * kk + 2, :]))])
     dmas("lform", "", "fi", [("ys"[kk & 1], c_("fi", kk * 32, 32), T.form[2 * kk:2 * kk + 2, :]) for kk in range(4)])
+    dmas("lcls", "", "ct", [("ys"[j & 1], T.ct[(j >> 1) * 32 + (j & 1):(j >> 1) * 32 + 32:2, :], T.cls[(j >> 2)::2, :]) for j in range(8)])
 
     p0 = c_("pi", 0, 1)
     op("g", "", "pi", g.iota, p0, [[0, 1]], 0, 1)
-    iota("iB", T.iB[:], [[0, 4], [1, 32]])
-    iota("iA", T.iA[:], [[2048, 4], [0, 32]])
+    iota("iB", T.iB[:], [[0, 4], [1, 32]], 32)
+    iota("iA", T.iA[:], [[2048, 4], [0, 32]], 32)
     iota("iX", T.iX[:], [[32, 16]])
     iota("one8", c_("one8"), [[0, 4], [-1, 2], [0, 8]], 1)
     iota("FS", c_("FS", 0, 16), [[0, 16]])
@@ -162,7 +169,7 @@ def rank_program(g, core, T, topo):
         for j in js:
             sel("one8", "FS", c_("FS", 16 + j * 64, 64), c_("one8"), [[-16, 2], [0, 2], [-1, 16]], EQ, 0.0,
                 -64 * (j & 1) - 32 * (j >> 2) - 8 * ((j >> 1) & 1), 1)
-    formula_matrices(range(2))
+    formula_matrices(range(5))
     fill("wz0", c_("win", SH, 1024))
     dmas("zero", "wz0", "wrow", [("y", win[x::16, 16384:16384 + SH], c_("win", SH, SH // 16)) for x in range(3)])
     pb = [c_("pb", j, 1) for j in range(9)]
@@ -173,298 +180,350 @@ def rank_program(g, core, T, topo):
         for j, (sh, m) in enumerate(fields):
             ts2("pi", "pb%d" % a, pb[a + j], p0, sh, m, SHR, AND)
         cp("pb%d" % a, "pf%d" % a, c_("pf", a, len(fields)), c_("pb", a, len(fields)))
+    fill("one", T.one[:], 1.0)
     bits(0, ((0, 15), (4, 3), (0, 1)))
-    ts1("iB pf0", "m3", c_("m3", 0, 3), c_("iB", 0, 3), pf[0], EQ)
+    ts2("iB pf0", "m3", c_("m3", 0, 3), c_("iB", 0, 3), -32.0, pf[0], ADD, EQ)
     ts1("pf0", "pc0", pc[0], pf[1], 512.0, MUL)
-    ts2("pf0", "pc1", pc[1], pf[2], 256.0, 32.0 * k, MUL, ADD)
+    ts2("pf0", "pc1", pc[1], pf[2], 256.0, 64.0 * k, MUL, ADD)
     m0, m1, m2 = c_("m3", 0, 1), c_("m3", 1, 1), c_("m3", 2, 1)
-    ts2("iB m3", "q2", T.q2[:], T.iB[:], m1, m2, MUL, ADD)
+    ts1("m3", "pc2", pc[2], m2, 32.0, MUL)
     ts2("iA m3 pc0", "q1", T.q1[:], T.iA[:], pc[0], m0, ADD, MUL)
-    ts1("iX m3", "bb", T.bb[:], T.iX[:], m0, MUL)
+    ts2("iB m3 pc2", "q2", T.q2[:], T.iB[:], m1, pc[2], MUL, ADD)
+    act("iX m3", "bb", T.bb[:], T.iX[:], F_.Identity, scale=m0)
     tt("q1 q2", "Q", T.Q[:], T.q1[:], T.q2[:], ADD)
+    bits(4, ((0, 64), (0, 3), (2, 3), (0, 0x70), (0, 0x7C)))
     for x in range(16):
         act("Q bb", "pay", c_("pay", x, None, 16), T.Q[:], F_.Identity, bias=c_("bb", x, 1))
 
-    ts2("ct", "cf0", c_("cf", 0, 32), T.ct[:], 32.0, 96.0, GE, MUL)
-    ts1("ct pc1", "cf1", c_("cf", 32, 32), T.ct[:], pc[1], ADD)
-    tt("cf0 cf1", "cf2", c_("cf", 64, 32), c_("cf", 0, 32), c_("cf", 32, 32), ADD)
-    tr("cf2", "cT", T.cT[:], c_("cf", 64, 32))
-    cp("cT", "ls", T.ls[:], T.cT[:])
-    send("slist", "alist", "ls", [(d, c_("ls", d * 8, 8), c_("lr", k * 8, 8)) + E3[j] for j, d in enumerate(others)])
-    arrives("alist", 16, "lr")
-    ts1("ai", "B7", c_("B7", 0, 128), T.ai[:], 512.0, MUL)
-    tt("B7 ei", "k5", T.k5[:], c_("B7", 0, 128), T.ei[:], ADD)
-    cp("k5", "ks", T.ks[:], T.k5[:])
-    send("skey", "akey", "ks", [(d, c_("ks", d * 32, 32), c_("kl", j * 32, 32)) + E3[j] for j, d in enumerate(others)])
+    ts1("ai", "ka", T.ka[:], T.ai[:], 512.0, MUL)
+    cp("ei", "ke", T.ke[:], T.ei[:])
+    send("skey", "akey", "ka ke", [(d, [c_("ka", d * 32, 32), c_("ke", d * 32, 32)], c_("kl", j * 32, 32)) + E3[j] for j, d in enumerate(others)])
     arrives("akey", 16, "kl")
-    cp("fi", "ph", c_("ph", 0, 128), T.fi[:])
-    ts2("fi", "ph", c_("ph", 128, 128), T.fi[:], 1.0 / 32, 1536 - 0.484375, MUL, ADD)
+    ts1("fi", "f12", c_("u2", 0, 128), T.fi[:], 31, AND)
+    ts1("fi", "f12", c_("u2", 128, 128), T.fi[:], 5, SHR)
+    ts1("ct pc1", "cf", T.cf[:], T.ct[:], pc[1], ADD)
+    ts1("ai", "B7", c_("B7", 0, 32), c_("ai", k * 32, 32), 512.0, MUL)
+    cp("f12", "ph", T.ph[:], c_("u2", 0, 256))
     tr("ph", "tt", T.tt[:], T.ph[:])
     send("sform", "aform", "tt", [(d, c_("tt", f * 128 + d * 32, 32), c_("tl", f * 128 + k * 32, 32), 4 * j + 2 * f, 4 * j + 2 * f + 2)
                                   for j, d in enumerate(others) for f in range(2)])
     arrives("aform", 12, "tlrem")
+    tt("B7 ei", "k5", T.k5[:], c_("B7", 0, 32), c_("ei", k * 32, 32), ADD)
+    tr("cf", "cT", T.cT[:], T.cf[:])
     for f in range(2):
         cp("tt", "tlown", c_("tl", f * 128 + k * 32, 32), c_("tt", f * 128 + k * 32, 32))
-    bits(3, ((3, 1), (0, 64), (0, 3), (2, 3), (0, 0x70), (0, 0x7C)))
-    formula_matrices(range(2, 8))
-    act("pf0", "pw", c_("pw", 0, 1), pf[0], F_.Exp, scale=LN2, bias=LN2)
-    act("pf3", "pc10", pc[10], pf[3], F_.Identity, scale=-49152.0 - 1536.0, bias=49152.0)
+    cp("k5", "ks", T.ks[:], T.k5[:])
+    cp("cT", "ls", T.ls[:], T.cT[:])
+    cp("cT", "lrown", c_("lr", k * 8, 8), c_("cT", k * 8, 8))
+    send("slist", "alist", "ls", [(d, c_("ls", d * 8, 8), c_("lr", k * 8, 8)) + E3[j] for j, d in enumerate(others)])
+    arrives("alist", 16, "lr")
+    formula_matrices(range(5, 8))
+    act("pf0", "pw", c_("pw", 0, 1), pf[0], F_.Exp, scale=LN2, bias=-4 * LN2)
     act("pw", "pc9", pc[9], c_("pw", 0, 1))
     for j, (a, sc, b) in enumerate((
-            (6, 32.0, Z0), (5, 32.0, Z0),
+            (6, 32.0, 0.0), (5, 32.0, 0.0),
             (8, 1.0, 3.0), (7, 1.0, pf[5]),
             (4, 1.0, pf[0]), (7, 1.0, 15.0),
-            (4, 0.25, pf[0]), (5, 20.0, pf[6]),
+            (4, 0.25, pf[0]), (1, 32.0, pf[0]),
             (0, -1.0 / 16, 160 + 15.0 / 16 - 0.46875), (5, 1.0, -2.0), (4, 1.0 / 128, pf[1]))):
-        act("pf0 pf3", "pcs", pc[11 + j], pf[a], F_.Relu if j == 9 else F_.Identity, scale=sc, bias=b)
+        act("pf0 pf4", "pcs", pc[11 + j], pf[a], F_.Relu if j == 9 else F_.Identity, scale=sc, bias=b)
     act("pcs", "pc20", pc[20], pc[20], F_.Identity, scale=-1024.0, bias=1024.0)
     act("pcs", "pc22", pc[22], pc[21], F_.Identity, scale=2.0, bias=1.0)
-    for j in range(3):
-        act("pcs", "th", c_("q1", j, 1), pc[11], F_.Identity, bias=0.5 - 512.0 * (j + 1))
+    act("pf4 pcs", "pc18", pc[18], pf[4], F_.Identity, scale=0.25, bias=pc[18])
     act("m3", "pc5", pc[5], m0, F_.Identity, bias=m1)
     act("pc22 m3", "pc23", pc[23], pc[22], F_.Identity, scale=m0, bias=-1.0)
-    scaled("FS", "FN", -32.0)
     wait("y", "skey", count["skey"])
     dmas("lval", "", "vs", [("y", c_("vs", j * 512, 512), T.val[32 * d:32 * d + 32, :]) for j, d in enumerate(others)])
+
+    def scatter(key, a, n):
+        op("v", "tab pay " + key, "wz0 wrow tab", V.tensor_copy, c_("win", SH, 16384).indirect(T[key][:]), c_("pay", a, n))
+    scatter("ks", 0, 512)
+    fill("SG0", T.SG[:, 0::2, :])
+    fill("pres0", T.pres[:, 0:258:257])
+    fill("GWp", T.GW[:, 0:258:257])
+    fill("ub0", c_("ub", 160, 48))
+    scatter("kl", 512, 1536)
+    one = c_("one", 0, 128)
+    sel("one", "I1", T.I1[:], one, [[-1, 128]], EQ, 0.0, 0, 1)
     iota("J", T.J[:], [[1, 224]])
     iota("iC", c_("iC", 0, 16), [[0, 16]], 999)
     iota("iC", c_("iC", 16, 128), [[64, 2], [0, 4], [1, 16]])
-    iota("one", T.one[:], [[0, 256]], 1)
-    send("sval", "aval", "vs", [(d, c_("vs", j * 512, 512), T.vl[k]) + E3[j] for j, d in enumerate(others)])
-    arrives("aval", 16, "vl")
-    one = c_("one", 0, 128)
-    sel("one", "I1", T.I1[:], one, [[-1, 128]], EQ, 0.0, 0, 1)
     sel("one", "N1", c_("N1"), one, [[-16, 8], [0, 16]], GE, 0.0, 0, 1)
     iota("i3", T.i3[:], [[0, 32], [1, 4]])
     sel("N1", "NW", c_("NW"), c_("N1"), [[16, 8], [0, 16]], GE, 0.0, 15, -1)
-    iota("i4", T.i4[:], [[4, 8]], 1)
-    sel("NW", "GT", c_("GT"), c_("NW"), [[-1, 128]], GE, 0.0, -1, 1)
+    iota("i4", T.i4[:], [[16, 8]], 1)
     sel("NW", "RW", c_("RW"), c_("NW"), [[-1, 128]], GE, 0.0, 0, 1)
     sel("NW", "LT", c_("LT"), c_("NW"), [[1, 128]], GE, 0.0, -1, -1)
-    iota("nA", T.nA[:], [[0, 8], [128, 4], [0, 4]], -384)
-    iota("rest", c_("rest"), [[0, AT["rest"][1]]])
-    iota("iE", T.iE[:], [[0, 8], [128, 32]])
-    iota("rA", c_("rA", 0, 80), [[-1, 20], [-20, 4]], -161)
-    iota("rA", c_("rA", 80, 80), [[1, 20], [20, 4]], 162)
+    sel("NW", "GT", c_("GT"), c_("NW"), [[-1, 128]], GE, 0.0, -1, 1)
+
+    def spread(s, names, rows):
+        dmas(s, "tab", names, [("y", c_(nm, x * 512, 512), win[row::16, SH + x * 8192:SH + x * 8192 + 8192])
+                               for nm, row in zip(names.split(), rows) for x in range(2)])
 
     def windows(s, r, rs):
         dmas(s, r, s, [("y", T.vw[c * 32:c * 32 + 32, (k - q) % 4 * 2048:(k - q) % 4 * 2048 + 2048],
                         T.val[32 * k:32 * k + 32, :] if q == k else T.vl[q]) for q in rs for c in range(4)])
 
-    for key, off, a, n in (("ks", c_("ks", k * 32, 32), 0, 512), ("kl", T.kl[:], 512, 1536)):
-        op("v", "tab pay " + key, "wz0 wrow tab", V.tensor_copy, c_("win", SH, 16384).indirect(off), c_("pay", a, n))
-
-    for j in range(4):
-        a = ((j & 1) * 2 + (j >> 1)) * 128
-        r = "FS FN tlown tlrem"
-        mms("B5", c_("B5", j * 128, 128), [(r, c_("FS", a + 16, 128), c_("tl", 0, 128)), (r, c_("FS", a + 8, 128), c_("tl", 128, 128)),
-                                           (r, c_("FN", a + 16, 128), c_("tl", 128, 128))])
-    act("B5 pc10", "FW", c_("FW"), T.B5[:], F_.Identity, bias=pc[10])
-    for q in range(4):
-        act("FW ls lr", "FG", c_("FG", q * 128, 128), c_("FW").indirect(c_("ls" if q == k else "lr", q * 8, 8)))
-    dmas("wrp", "tab", "pt", [("y", c_("pt", w * 512, 512), win[2::16, SH + w * 8192:SH + w * 8192 + 8192]) for w in range(2)])
-    dmas("wrh", "tab pt", "ht lt", [("y", c_(("ht", "lt")[h]), win[h::16, SH:SH + 16384]) for h in range(2)])
+    for j in range(16):
+        a, q = ((j & 1) * 2 + (j >> 3)) * 128, (j >> 1) & 3
+        mms("B5", c_("B5", j * 32, 32), [("FS tlown tlrem", c_("FS", a + 16 - 8 * f, 128), c_("tl", f * 128 + q * 32, 32)) for f in range(2)])
+    act("pay", "clr", c_("clr", 0, 1280), c_("pay", 0, 1280), F_.Identity, scale=0.0)
+    act("B5", "FW", c_("FW"), T.B5[:])
+    act("FW lrown lr", "FG", c_("FG"), c_("FW").indirect(T.lr[:]))
+    act("pay", "clr", c_("clr", 1280, 768), c_("pay", 0, 768), F_.Identity, scale=0.0)
+    spread("wrp", "pt", [2])
+    spread("wrh", "ht lt", [0, 1])
+    iota("zt", c_("zt"), [[0, 128]])
+    for nm, c in (("I15", -15.5), ("I4k", 4096.0), ("I512", 512.0), ("I32", -32.0), ("I480", -480.0), ("In", -1.0)):
+        sel("zt", nm, c_(nm), c_("zt"), [[-1, 128]], A_.not_equal, c, 0, 1)
+    deps("g", ["pt"], [], None)
+    send("sval", "aval", "vs", [(d, c_("vs", j * 512, 512), T.vl[k]) + E3[j] for j, d in enumerate(others)])
+    arrives("aval", 16, "vl")
+    iota("nA", T.nA[:], [[0, 8], [128, 4], [0, 4]], -384)
+    iota("iE", T.iE[:], [[0, 4], [128, 32]])
+    iota("rest", c_("rest"), [[0, AT["rest"][1]]])
+    iota("rA", c_("rA", 0, 80), [[-1, 80]], -161)
+    iota("rA", c_("rA", 80, 80), [[1, 80]], 162)
     windows("lown", "", [k])
     windows("lwin", "vl", others)
-    for nm, c in (("I4k", 4096.0), ("I512", 512.0), ("I32", -32.0), ("I480", -480.0), ("In", -1.0)):
-        scaled("I1", nm, c)
+    ts2("iC pf4 pc9", "MW", c_("MW"), T.iC[:], pf[4], pc[9], EQ, MUL)
     tr("FG", "Fe", c_("Fe"), c_("FG"))
+    act("Fe", "SG1", T.SG[:, 1::2, :], c_("Fe"), F_.Sign, bias=-15.5)
     for j in range(16):
-        mm("I1 Fe", "B5", c_("B5", j * 32, 32), T.I1[:], c_("Fe", j, None, 16), True, True)
-    act("B5", "SG1", c_("SG", 1, None, 2), T.B5[:], F_.Sign, bias=-15.5)
+        mm("I1 Fe", "B5", c_("B5", j * 32, 32), T.I1[:], c_("Fe", (j >> 2 & 1) * 8 + (j >> 3) * 4 + (j & 3), None, 16), True, True)
     act("B5", "W", c_("W"), T.B5[:], F_.Exp, scale=-LN2, bias=-LN2)
-    act("B5", "fb", c_("fb"), T.B5[:])
-    ts2("iC pf3 pc9", "MW", c_("MW"), T.iC[:], pf[4], pc[9], EQ, MUL)
-    fill("SG0", c_("SG", 0, None, 2))
-    fill("pres0", T.pres[:, 0:258:257])
-    fill("o32", T.o32[:], 1.0)
+    for j in range(4):
+        act("B5 pcs", "fb", c_("fb", j * 128, 128), c_("B5", j * 128, 128), F_.Identity, scale=2.0, bias=pc[11 + (j & 1)])
+    act("B5", "sg", c_("sg"), T.B5[:], F_.Sign, bias=-15.5)
     ts2("J pcs", "ME", c_("ME"), c_("J", 0, 176), -48.0, pc[15], ADD, EQ)
-    ts1("J pcs", "P1", T.P1[:], c_("J", 0, 144), pc[13], EQ)
     ts2("J pcs", "P2", T.P2[:], c_("J", 0, 144), -12.0, pc[14], ADD, EQ)
-    ts2("i3 pf3", "c4", c_("c4"), T.i3[:], pf[5], 128.0, EQ, MUL)
+    ts1("J pcs", "P1", T.P1[:], c_("J", 0, 144), pc[13], EQ)
+    ts2("i3 pf4", "c4", c_("c4"), T.i3[:], pf[5], 128.0, EQ, MUL)
+    ts2("i4 pf0", "TB0", c_("TB", 8, 8), T.i4[:], pf[0], 16.0, ADD, MUL)
     tt("P1", "E1", c_("E1", 0, 143), c_("P1", 0, 143), c_("P1", 1, 143), SUB)
     tt("P2", "E2", c_("E2", 0, 140), c_("P2", 0, 140), c_("P2", 4, 140), SUB)
-    tt("c4 GT", "Ta", T.Ta[:], c_("c4"), c_("GT"), MUL)
-    ts2("i4 pcs", "TB0", c_("TB", 8, 8), T.i4[:], pc[18], 16.0, ADD, MUL)
-    ts2("J pcs", "Z", T.Z[:], T.J[:], -96.0, pc[17], ADD, EQ)
     ts1("TB0", "TB", c_("TB", 0, 8), c_("TB", 8, 8), -0.5, ADD)
+    tt("c4 GT", "Ta", T.Ta[:], c_("c4"), c_("GT"), MUL)
     ts1("J pf0", "lm", T.lm[:], c_("J", 0, 4), pf[1], EQ)
-    fill("GWp", T.GW[:, 0:258:257])
-    sel("o32", "CZ", c_("CZ", 0, 80), c_("o32", 0, 80), [[-32, 4], [-1, 20]], EQ, 0.0, 0, 1)
-    iota("CZ", c_("CZ", 80, 48), [[0, 48]])
+    ts2("J pcs", "Z", T.Z[:], T.J[:], -96.0, pc[17], ADD, EQ)
+    ts1("J pc23", "Cp", T.Cp[:], c_("J", 0, 144), pc[23], EQ)
+    ts1("J pc18", "Pm", T.Pm[:], c_("J", 0, 128), pc[18], EQ)
+    ts2("J pcs pc5", "Hm", T.Hm[:], c_("J", 0, 144), pc[16], pc[5], EQ, MUL)
+    scaled("Cp", "Cn", -1.0)
 
     mms("B0", T.B0[:, 1:128:2], [("one", T.one[0:1, 0:128], T.one[0:1, 0:64])] +
         [("MW pt", c_("MW", 16 - x, 128), c_("pt", x, None, 16)) for x in range(16)])
-    for f in range(2):
-        mm("I1 fb", "B%d" % (4 + 2 * f), c_("B%d" % (4 + 2 * f), 0, 256), T.I1[:], c_("fb", f * 256, 256), True, False)
-    for h in range(2):
-        for x in range(4):
-            mms("B7", T.B7[:, h * 256 + x:h * 256 + 256:4],
-                [("ME ht lt", c_("ME", 48 - 16 * b, 128), c_(("ht", "lt")[h], 4 * x + b, None, 16)) for b in range(4)])
-    act("NW m3", "Rb", c_("Rb"), c_("NW"), F_.Identity, scale=m0)
-    scaled("P2", "P2k", 4096.0)
-    act("E2", "E2k", c_("E2k", 0, 140), c_("E2", 0, 140), F_.Identity, scale=4096.0)
-    scaled("nA", "nB", 4096.0)
-    scaled("Ta", "Tb", 4096.0)
-    act("B7", "mg", T.mg[:], T.B7[:])
-    ts2("B0", "B0", T.B0[:, 0:64:2], T.B0[:, 65:128:2], 131072.0, 65536.0, ADD, MUL)
-    for j in range(16):
-        b = "B%d" % (1 + (j >> 3))
-        scan("SG0 SG1 B0", b, c_(b, (j & 7) * 64, 64), c_("SG", j * 64, 64), c_("B0", 0, 64), 0.0, MUL, MAX)
-    for f in range(2):
-        tt("W B%d" % (1 + f), "B3", c_("B3", f * 256, 256), T["B%d" % (1 + f)][:, 1::2], c_("W", f * 256, 256), MUL)
-    ts2("B3", "rr", T.rr[:], T.B3[:], 1.5 * 2 ** 24, -1.5 * 2 ** 24, ADD, ADD)
-    tt("B3 rr", "B1", c_("B1", 0, 256), c_("B3", 0, 256), c_("rr", 0, 256), LT_)
-    tt("B3 rr", "bt", T.bt[:], c_("B3", 256, 256), c_("rr", 256, 256), LT_)
-    pres = c_("pres", 1, 256)
-    tt("B1 bt", "pres", pres, c_("B1", 0, 256), T.bt[:], MUL)
-    mms("B2", c_("B2", 0, 257), [("LT pres pres0", c_("LT"), c_("pres", 1, 257)), ("RW pres pres0", c_("RW"), c_("pres", 0, 257))])
-    for b in ("B4", "B6"):
-        mm("I4k pres", b, c_(b, 0, 256), c_("I4k"), pres, False, False)
-    ts2("J pcs pc5", "Hm", T.Hm[:], c_("J", 0, 144), pc[16], pc[5], EQ, MUL)
-    ts1("J pc23", "Cp", T.Cp[:], c_("J", 0, 144), pc[23], EQ)
-    s1 = c_("s1", 0, 256)
-    scan("o32 B2", "s1", c_("s1", 0, 257), c_("o32", 0, 257), c_("B2", 0, 257), 0.0, MUL, ADD)
-    ts1("s1", "r16", T.r16[:], s1, 24576 - 7.5, ADD)
-    ts1("s1", "r4", T.r4[:], s1, 6144 - 1.5, ADD)
-    fill("ub0", c_("ub", 160, 16))
-    scaled("Cp", "Cn", -1.0)
-    for b in ("B4", "B6"):
-        for nm, r in (("I512", "s1"), ("I32", "r16"), ("I480", "r4")):
-            mm(nm + " " + r, b, c_(b, 0, 256), c_(nm), c_(r, 0, 256), False, r == "r4")
-        if b == "B4":
-            mm("Rb s1", "B0", c_("B0", 0, 257), c_("Rb"), c_("s1", 0, 257), True, True)
-    dmas("unw", "mg", "tab lk SG0 SG1 " + " ".join(AT), [("y", win[c * 32 + h:c * 32 + 32:16, 0:16384], c_("mg", h * 256, 256))
-                                                         for c in range(4) for h in range(2)])
-    for f in range(2):
-        ts2("B%d pcs" % (4 + 2 * f), "U0", c_("U", f * 256, 256), c_("B%d" % (4 + 2 * f), 0, 256), pc[11 + f], 0.0, ADD, MAX)
-    act("B0 pcs", "Gb", c_("Gb", 0, 257), c_("B0", 0, 257), F_.Identity, scale=1.0 / 16, bias=pc[19])
-    for j in range(3):
-        act("B4 th", "Gs%d" % j, c_("Gs", j * 256, 256), c_("B4", 0, 256), F_.Sign, bias=c_("q1", j, 1))
-    for j in range(1, 4):
-        ts2("U0", "U%d" % j, c_("U", j * 512, 512), c_("U", 0, 512), -512.0 * j, 0.0, ADD, MAX)
+    mm("one SG0", "B7", T.B7[:], T.one[0:1, 0:128], T.SG[0:1, 0::2, :], True, False)
+    ts2("B0", "B0 M", T.B0[:, 0:64:2], T.B0[:, 65:128:2], 131072.0, 65536.0, ADD, MUL)
 
-    def stage1(j):
-        mm("P1 E1 U%d" % j, "B1", T.B1[:], c_("E1" if j else "P1", 3 - j, 128), c_("U", j * 512, 512), j == 0, j == 3)
+    def merge(j, b):
+        nm = ("ht", "lt")[j >> 1]
+        for x in range((j & 1) * 8, (j & 1) * 8 + 8):
+            mm("ME " + nm, "B7", T.B7[:, (j >> 1) * 256 + (x >> 2):(j >> 1) * 256 + 256:4], c_("ME", 48 - 16 * (x & 3), 128), c_(nm, x, None, 16),
+               False, j == 3 and x == 15)
 
-    def excess(j):
-        mm("P1 Gs%d" % j, "B7", c_("B7", 0, 256), c_("P1", 3 - j, 128), c_("Gs", j * 256, 256), j == 0, j == 2)
+    def evac(h, b):
+        act("B7", "mg", T.mg[:], T.B7[:])
 
-    def columns(j):
-        act("B0 TB", "acc", c_("junk", j * 256, 256), c_("B0", 1, 256), F_.Sign, scale=-1.0, bias=c_("TB", j, 1), accum_out=c_("acc", j, 1))
-    for f, j in ((stage1, 0), (excess, 0), (stage1, 1), (excess, 1), (excess, 2), (stage1, 2), (stage1, 3)):
-        f(j)
-    mms("B3", c_("B3", 0, 256), [("I1 Gb", T.I1[:], c_("Gb", 1, 256)), ("In Gb", T.In[:], c_("Gb", 0, 256))])
-    act("Gb", "Gb1", c_("Gb", 257, 1), c_("Gb", 256, 1), F_.Identity, bias=1.0)
-    ts2("B7 pc20", "Jb", T.Jb[:], c_("B7", 0, 256), 256.0, pc[20], MUL, ADD)
-    for j in range(4):
-        columns(j)
-    act("B3", "keep", T.keep[:], c_("B3", 0, 256), F_.Identity, scale=-1.0, bias=1.0)
-    columns(4)
-    X = c_("B5", 0, 256)
-    mm("one iE", "B5", X, T.one[0:1, 0:128], T.iE[0:1, :], True, False)
-    for nm in ("nA", "nB"):
-        mm("one " + nm, "B5", X, T[nm][0:1, :], T.one[0:1, :], False, False)
-    for f in range(2):
-        tt("B1 Jb", "V0%d" % f, c_("V", f * 256, 256), c_("B1", f * 256, 256), T.Jb[:], SUB)
-        mm("P2 P2k V0%d" % f, "B5", X, c_(("P2", "P2k")[f], 12, 128), c_("V", f * 256, 256), False, False)
-    for nm in ("Ta", "Tb"):
-        mm("keep " + nm, "B5", X, T[nm][:], T.keep[:], False, False)
-    for j in range(1, 4):
-        ts2("V00 V01", "V%d" % j, c_("V", j * 512, 512), c_("V", 0, 512), -128.0 * j, 0.0, ADD, MAX)
+    def table(h, b):
+        dmas("unw", "mg", "tab lk " + " ".join(AT), [("y", win[c * 32 + x:c * 32 + 32:16, 0:16384], c_("mg", x * 256, 256))
+                                                     for c in range(4) for x in range(2)])
+
+    def scale(h, b):
+        if h == 0:
+            return act("NW m3", "Rb", c_("Rb"), c_("NW"), F_.Identity, scale=m0)
+        scaled("P2", "P2k", 4096.0)
+        act("E2", "E2k", c_("E2k", 0, 140), c_("E2", 0, 140), F_.Identity, scale=4096.0)
+        scaled("nA", "nB", 4096.0)
+        scaled("Ta", "Tb", 4096.0)
+
+    def open_(h, b):
+        mms(b[2], c_(b[2], 0, 256), [("I1 fb", T.I1[:], c_("fb", h * 256, 256)), ("I15 sg", c_("I15"), c_("sg", h * 256, 256))], stop=False)
+
+    def pick(h, b):
+        for j in range(8):
+            scan("SG0 SG1 M B0", b[1], c_(b[1], j * 64, 64), T.SG[:, :, (j >> 2) * 8 + h * 4 + (j & 3)], c_("B0", 0, 64), 0.0, MUL, MAX)
+
+    def shift(h, b):
+        tt("W " + b[1], b[4], c_(b[4], 0, 256), T[b[1]][:, 1::2], c_("W", h * 256, 256), MUL)
+
+    def round_(h, b):
+        if h == 0:
+            return ts2("B3", "rr0", c_("rr", 0, 256), c_("B3", 0, 256), EVEN, -EVEN, ADD, ADD)
+        act("B5", "rq", c_("rr", 512, 256), c_("B5", 0, 256), F_.Identity, bias=EVEN)
+        act("rq", "rr1", c_("rr", 256, 256), c_("rr", 512, 256), F_.Identity, bias=-EVEN)
+
+    def test(h, b):
+        tt("rr%d %s" % (h, b[4]), b[1], c_(b[1], 0, 128), c_(b[4], 0, 128), c_("rr", h * 256, 128), LT_)
+        tt("rr%d %s" % (h, b[4]), "bt" + b[0], c_("bt", h * 128, 128), c_(b[4], 128, 128), c_("rr", h * 256 + 128, 128), LT_)
+
+    def both(h, b):
+        tt(b[1] + " bt" + b[0], "pres" + b[0] * 2, c_("pres", 1 + h * 128, 128), c_(b[1], 0, 128), c_("bt", h * 128, 128), MUL)
+        r = " pres0 pres00 pres" + b[0] * 2
+        mm("RW" + r, b[1], c_(b[1], 128, 129), c_("RW"), c_("pres", h * 128, 129), True, False)
+        mm("LT" + r, b[1], c_(b[1], 128, 128), c_("LT"), c_("pres", h * 128 + 1, 128), False, True)
         for f in range(2):
-            mm("E2 E2k V%d" % j, "B5", X, c_(("E2", "E2k")[f], 12 - 4 * j, 128), c_("V", j * 512 + f * 256, 256), False, j + f == 4)
-        if j == 1:
-            ts2("acc", "gl1", c_("gl", 6, 5), c_("acc", 0, 5), 0.5, 129.0, MUL, ADD)
-        if j == 2:
-            act("Gb Gb1 gl1", "Fg", T.Fg[:], T.Gb[:].indirect(c_("gl", 6, 5)))
-            for h, nm in enumerate(("I1", "In")):
-                mms("B4", c_("B4", h * 80, 80), [("one rA", T.one[0:1, 0:128], T.rA[0:1, h * 80:h * 80 + 80]), (nm + " Fg", T[nm][:], T.Fg[:])])
-            act("B4", "om", T.om[:], c_("B4", 0, 160), F_.Relu)
-    ts2("acc", "gl0", c_("gl", 0, 5), c_("acc", 0, 5), 0.5, 128.0, MUL, ADD)
-    scan("keep B5", "GWf", c_("GW", 1, 256), T.keep[:], X, 0.0, MUL, MAX)
+            mm("I4k" + r, b[2], c_(b[2], f * 128, 128), c_("I4k"), c_("pres", h * 128 + 1, 128), False, False)
+
+    def route(h, b, nm, r, a):
+        for f in range(2):
+            mm("%s %s%d" % (nm, r, h), b[2], c_(b[2], f * 128, 128), c_(nm), c_(r, a, 128), False, r == "r4" and f == 1)
+
+    def number(h, b):
+        scan("one s10 " + b[1], "s1" + b[0], c_("s1", h * 136, 129), c_("one", 0, 129), c_(b[1], 128, 129), c_("s1", 127, 1) if h else 0.0, MUL, ADD)
+        route(h, b, "I512", "s1", h * 136)
+
+    def floor(h, b):
+        for nm, r, c in (("I32", "r16", 24576 - 7.5), ("I480", "r4", 6144 - 1.5)):
+            ts1("s1" + b[0], r + b[0], c_(r, h * 128, 128), c_("s1", h * 136, 128), c, ADD)
+            route(h, b, nm, r, h * 128)
+
+    def rows(h, b):
+        mm("Rb s1" + b[0], "B0", c_("B0", 128 + h * 129, 129 - h), c_("Rb"), c_("s1", h * 137, 129 - h), True, True)
+
+    def held(h, b):
+        act("B0 pcs", "Gb" + b[0], c_("Gb", h * 129, 129 - h), c_("B0", 128 + h * 129, 129 - h), F_.Identity, scale=1.0 / 16, bias=pc[19])
+
+    def kept(h, b):
+        mms(b[3], c_(b[3], 256, 128), [("I1 Gb0 Gb" + b[0], T.I1[:], c_("Gb", h * 128 + 1, 128)), ("In", T.In[:], c_("Gb", h * 128, 128))])
+
+    def keep(h, b):
+        act(b[3], "keep" + b[0], c_("keep", h * 128, 128), c_(b[3], 256, 128), F_.Identity, scale=-1.0, bias=1.0)
+
+    def count_(h, b, js=(2, 3, 4)):
+        for j in js:
+            act("B0 TB", "acc" + b[0], c_("junk", j * 256 + h * 128, 128), c_("B0", 129 + h * 128, 128), F_.Sign, scale=-1.0, bias=c_("TB", j, 1),
+                accum_out=c_("acc", h * 8 + j, 1))
+
+    def stage1(h, b, j):
+        mm("P1 E1 U%d%d" % (h, j), b[1], c_(b[1], 0, 256), c_("E1" if j else "P1", 3 - j, 128), c_("U", h * 1024 + j * 256, 256), j == 0, j == 3)
+
+    def step(h, b):
+        ts2(b[2], "U%d0" % h, c_("U", h * 1024, 256), c_(b[2], 0, 256), Z0, 0.0, ADD, MAX)
+        stage1(h, b, 0)
+
+    def steps(h, b):
+        for j in range(1, 4):
+            ts2("U%d0" % h, "U%d%d" % (h, j), c_("U", h * 1024 + j * 256, 256), c_("U", h * 1024, 256), -512.0 * j, 0.0, ADD, MAX)
+            stage1(h, b, j)
+
+    def signs(h, b):
+        for j in range(3):
+            act(b[2], "Gs%d%d" % (h, j), c_("Gs", h * 384 + j * 128, 128), c_(b[2], 0, 128), F_.Sign, bias=Z0 + 0.5 - 512.0 * (j + 1))
+
+    def junk(h, b):
+        mms("B3", c_("B3", h * 128, 128), [("P1 Gs%d%d" % (h, j), c_("P1", 3 - j, 128), c_("Gs", h * 384 + j * 128, 128)) for j in range(3)])
+
+    def excess(h, b):
+        ts2("B3 pc20", "Jb" + b[0], c_("Jb", h * 128, 128), c_("B3", h * 128, 128), 256.0, pc[20], MUL, ADD)
+
+    def again(h, b):
+        mms(b[3], c_(b[3], 0, 128), [("one iE", T.one[0:1, 0:128], T.iE[0:1, :])] +
+            [("one " + nm, T[nm][0:1, :], T.one[0:1, 0:128]) for nm in ("nA", "nB")] +
+            [("keep%d %s" % (h, nm), T[nm][:], c_("keep", h * 128, 128)) for nm in ("Ta", "Tb")], stop=False)
+
+    def anew(h, b):
+        for f in range(2):
+            tt("%s Jb%d" % (b[1], h), "V%d0%d" % (h, f), c_("V", h * 1024 + f * 128, 128), c_(b[1], f * 128, 128), c_("Jb", h * 128, 128), SUB)
+            mm("P2 P2k V%d0%d" % (h, f), b[3], c_(b[3], 0, 128), c_(("P2", "P2k")[f], 12, 128), c_("V", h * 1024 + f * 128, 128), False, False)
+
+    def spread_(h, b):
+        for j in range(1, 4):
+            ts2("V%d00 V%d01" % (h, h), "V%d%d" % (h, j), c_("V", h * 1024 + j * 256, 256), c_("V", h * 1024, 256), -128.0 * j, 0.0, ADD, MAX)
+            for f in range(2):
+                mm("E2 E2k V%d%d" % (h, j), b[3], c_(b[3], 0, 128), c_(("E2", "E2k")[f], 12 - 4 * j, 128), c_("V", h * 1024 + j * 256 + f * 128, 128),
+                   False, j + f == 4)
+
+    def carry(h, b):
+        scan("keep%d GW0 %s" % (h, b[3]), "GW" + b[0], c_("GW", 1 + h * 128, 128), c_("keep", h * 128, 128), c_(b[3], 0, 128),
+             c_("GW", 128, 1) if h else 0.0, MUL, MAX)
+
+    def lists(h, b):
+        tt("acc0 acc1", "acc", c_("acc", 16, 5), c_("acc", 0, 5), c_("acc", 8, 5), ADD)
+        act("Gb1", "Gb2", c_("Gb", 257, 1), c_("Gb", 256, 1), F_.Identity, bias=1.0)
+        for j in (1, 0):
+            ts2("acc", "gl%d" % j, c_("gl", 6 * j, 5), c_("acc", 16, 5), 0.5, 128.0 + j, MUL, ADD)
+
+    def over(h, b):
+        act("Gb0 Gb1 Gb2 gl1", "Fg", T.Fg[:], T.Gb[:].indirect(c_("gl", 6, 5)))
+        for j, nm in enumerate(("I1", "In")):
+            mms("B6", c_("B6", j * 80, 80), [("one rA", T.one[0:1, 0:128], T.rA[0:1, j * 80:j * 80 + 80]), (nm + " Fg", T[nm][:], T.Fg[:])])
+        act("B6", "om", T.om[:], c_("B6", 0, 160), F_.Relu)
+    for st in MIDDLE.split():
+        h = int(st[-1])
+        {"pick": pick, "shift": shift, "round": round_, "test": test, "both": both, "number": number, "floor": floor, "rows": rows, "kept": kept,
+         "count": count_, "step": step, "steps": steps, "signs": signs, "excess": excess, "again": again, "spread": spread_, "carry": carry,
+         "lists": lists, "over": over, "junk": junk, "keep": keep, "held": held, "anew": anew, "scale": scale, "merge": merge, "evac": evac,
+         "table": table, "open": open_, "tally": lambda h, b: count_(h, b, (0, 1))
+         }[st[:-1]](h, (str(h), "B%d" % (1 + h), "B%d" % (4 + 2 * h), "B%d" % (5 - h), "B%d" % (3 + 2 * h)))
     g1 = [c_("g1", j * 80, 80) for j in range(3)]
     for j in range(2):
-        tt("GWf GWp gl%d om" % j, "g%d" % j, g1[j], T.GW[:].indirect(c_("gl", 6 * j, 5)), c_("om", j * 80, 80), MUL)
+        tt("GW0 GW1 GWp gl%d om" % j, "g%d" % j, g1[j], T.GW[:].indirect(c_("gl", 6 * j, 5)), c_("om", j * 80, 80), MUL)
     tt("g0 g1", "g2", g1[2], g1[0], g1[1], ADD)
     for j, d in enumerate(order):
-        ts1("g2 lm", "zp", c_("zp", j * 80, 80), g1[2], c_("lm", d, 1), MUL)
-    mms("B0", c_("B0", 0, 80), [("Z zp", c_("Z", 96 - 32 * c, 128), T.zp[:, c::4]) for c in range(4)])
-    u2 = [c_("u2", j * 80, 80) for j in range(6)]
+        ts1("g2 lm", "zp", T.zp[:, :, j * 20:j * 20 + 20], g1[2], c_("lm", d, 1), MUL)
+    mms("B0", c_("B0", 0, 80), [("Z zp", c_("Z", 96 - 32 * c, 128), T.zp[:, c, :]) for c in range(4)])
+    u2 = [c_("u2", j * 80, 80) for j in range(7)]
     u3 = [c_("u3", j * 80, 80) for j in range(2)]
+    ts2("g2", "e0", u2[4], g1[2], 1.0 / 32, -0.484375, MUL, ADD)
+    ts1("g2", "c2", u3[1], g1[2], 0.0, EQ)
+    ts1("e0", "a3", u2[5], u2[4], 127, AND)
+    ts1("e0", "a4", u2[6], u2[4], 12, SHR)
+    ts1("a3", "c3", c_("ub", 0, 80), u2[5], 4.0, MUL)
+    tt("a4 c2", "c4b", c_("ub", 80, 80), u2[6], u3[1], SUB)
+    for d in range(4):
+        for h in range(2):
+            mms("B2", c_("B2", d * 40 + 32 + 4 * h, 4), [("Cp s10 s11", c_("Cp", 2 * d, 128), c_("s1", h * 136 + 32, 97, 32)),
+                                                        ("Cn", c_("Cn", 2 * d, 128), c_("s1", h * 136, 97, 32))])
+    for d in range(4):
+        mms("B2", c_("B2", d * 40, 32), [("Pm c3 c4b ub0", c_("ub", h * 80, 128), c_("Pm", d * 32, 32)) for h in range(2)])
     lw = c_("win", 0, 16384)
     word = c_("B0", 0, 80)
+    banks = {}
 
     def look(f, j, h):
         f("ll%d lk" % h, "LK%d%d" % (j, h), c_("LK", j * 640 + h * 320, 320), lw.indirect(c_("ll", h * 80 + j * 20, 20)))
 
-    def wrap(j):
-        b = "B%d" % (3 + j)
-        mms(b, c_(b, 0, 40), [("Hm LK%d0 LK%d1" % (j, j), c_("Hm", 15 - x, 128), c_("LK", j * 640 + x, 640 - x, 16)) for x in range(16)])
+    def wrap(j, hs):
+        b = banks[j, hs[0]] = "B%d" % (3 + len(banks) % 5)
+        a, n = j * 640 + hs[0] * 320, 320 * len(hs)
+        mms(b, c_(b, 0, n // 16), [("Hm " + " ".join("LK%d%d" % (j, h) for h in hs), c_("Hm", 15 - x, 128), c_("LK", a + x, n - x, 16))
+                                   for x in range(16)])
 
-    def lst(j):
-        cp("B%d" % (3 + j), "lo%d" % j, c_("lo", j * 40, 40), c_("B%d" % (3 + j), 0, 40))
+    def lst(j, hs):
+        b = banks[j, hs[0]]
+        ts1(b, " ".join("lo%d%d" % (j, h) for h in hs), c_("lo", j * 40 + hs[0] * 20, 20 * len(hs)), c_(b, 0, 20 * len(hs)), -64.0, ADD)
 
     def second(j):
-        act("lo%d lown lwin" % j, "t2%d" % j, c_("t2", j * 320, 320), T.vw[:].indirect(c_("lo", j * 40, 20)))
+        act("lo%d0 lown lwin" % j, "t2%d" % j, c_("t2", j * 320, 320), T.vw[:].indirect(c_("lo", j * 40, 20)))
 
     def first(j):
         d = order[j]
-        tt("lo%d lown lwin t2%d" % (j, j), "Y%d" % d, c_("Y", j * 320, 320), T.vw[:].indirect(c_("lo", j * 40 + 20, 20)),
+        tt("lo%d1 lown lwin t2%d" % (j, j), "Y%d" % d, c_("Y", j * 320, 320), T.vw[:].indirect(c_("lo", j * 40 + 20, 20)),
            c_("t2", j * 320, 320), SUB)
         if d != k:
             send("sy%d" % d, "ay%d" % k, "Y%d" % d, [(d, c_("Y", j * 320, 320), c_("YL", k * 320, 320), 0, 16)])
+
+    def entities():
+        act("B2", "wS", T.wS[:], c_("B2", 0, 160))
+        send("swho", "awho", "wS", [(d, c_("wS", d * 40, 40), c_("wL", k * 40, 40), 4 * j, 4 * j + 4) for j, d in enumerate(far_first)])
+        arrives("awho", 12, "wL")
+        for s, nm, ks in (("who1", "wS", [k]), ("who2", "wL", others)):
+            dmas(s, nm, "", [it for kk in ks for c0 in [kk * 40]
+                             for it in (("y", T.who[2 * kk:2 * kk + 1, :], T[nm][0:80, c0:c0 + 16]),
+                                        ("y", T.who[2 * kk + 1:2 * kk + 2, :], T[nm][0:80, c0 + 16:c0 + 32]),
+                                        ("y", T.cnt[2 * kk:2 * kk + 2, :], T[nm][0:2, c0 + 32:c0 + 40]))])
     ts2("B0", "ll0", c_("ll", 0, 80), word, 1.0 / 32, -0.484375, MUL, ADD)
     ts2("B0", "a0", u2[0], word, 1.0 / 32, -0.484375, MUL, ADD)
     ts1("B0", "u1", u2[1], word, 128.0, MUL)
-    look(act, 0, 0)
-    look(act, 1, 0)
     ts1("a0", "a2", u2[2], u2[0], 0x307F, AND)
     ts1("u1", "a1", u2[3], u2[1], 0xF80, AND)
-    ts1("a0", "a3", u2[4], u2[0], 127, AND)
     tt("a1 a2", "c1", u3[0], u2[2], u2[3], ADD)
-    ts1("a0", "a4", u2[5], u2[0], 12, SHR)
     cp("c1", "ll1", c_("ll", 80, 80), u3[0])
-    ts1("a0", "c2", u3[1], u2[0], 0.0, EQ)
-    look(cp, 0, 1)
-    look(act, 1, 1)
-    look(act, 2, 0)
-    for j, d in enumerate(order):
-        mms("B2", c_("B2", j * 40 + 32, 8), [("Cp s1", c_("Cp", 2 * d, 128), T.s1[:, 32:257:32]), ("Cn s1", c_("Cn", 2 * d, 128), T.s1[:, 0:256:32])])
-    wrap(0)
-    ts1("a3", "c3", c_("ub", 0, 80), u2[4], 4.0, MUL)
-    tt("a4 c2", "c4b", c_("ub", 80, 80), u2[5], u3[1], SUB)
-    for j in range(4):
-        mms("B1", c_("B1", j * 32, 32), [("I1 c3 c4b ub0", T.I1[:], c_("ub", h * 80 + j * 20, 32)) for h in range(2)])
-    wrap(1)
-    lst(0)
-    look(act, 3, 0)
-    second(0)
-    tr("B1", "wT", T.wT[:], c_("B1", 0, 128))
-    look(cp, 2, 1)
-    for j in range(4):
-        mm("CZ wT", "B2", c_("B2", j * 40, 32), T.CZ[:], c_("wT", j * 32, 32), True, True)
-    wrap(2)
-    lst(1)
-    act("B2", "wS", T.wS[:], c_("B2", 0, 160))
-    send("swho", "awho", "wS", [(d, c_("wS", j * 40, 40), c_("wL", k * 40, 40), 4 * j, 4 * j + 4) for j, d in enumerate(far_first)])
-    arrives("awho", 12, "wL")
-    for s, nm, ks in (("who1", "wS", [k]), ("who2", "wL", others)):
-        dmas(s, nm, "", [it for kk in ks for c0 in [120 if kk == k else kk * 40]
-                         for it in (("y", T.who[2 * kk:2 * kk + 1, :], T[nm][0:80, c0:c0 + 16]),
-                                    ("y", T.who[2 * kk + 1:2 * kk + 2, :], T[nm][0:80, c0 + 16:c0 + 32]),
-                                    ("y", T.cnt[2 * kk:2 * kk + 2, :], T[nm][0:2, c0 + 32:c0 + 40]))])
-    second(1)
-    first(0)
-    lst(2)
-    second(2)
-    first(1)
-    look(act, 3, 1)
-    first(2)
-    wrap(3)
-    lst(3)
-    second(3)
-    first(3)
+    for st in TAIL.split():
+        j, hs = int(st[1:2] or 0), [int(x) for x in st[2:]]
+        {"S": lambda: look(act, j, hs[0]), "V": lambda: look(cp, j, hs[0]), "w": lambda: wrap(j, hs), "l": lambda: lst(j, hs),
+         "s": lambda: second(j), "f": lambda: first(j), "W": entities}[st[0]]()
     for r in others:
         arrives("ay%d" % r, 16, "YL%d" % r)
     for r in far_first[:2] + [k] + far_first[2:]:

@@ -5,8 +5,8 @@ from concourse.mybir import AluOpType, ActivationFunctionType
 A_ = AluOpType
 F_ = ActivationFunctionType
 SH = 15360
-SPENT = ("pay:2048 vs:1536 pt:1024 ht:1024 lt:1024 clr:2048 sg:512 W:512 FW:512 FG:512 Fe:512 fb:512 FS:528 MW:144 "
-         "ME:176 c4:128 GT:128 NW:128 LT:128 RW:128 I4k:128 I512:128 I32:128 I15:128 I480:128 N1:128 one8:64 zt:128 Rb:128")
+SPENT = ("pay:2048 vs:1536 pt:1024 ht:1024 lt:1024 clr:2048 sg:512 FW:512 FG:512 Fe:512 fb:512 FS:528 MW:144 "
+         "ME:176 c4:128 GT:128 NW:128 LT:128 RW:128 I4k:128 I512:128 I32:128 I15:128 N1:128 one8:64 zt:128 Rb:128 ph:256 tt:256 tl:256")
 AT = {}
 for _e in SPENT.split():
     AT[_e.split(":")[0]] = (sum(n for _, n in AT.values()), int(_e.split(":")[1]))
@@ -14,26 +14,30 @@ AT["rest"] = (sum(n for _, n in AT.values()), SH - sum(n for _, n in AT.values()
 LN2 = math.log(2.0)
 Z0 = 480.0 * 6144 + 32.0 * 24576 - 4096 - 15.5
 EVEN = 1.5 * 2 ** 24
-MIDDLE = ("merge0 merge1 merge2 merge3 pick1 pick0 shift1 shift0 open1 round0 scale0 round1 test0 test1 open0 both0 scale1 both1 "
-          "number0 rows0 floor0 evac0 tally0 held0 number1 floor1 kept0 step0 rows1 signs0 count0 held1 junk0 steps0 step1 table0 kept1 "
-          "excess0 keep0 signs1 keep1 steps1 junk1 count1 again0 tally1 anew0 again1 spread0 excess1 anew1 lists0 spread1 over0 carry0 carry1")
-TAIL = "S00 w00 S10 V01 S20 S21 V11 w01 l00 V30 w101 l01 s0 W w201 l101 s1 f0 l201 f1 s2 S31 w301 f2 l301 s3 f3"
+STEPS = ("pickb0 open0 picka1 picka0 scale1 merge2 roundb0 scale0 pickb1 open1 wipe0 rounda0 rounda1 merge1 merge0 merge3 testb0 roundb1 testa0 "
+         "both0 total0 testb1 testa1 flag0 evac0 both1 number0 wipe1 total1 floor0 rows0 flag1 number1 signs0 rows1 floor1 held0 junk0 again0 "
+         "count0 step0 kept0 step1 steps0 tally0 table0 excess0 held1 signs1 steps1 junk1 anew0 kept1 tally1 count1 lists0 spread0 outside0 "
+         "keep0 over0 excess1 beyond0 keep1 lists1 outside1 again1 anew1 under0 carry0 spread1 over1 close0 beyond1 join0 carry1 move0 under1 "
+         "namea0 close1 nameb0 wipe2 join1 seconds0 firsta0 move1 firstb0 namec0 namea1 firstc0 Sb0 Sb1 firsta1 firstd0 turn0 Sa1 nameb1 "
+         "firstb1 namec1 Sa0 firstc1 wrapb0 seconds1 turn1 firstd1 Vb2 Va2 wrap1 Sa3 wrapa0 wrap2 entities0 list1 Vb3 told0 listb0 lista0 "
+         "second1 list2 second0 first1 wrap3 second2 list3 second3 told1 first0 store1 first2 first3 store3 store0 store2")
 
-SCRATCH = {"vl": ("dram", [4, 128, 512], "bfloat16"), "zp": ("sbuf", [128, 4, 80], "float32"), "SG": ("sbuf", [128, 64, 16], "bfloat16")}
+SCRATCH = {"vl": ("dram", [4, 128, 512], "bfloat16"), "zp": ("sbuf", [128, 8, 40], "float32"), "fi": ("sbuf", [128, 8, 16], "int32"),
+           "f12": ("sbuf", [128, 32, 2, 4], "int32"), "SG": ("sbuf", [128, 96, 16], "bfloat16")}
 for _d, _l in (
-        ("bfloat16", "win:31744 vw:8192 one:256 I1:128 In:128 pw:16 Hm:144 P1:144 E1:144 P2:144 E2:144 P2k:144 E2k:144 Ta:128 Tb:128 "
-                     "nA:128 nB:128 Cp:144 Cn:144 mg:512 pres:272 Gs:768 Gb:272 Fg:80 keep:256 iE:128 rA:160 junk:1280 LK:2560 "
-                     "t2:1280 Y:1280 YL:1280 ub:208 Pm:128"),
-        ("int32", "ei:128 ai:128 fi:128 ct:32 pi:8 pb:16 u2:560"),
-        ("float32", "cf:32 cT:32 k5:32 pf:16 pc:32 J:224 iA:128 iB:128 iX:16 iC:144 i3:128 wS:160 i4:8 m3:4 lm:4 q1:128 q2:128 Q:128 "
-                    "bb:16 Z:224 TB:16 rr:768 bt:256 Jb:256 GW:264 acc:24 om:160 g1:240 u3:160 wL:160"),
-        ("float16", "ph:256 tt:256 tl:256 s1:272 r4:256 r16:256 U:2048 V:2048"),
-        ("uint16", "ks:32 ka:128 ke:128 kl:96 ls:32 lr:32 gl:16 ll:160 lo:160")):
+        ("bfloat16", "win:31744 vw:8192 one:256 I1:128 In:128 I480:128 pw:16 Hm:144 P1:144 E1:144 P2:144 E2:144 P2k:144 E2k:144 Ta:128 Tb:128 "
+                     "nA:128 nB:128 Cp:144 Cn:144 mg:512 pres:272 Gs:768 Gb:288 out:160 Fg:160 keep:256 iE:128 rA:160 junk:1536 LK:2560 "
+                     "t2:1280 Y:1280 YL:1280 ub:416 Pm:64"),
+        ("int32", "ei:128 ai:128 ct:32 pi:8 pb:16 u2:800"),
+        ("float32", "cf:32 cT:32 k5:32 pf:16 pc:32 J:176 iA:128 iB:128 iX:16 iC:144 i3:128 wS:160 i4:8 m3:4 lm:4 q1:128 q2:128 Q:128 "
+                    "bb:16 Z:32 TB:16 rr:768 bt:256 Jb:256 GW:272 Of:128 tot:2 acc:24 om:320 g1:480 u3:240 wL:160"),
+        ("float16", "s1:272 r4:256 r16:256 U:2048 V:2048"),
+        ("uint16", "ks:32 ka:96 ke:96 kl:96 ls:32 lr:32 gl:24 ll:160 lo:160")):
     for _e in _l.split():
         SCRATCH[_e.split(":")[0]] = ("sbuf", [128, int(_e.split(":")[1])], _d)
 for _j in range(8):
     SCRATCH["B%d" % _j] = ("psum", [128, 512], "float32")
-SEMAPHORES = ("pv ps pe pg lkey lcls lform zero lval lown wrp wrh unw lwin alist akey aform aval awho ay0 ay1 ay2 ay3 "
+SEMAPHORES = ("pv ps pe pg lkey lkown lcls lform zero lval lown wrp wrh unw lwin alist akey aform aval awho ay0 ay1 ay2 ay3 "
               "slist skey sform sval swho sy0 sy1 sy2 sy3 who1 who2 st0 st1 st2 st3").split()
 
 
@@ -43,8 +47,7 @@ def rank_program(g, core, T, topo):
         return
     cores = T.cores
     others = [(k + 1) % 4, (k + 2) % 4, (k + 3) % 4]
-    far_first = sorted(others, key=lambda d: topo.die(cores[d]) == topo.die(core))
-    order = far_first + [k]
+    order = sorted(range(4), key=lambda d: (d >> 1 == k >> 1, d == k))
     Q = {"v": g.vector, "s": g.scalar, "t": g.tensor, "g": g, "y": g.sync}
     count, wrote, read = {}, {}, {}
     seen = {q: {} for q in Q}
@@ -152,9 +155,10 @@ def rank_program(g, core, T, topo):
     AND, SHR, MUL, ADD, SUB, EQ, MAX, LT_, GE = (A_.bitwise_and, A_.logical_shift_right, A_.mult, A_.add, A_.subtract, A_.is_equal,
                                                  A_.max, A_.is_lt, A_.is_ge)
     E3 = ((0, 4), (4, 8), (8, 16))
-    dmas("lkey", "", "ei ai", [it for kk in range(4) for it in (("y", c_("ei", kk * 32, 32), T.ent[2 * kk:2 * kk + 2, :]),
-                                                               ("s", c_("ai", kk * 32, 32), T.att[2 * kk:2 * kk + 2, :]))])
-    dmas("lform", "", "fi", [("ys"[kk & 1], c_("fi", kk * 32, 32), T.form[2 * kk:2 * kk + 2, :]) for kk in range(4)])
+    for s, w, ks in (("lkey", "ei ai", others), ("lkown", "eo ao", [k])):
+        dmas(s, "", w, [it for kk in ks for j in [(kk - k - 1) % 4] for it in (("y", c_("ei", j * 32, 32), T.ent[2 * kk:2 * kk + 2, :]),
+                                                                              ("s", c_("ai", j * 32, 32), T.att[2 * kk:2 * kk + 2, :]))])
+    dmas("lform", "", "fi", [("ys"[kk & 1], T.fi[:, 2 * kk:2 * kk + 2, :], T.form[2 * kk:2 * kk + 2, :]) for kk in range(4)])
     dmas("lcls", "", "ct", [("ys"[j & 1], T.ct[(j >> 1) * 32 + (j & 1):(j >> 1) * 32 + 32:2, :], T.cls[(j >> 2)::2, :]) for j in range(8)])
 
     p0 = c_("pi", 0, 1)
@@ -169,11 +173,11 @@ def rank_program(g, core, T, topo):
         for j in js:
             sel("one8", "FS", c_("FS", 16 + j * 64, 64), c_("one8"), [[-16, 2], [0, 2], [-1, 16]], EQ, 0.0,
                 -64 * (j & 1) - 32 * (j >> 2) - 8 * ((j >> 1) & 1), 1)
-    formula_matrices(range(5))
+    formula_matrices(range(4))
     fill("wz0", c_("win", SH, 1024))
     dmas("zero", "wz0", "wrow", [("y", win[x::16, 16384:16384 + SH], c_("win", SH, SH // 16)) for x in range(3)])
-    pb = [c_("pb", j, 1) for j in range(9)]
-    pf = [c_("pf", j, 1) for j in range(9)]
+    pb = [c_("pb", j, 1) for j in range(10)]
+    pf = [c_("pf", j, 1) for j in range(10)]
     pc = [c_("pc", j, 1) for j in range(24)]
 
     def bits(a, fields):
@@ -191,61 +195,62 @@ def rank_program(g, core, T, topo):
     ts2("iB m3 pc2", "q2", T.q2[:], T.iB[:], m1, pc[2], MUL, ADD)
     act("iX m3", "bb", T.bb[:], T.iX[:], F_.Identity, scale=m0)
     tt("q1 q2", "Q", T.Q[:], T.q1[:], T.q2[:], ADD)
-    bits(4, ((0, 64), (0, 3), (2, 3), (0, 0x70), (0, 0x7C)))
+    bits(3, ((5, 1), (0, 64), (0, 3), (2, 3)))
     for x in range(16):
         act("Q bb", "pay", c_("pay", x, None, 16), T.Q[:], F_.Identity, bias=c_("bb", x, 1))
 
-    ts1("ai", "ka", T.ka[:], T.ai[:], 512.0, MUL)
-    cp("ei", "ke", T.ke[:], T.ei[:])
-    send("skey", "akey", "ka ke", [(d, [c_("ka", d * 32, 32), c_("ke", d * 32, 32)], c_("kl", j * 32, 32)) + E3[j] for j, d in enumerate(others)])
-    arrives("akey", 16, "kl")
-    ts1("fi", "f12", c_("u2", 0, 128), T.fi[:], 31, AND)
-    ts1("fi", "f12", c_("u2", 128, 128), T.fi[:], 5, SHR)
+    ts1("ai", "ka", T.ka[:], c_("ai", 0, 96), 512.0, MUL)
+    cp("ei", "ke", T.ke[:], c_("ei", 0, 96))
+    send("skey", "akey", "ka ke", [(d, [c_("ka", j * 32, 32), c_("ke", j * 32, 32)], c_("kl", j * 32, 32), 4 * j, 4 * j + 4)
+                                   for j, d in enumerate(others)])
+    arrives("akey", 12, "kl")
+    for f, (n, o) in enumerate(((31, AND), (5, SHR))):
+        for kk in (0, 2):
+            for h in range(2):
+                ts1("fi", "f12", T.f12[:, f * 16 + kk * 4:f * 16 + kk * 4 + 8, h, :], T.fi[:, 2 * kk + (h ^ 1 ^ kk >> 1):2 * kk + 4:2, :], n, o)
     ts1("ct pc1", "cf", T.cf[:], T.ct[:], pc[1], ADD)
-    ts1("ai", "B7", c_("B7", 0, 32), c_("ai", k * 32, 32), 512.0, MUL)
-    cp("f12", "ph", T.ph[:], c_("u2", 0, 256))
-    tr("ph", "tt", T.tt[:], T.ph[:])
+    ts1("ao", "B7", c_("B7", 0, 32), c_("ai", 96, 32), 512.0, MUL)
+    cp("f12", "ph", c_("ph"), T.f12[:])
+    tr("ph", "tt", c_("tt"), c_("ph"))
     send("sform", "aform", "tt", [(d, c_("tt", f * 128 + d * 32, 32), c_("tl", f * 128 + k * 32, 32), 4 * j + 2 * f, 4 * j + 2 * f + 2)
                                   for j, d in enumerate(others) for f in range(2)])
     arrives("aform", 12, "tlrem")
-    tt("B7 ei", "k5", T.k5[:], c_("B7", 0, 32), c_("ei", k * 32, 32), ADD)
+    tt("B7 eo", "k5", T.k5[:], c_("B7", 0, 32), c_("ei", 96, 32), ADD)
     tr("cf", "cT", T.cT[:], T.cf[:])
-    for f in range(2):
-        cp("tt", "tlown", c_("tl", f * 128 + k * 32, 32), c_("tt", f * 128 + k * 32, 32))
     cp("k5", "ks", T.ks[:], T.k5[:])
     cp("cT", "ls", T.ls[:], T.cT[:])
     cp("cT", "lrown", c_("lr", k * 8, 8), c_("cT", k * 8, 8))
     send("slist", "alist", "ls", [(d, c_("ls", d * 8, 8), c_("lr", k * 8, 8)) + E3[j] for j, d in enumerate(others)])
     arrives("alist", 16, "lr")
-    formula_matrices(range(5, 8))
+    formula_matrices(range(4, 8))
     act("pf0", "pw", c_("pw", 0, 1), pf[0], F_.Exp, scale=LN2, bias=-4 * LN2)
     act("pw", "pc9", pc[9], c_("pw", 0, 1))
+    for f in range(2):
+        act("tt", "tlown", c_("tl", f * 128 + k * 32, 32), c_("tt", f * 128 + k * 32, 32))
+    act("pf0 pf3", "pf7", pf[7], pf[1], F_.Identity, scale=16.0, bias=pf[4])
+    act("pf0 pf3", "pf9", pf[9], pf[3], F_.Identity, scale=-2.0, bias=pf[1])
+    act("pf3 pf7", "pf8", pf[8], pf[6], F_.Identity, scale=4.0, bias=pf[7])
     for j, (a, sc, b) in enumerate((
             (6, 32.0, 0.0), (5, 32.0, 0.0),
             (8, 1.0, 3.0), (7, 1.0, pf[5]),
             (4, 1.0, pf[0]), (7, 1.0, 15.0),
-            (4, 0.25, pf[0]), (1, 32.0, pf[0]),
+            (4, 0.25, pf[0]), (3, 32.0, pf[0]),
             (0, -1.0 / 16, 160 + 15.0 / 16 - 0.46875), (5, 1.0, -2.0), (4, 1.0 / 128, pf[1]))):
-        act("pf0 pf4", "pcs", pc[11 + j], pf[a], F_.Relu if j == 9 else F_.Identity, scale=sc, bias=b)
+        act("pf0 pf3 pf7 pf8", "pcs", pc[11 + j], pf[a], F_.Relu if j == 9 else F_.Identity, scale=sc, bias=b)
     act("pcs", "pc20", pc[20], pc[20], F_.Identity, scale=-1024.0, bias=1024.0)
     act("pcs", "pc22", pc[22], pc[21], F_.Identity, scale=2.0, bias=1.0)
-    act("pf4 pcs", "pc18", pc[18], pf[4], F_.Identity, scale=0.25, bias=pc[18])
+    act("pf3 pcs", "pc18", pc[18], pf[4], F_.Identity, scale=0.25, bias=pc[18])
+    act("pf9", "pc6", pc[6], pf[9], F_.Identity, scale=-1.0, bias=1.0)
     act("m3", "pc5", pc[5], m0, F_.Identity, bias=m1)
     act("pc22 m3", "pc23", pc[23], pc[22], F_.Identity, scale=m0, bias=-1.0)
     wait("y", "skey", count["skey"])
     dmas("lval", "", "vs", [("y", c_("vs", j * 512, 512), T.val[32 * d:32 * d + 32, :]) for j, d in enumerate(others)])
 
-    def scatter(key, a, n):
+    for key, a, n in (("ks", 0, 512), ("kl", 512, 1536)):
         op("v", "tab pay " + key, "wz0 wrow tab", V.tensor_copy, c_("win", SH, 16384).indirect(T[key][:]), c_("pay", a, n))
-    scatter("ks", 0, 512)
-    fill("SG0", T.SG[:, 0::2, :])
-    fill("pres0", T.pres[:, 0:258:257])
-    fill("GWp", T.GW[:, 0:258:257])
-    fill("ub0", c_("ub", 160, 48))
-    scatter("kl", 512, 1536)
     one = c_("one", 0, 128)
     sel("one", "I1", T.I1[:], one, [[-1, 128]], EQ, 0.0, 0, 1)
-    iota("J", T.J[:], [[1, 224]])
+    iota("J", T.J[:], [[1, 176]])
     iota("iC", c_("iC", 0, 16), [[0, 16]], 999)
     iota("iC", c_("iC", 16, 128), [[64, 2], [0, 4], [1, 16]])
     sel("one", "N1", c_("N1"), one, [[-16, 8], [0, 16]], GE, 0.0, 0, 1)
@@ -264,57 +269,65 @@ def rank_program(g, core, T, topo):
         dmas(s, r, s, [("y", T.vw[c * 32:c * 32 + 32, (k - q) % 4 * 2048:(k - q) % 4 * 2048 + 2048],
                         T.val[32 * k:32 * k + 32, :] if q == k else T.vl[q]) for q in rs for c in range(4)])
 
+    def identities(pairs):
+        for nm, c in pairs:
+            sel("zt", nm, c_(nm), c_("zt"), [[-1, 128]], A_.not_equal, c, 0, 1)
+
     for j in range(16):
         a, q = ((j & 1) * 2 + (j >> 3)) * 128, (j >> 1) & 3
         mms("B5", c_("B5", j * 32, 32), [("FS tlown tlrem", c_("FS", a + 16 - 8 * f, 128), c_("tl", f * 128 + q * 32, 32)) for f in range(2)])
-    act("pay", "clr", c_("clr", 0, 1280), c_("pay", 0, 1280), F_.Identity, scale=0.0)
+    act("pay", "SG0", T.SG[:, 0::3, :], c_("pay", 0, 512), F_.Identity, scale=0.0)
+    act("pay", "clr", c_("clr", 0, 768), c_("pay", 0, 768), F_.Identity, scale=0.0)
     act("B5", "FW", c_("FW"), T.B5[:])
     act("FW lrown lr", "FG", c_("FG"), c_("FW").indirect(T.lr[:]))
-    act("pay", "clr", c_("clr", 1280, 768), c_("pay", 0, 768), F_.Identity, scale=0.0)
     spread("wrp", "pt", [2])
     spread("wrh", "ht lt", [0, 1])
     iota("zt", c_("zt"), [[0, 128]])
-    for nm, c in (("I15", -15.5), ("I4k", 4096.0), ("I512", 512.0), ("I32", -32.0), ("I480", -480.0), ("In", -1.0)):
-        sel("zt", nm, c_(nm), c_("zt"), [[-1, 128]], A_.not_equal, c, 0, 1)
+    identities((("I15", -15.5), ("I4k", 4096.0), ("I512", 512.0)))
     deps("g", ["pt"], [], None)
     send("sval", "aval", "vs", [(d, c_("vs", j * 512, 512), T.vl[k]) + E3[j] for j, d in enumerate(others)])
     arrives("aval", 16, "vl")
-    iota("nA", T.nA[:], [[0, 8], [128, 4], [0, 4]], -384)
+    identities((("I32", -32.0), ("I480", -480.0), ("In", -1.0)))
     iota("iE", T.iE[:], [[0, 4], [128, 32]])
     iota("rest", c_("rest"), [[0, AT["rest"][1]]])
-    iota("rA", c_("rA", 0, 80), [[-1, 80]], -161)
-    iota("rA", c_("rA", 80, 80), [[1, 80]], 162)
-    windows("lown", "", [k])
-    windows("lwin", "vl", others)
-    ts2("iC pf4 pc9", "MW", c_("MW"), T.iC[:], pf[4], pc[9], EQ, MUL)
+    for h in range(2):
+        iota("ub0", c_("ub", h * 208 + 160, 48), [[0, 48]])
+    iota("rA", c_("rA", 80, 80), [[-1, 80]], -160)
+    iota("rA", c_("rA", 0, 80), [[1, 80]], 163)
+    windows("lown", "pt", [k])
+    fill("B0", T.B0[:, 2:96:3])
+    fill("Of0", c_("Of", 0, 16))
+    fill("GWp", T.GW[:, 0:137:136])
+    fill("GWp", T.GW[:, 129:266:136])
+    fill("pres0", T.pres[:, 0:137:136])
+    ts2("iC pf3 pc9", "MW", c_("MW"), T.iC[:], pf[4], pc[9], EQ, MUL)
     tr("FG", "Fe", c_("Fe"), c_("FG"))
-    act("Fe", "SG1", T.SG[:, 1::2, :], c_("Fe"), F_.Sign, bias=-15.5)
+    act("Fe", "SG1", T.SG[:, 1::3, :], c_("Fe"), F_.Sign, bias=-15.5)
+    act("Fe", "SG1", T.SG[:, 2::3, :], c_("Fe"), F_.Exp, scale=-LN2, bias=-LN2)
     for j in range(16):
         mm("I1 Fe", "B5", c_("B5", j * 32, 32), T.I1[:], c_("Fe", (j >> 2 & 1) * 8 + (j >> 3) * 4 + (j & 3), None, 16), True, True)
-    act("B5", "W", c_("W"), T.B5[:], F_.Exp, scale=-LN2, bias=-LN2)
     for j in range(4):
         act("B5 pcs", "fb", c_("fb", j * 128, 128), c_("B5", j * 128, 128), F_.Identity, scale=2.0, bias=pc[11 + (j & 1)])
     act("B5", "sg", c_("sg"), T.B5[:], F_.Sign, bias=-15.5)
     ts2("J pcs", "ME", c_("ME"), c_("J", 0, 176), -48.0, pc[15], ADD, EQ)
     ts2("J pcs", "P2", T.P2[:], c_("J", 0, 144), -12.0, pc[14], ADD, EQ)
     ts1("J pcs", "P1", T.P1[:], c_("J", 0, 144), pc[13], EQ)
-    ts2("i3 pf4", "c4", c_("c4"), T.i3[:], pf[5], 128.0, EQ, MUL)
+    ts2("i3 pf3", "c4", c_("c4"), T.i3[:], pf[5], 128.0, EQ, MUL)
     ts2("i4 pf0", "TB0", c_("TB", 8, 8), T.i4[:], pf[0], 16.0, ADD, MUL)
     tt("P1", "E1", c_("E1", 0, 143), c_("P1", 0, 143), c_("P1", 1, 143), SUB)
     tt("P2", "E2", c_("E2", 0, 140), c_("P2", 0, 140), c_("P2", 4, 140), SUB)
     ts1("TB0", "TB", c_("TB", 0, 8), c_("TB", 8, 8), -0.5, ADD)
     tt("c4 GT", "Ta", T.Ta[:], c_("c4"), c_("GT"), MUL)
-    ts1("J pf0", "lm", T.lm[:], c_("J", 0, 4), pf[1], EQ)
-    ts2("J pcs", "Z", T.Z[:], T.J[:], -96.0, pc[17], ADD, EQ)
+    ts1("J pf3", "lm", c_("lm", 0, 2), c_("J", 0, 2), pf[3], EQ)
+    ts1("J pcs", "Z", T.Z[:], c_("J", 0, 32), pc[17], EQ)
     ts1("J pc23", "Cp", T.Cp[:], c_("J", 0, 144), pc[23], EQ)
-    ts1("J pc18", "Pm", T.Pm[:], c_("J", 0, 128), pc[18], EQ)
+    ts1("J pc18", "Pm", T.Pm[:], c_("J", 0, 64), pc[18], EQ)
     ts2("J pcs pc5", "Hm", T.Hm[:], c_("J", 0, 144), pc[16], pc[5], EQ, MUL)
-    scaled("Cp", "Cn", -1.0)
 
-    mms("B0", T.B0[:, 1:128:2], [("one", T.one[0:1, 0:128], T.one[0:1, 0:64])] +
+    mms("B0", T.B0[:, 1:192:3], [("one", T.one[0:1, 0:128], T.one[0:1, 0:64])] +
         [("MW pt", c_("MW", 16 - x, 128), c_("pt", x, None, 16)) for x in range(16)])
-    mm("one SG0", "B7", T.B7[:], T.one[0:1, 0:128], T.SG[0:1, 0::2, :], True, False)
-    ts2("B0", "B0 M", T.B0[:, 0:64:2], T.B0[:, 65:128:2], 131072.0, 65536.0, ADD, MUL)
+    mm("one SG0", "B7", T.B7[:], T.one[0:1, 0:128], T.SG[0:1, 0::3, :], True, False)
+    ts2("B0", "B0 M", T.B0[:, 0:96:3], T.B0[:, 97:192:3], 131072.0, 65536.0, ADD, MUL)
 
     def merge(j, b):
         nm = ("ht", "lt")[j >> 1]
@@ -322,55 +335,67 @@ def rank_program(g, core, T, topo):
             mm("ME " + nm, "B7", T.B7[:, (j >> 1) * 256 + (x >> 2):(j >> 1) * 256 + 256:4], c_("ME", 48 - 16 * (x & 3), 128), c_(nm, x, None, 16),
                False, j == 3 and x == 15)
 
+    def wipe(j, b):
+        if j == 2:
+            return scaled("Cp", "Cn", -1.0)
+        act("pay", "clr", c_("clr", 768 + j * 640, 640), c_("pay", 0, 640), F_.Identity, scale=0.0)
+
     def evac(h, b):
         act("B7", "mg", T.mg[:], T.B7[:])
 
     def table(h, b):
-        dmas("unw", "mg", "tab lk " + " ".join(AT), [("y", win[c * 32 + x:c * 32 + 32:16, 0:16384], c_("mg", x * 256, 256))
-                                                     for c in range(4) for x in range(2)])
+        dmas("unw", "mg", "tab lk tlown tlrem " + " ".join(AT), [("y", win[c * 32 + x:c * 32 + 32:16, 0:16384], c_("mg", x * 256, 256))
+                                                                 for c in range(4) for x in range(2)])
+        windows("lwin", "vl", others)
 
     def scale(h, b):
         if h == 0:
+            act("NW pc6", "Of", c_("Of", 16, 112), c_("NW", 0, 112), F_.Identity, scale=pc[6])
             return act("NW m3", "Rb", c_("Rb"), c_("NW"), F_.Identity, scale=m0)
         scaled("P2", "P2k", 4096.0)
         act("E2", "E2k", c_("E2k", 0, 140), c_("E2", 0, 140), F_.Identity, scale=4096.0)
-        scaled("nA", "nB", 4096.0)
-        scaled("Ta", "Tb", 4096.0)
+        for nm, c in (("Tb", 4096.0), ("nA", -1.0), ("nB", -4096.0)):
+            scaled("Ta", nm, c)
 
     def open_(h, b):
         mms(b[2], c_(b[2], 0, 256), [("I1 fb", T.I1[:], c_("fb", h * 256, 256)), ("I15 sg", c_("I15"), c_("sg", h * 256, 256))], stop=False)
 
-    def pick(h, b):
-        for j in range(8):
-            scan("SG0 SG1 M B0", b[1], c_(b[1], j * 64, 64), T.SG[:, :, (j >> 2) * 8 + h * 4 + (j & 3)], c_("B0", 0, 64), 0.0, MUL, MAX)
+    def pick(h, b, f):
+        for j in range(4):
+            scan("SG0 SG1 M B0", b[1 + 3 * f], c_(b[1 + 3 * f], j * 96, 96), T.SG[:, :, f * 8 + h * 4 + j], c_("B0", 0, 96), 0.0, MUL, MAX)
 
-    def shift(h, b):
-        tt("W " + b[1], b[4], c_(b[4], 0, 256), T[b[1]][:, 1::2], c_("W", h * 256, 256), MUL)
-
-    def round_(h, b):
+    def round_(h, b, f):
+        x, a = b[1 + 3 * f], h * 256 + f * 128
         if h == 0:
-            return ts2("B3", "rr0", c_("rr", 0, 256), c_("B3", 0, 256), EVEN, -EVEN, ADD, ADD)
-        act("B5", "rq", c_("rr", 512, 256), c_("B5", 0, 256), F_.Identity, bias=EVEN)
-        act("rq", "rr1", c_("rr", 256, 256), c_("rr", 512, 256), F_.Identity, bias=-EVEN)
+            return ts2(x, "rr0%d" % f, c_("rr", a, 128), c_(x, 2, 382, 3), EVEN, -EVEN, ADD, ADD)
+        act(x, "rq%d" % f, c_("rr", 512 + f * 128, 128), c_(x, 2, 382, 3), F_.Identity, bias=EVEN)
+        act("rq%d" % f, "rr1%d" % f, c_("rr", a, 128), c_("rr", 512 + f * 128, 128), F_.Identity, bias=-EVEN)
 
-    def test(h, b):
-        tt("rr%d %s" % (h, b[4]), b[1], c_(b[1], 0, 128), c_(b[4], 0, 128), c_("rr", h * 256, 128), LT_)
-        tt("rr%d %s" % (h, b[4]), "bt" + b[0], c_("bt", h * 128, 128), c_(b[4], 128, 128), c_("rr", h * 256 + 128, 128), LT_)
+    def test(h, b, f):
+        x = b[1 + 3 * f]
+        tt("rr%d%d %s" % (h, f, x), "bt" + b[0] if f else x, c_("bt", h * 128, 128) if f else c_(x, 384, 128), c_(x, 2, 382, 3),
+           c_("rr", h * 256 + f * 128, 128), LT_)
 
     def both(h, b):
-        tt(b[1] + " bt" + b[0], "pres" + b[0] * 2, c_("pres", 1 + h * 128, 128), c_(b[1], 0, 128), c_("bt", h * 128, 128), MUL)
-        r = " pres0 pres00 pres" + b[0] * 2
-        mm("RW" + r, b[1], c_(b[1], 128, 129), c_("RW"), c_("pres", h * 128, 129), True, False)
-        mm("LT" + r, b[1], c_(b[1], 128, 128), c_("LT"), c_("pres", h * 128 + 1, 128), False, True)
+        tt(b[1] + " bt" + b[0], "pres" + b[0] * 2, c_("pres", 1 + h * 136, 128), c_(b[1], 384, 128), c_("bt", h * 128, 128), MUL)
+        r = " pres0 pres" + b[0] * 2
+        act(r, "tot" + b[0], c_("junk", 1280 + h * 128, 128), c_("pres", h * 136 + 1, 128), accum_out=c_("tot", h, 1))
+        mm("RW" + r, b[1], c_(b[1], 128, 129), c_("RW"), c_("pres", h * 136, 129), True, False)
+        mm("LT" + r, b[1], c_(b[1], 128, 128), c_("LT"), c_("pres", h * 136 + 1, 128), False, True)
+
+    def flag(h, b):
         for f in range(2):
-            mm("I4k" + r, b[2], c_(b[2], f * 128, 128), c_("I4k"), c_("pres", h * 128 + 1, 128), False, False)
+            mm("I4k pres" + b[0] * 2, b[2], c_(b[2], f * 128, 128), c_("I4k"), c_("pres", h * 136 + 1, 128), False, False)
+
+    def total(h, b):
+        mm("Of Of0 tot" + b[0], b[1], c_(b[1], 260, 1), T.Of[:], c_("tot", h, 1), True, True)
 
     def route(h, b, nm, r, a):
         for f in range(2):
             mm("%s %s%d" % (nm, r, h), b[2], c_(b[2], f * 128, 128), c_(nm), c_(r, a, 128), False, r == "r4" and f == 1)
 
     def number(h, b):
-        scan("one s10 " + b[1], "s1" + b[0], c_("s1", h * 136, 129), c_("one", 0, 129), c_(b[1], 128, 129), c_("s1", 127, 1) if h else 0.0, MUL, ADD)
+        scan("one " + b[1], "s1" + b[0], c_("s1", h * 136, 129), c_("one", 0, 129), c_(b[1], 128, 129), c_(b[1], 260, 1), MUL, ADD)
         route(h, b, "I512", "s1", h * 136)
 
     def floor(h, b):
@@ -379,20 +404,20 @@ def rank_program(g, core, T, topo):
             route(h, b, nm, r, h * 128)
 
     def rows(h, b):
-        mm("Rb s1" + b[0], "B0", c_("B0", 128 + h * 129, 129 - h), c_("Rb"), c_("s1", h * 137, 129 - h), True, True)
+        mm("Rb s1" + b[0], "B0", c_("B0", 128 + h * 136, 129), c_("Rb"), c_("s1", h * 136, 129), True, True)
 
     def held(h, b):
-        act("B0 pcs", "Gb" + b[0], c_("Gb", h * 129, 129 - h), c_("B0", 128 + h * 129, 129 - h), F_.Identity, scale=1.0 / 16, bias=pc[19])
+        act("B0 pcs", "Gb" + b[0], c_("Gb", h * 144, 129), c_("B0", 128 + h * 136, 129), F_.Identity, scale=1.0 / 16, bias=pc[19])
 
     def kept(h, b):
-        mms(b[3], c_(b[3], 256, 128), [("I1 Gb0 Gb" + b[0], T.I1[:], c_("Gb", h * 128 + 1, 128)), ("In", T.In[:], c_("Gb", h * 128, 128))])
+        mms(b[2], c_(b[2], 256, 128), [("I1 Gb" + b[0], T.I1[:], c_("Gb", h * 144 + 1, 128)), ("In", T.In[:], c_("Gb", h * 144, 128))])
 
     def keep(h, b):
-        act(b[3], "keep" + b[0], c_("keep", h * 128, 128), c_(b[3], 256, 128), F_.Identity, scale=-1.0, bias=1.0)
+        act(b[2], "keep" + b[0], c_("keep", h * 128, 128), c_(b[2], 256, 128), F_.Identity, scale=-1.0, bias=1.0)
 
     def count_(h, b, js=(2, 3, 4)):
         for j in js:
-            act("B0 TB", "acc" + b[0], c_("junk", j * 256 + h * 128, 128), c_("B0", 129 + h * 128, 128), F_.Sign, scale=-1.0, bias=c_("TB", j, 1),
+            act("B0 TB", "acc" + b[0], c_("junk", j * 256 + h * 128, 128), c_("B0", 129 + h * 136, 128), F_.Sign, scale=-1.0, bias=c_("TB", j, 1),
                 accum_out=c_("acc", h * 8 + j, 1))
 
     def stage1(h, b, j):
@@ -419,8 +444,7 @@ def rank_program(g, core, T, topo):
 
     def again(h, b):
         mms(b[3], c_(b[3], 0, 128), [("one iE", T.one[0:1, 0:128], T.iE[0:1, :])] +
-            [("one " + nm, T[nm][0:1, :], T.one[0:1, 0:128]) for nm in ("nA", "nB")] +
-            [("keep%d %s" % (h, nm), T[nm][:], c_("keep", h * 128, 128)) for nm in ("Ta", "Tb")], stop=False)
+            [("Gb%d %s" % (h, nm), T[nm][:], c_("Gb", h * 144 + x, 128)) for x, nm in ((0, "Ta"), (0, "Tb"), (1, "nA"), (1, "nB"))], stop=False)
 
     def anew(h, b):
         for f in range(2):
@@ -435,100 +459,137 @@ def rank_program(g, core, T, topo):
                    False, j + f == 4)
 
     def carry(h, b):
-        scan("keep%d GW0 %s" % (h, b[3]), "GW" + b[0], c_("GW", 1 + h * 128, 128), c_("keep", h * 128, 128), c_(b[3], 0, 128),
-             c_("GW", 128, 1) if h else 0.0, MUL, MAX)
+        scan("keep%d %s" % (h, b[3]), "GW" + b[0], c_("GW", 1 + h * 136, 128), c_("keep", h * 128, 128), c_(b[3], 0, 128), 0.0, MUL, MAX)
 
     def lists(h, b):
-        tt("acc0 acc1", "acc", c_("acc", 16, 5), c_("acc", 0, 5), c_("acc", 8, 5), ADD)
-        act("Gb1", "Gb2", c_("Gb", 257, 1), c_("Gb", 256, 1), F_.Identity, bias=1.0)
-        for j in (1, 0):
-            ts2("acc", "gl%d" % j, c_("gl", 6 * j, 5), c_("acc", 16, 5), 0.5, 128.0 + j, MUL, ADD)
+        for j in range(2):
+            ts2("acc" + b[0], "gl%d%d" % (h, j), c_("gl", 12 * h + 5 * j, 5), c_("acc", 8 * h, 5), 0.5, 65.0 - j, MUL, ADD)
+
+    def outside(h, b):
+        act("Gb" + b[0], "Ge" + b[0], c_("Gb", h * 144 + 129, 1), c_("Gb", h * 144 + 128, 1), F_.Identity, bias=1.0)
+        act("rA Gb" + b[0], "out" + b[0], c_("out", h * 80, 80), c_("rA", 80, 80), F_.Relu, bias=c_("Gb", h * 144, 1))
 
     def over(h, b):
-        act("Gb0 Gb1 Gb2 gl1", "Fg", T.Fg[:], T.Gb[:].indirect(c_("gl", 6, 5)))
-        for j, nm in enumerate(("I1", "In")):
-            mms("B6", c_("B6", j * 80, 80), [("one rA", T.one[0:1, 0:128], T.rA[0:1, j * 80:j * 80 + 80]), (nm + " Fg", T[nm][:], T.Fg[:])])
-        act("B6", "om", T.om[:], c_("B6", 0, 160), F_.Relu)
-    for st in MIDDLE.split():
-        h = int(st[-1])
-        {"pick": pick, "shift": shift, "round": round_, "test": test, "both": both, "number": number, "floor": floor, "rows": rows, "kept": kept,
-         "count": count_, "step": step, "steps": steps, "signs": signs, "excess": excess, "again": again, "spread": spread_, "carry": carry,
-         "lists": lists, "over": over, "junk": junk, "keep": keep, "held": held, "anew": anew, "scale": scale, "merge": merge, "evac": evac,
-         "table": table, "open": open_, "tally": lambda h, b: count_(h, b, (0, 1))
-         }[st[:-1]](h, (str(h), "B%d" % (1 + h), "B%d" % (4 + 2 * h), "B%d" % (5 - h), "B%d" % (3 + 2 * h)))
-    g1 = [c_("g1", j * 80, 80) for j in range(3)]
-    for j in range(2):
-        tt("GW0 GW1 GWp gl%d om" % j, "g%d" % j, g1[j], T.GW[:].indirect(c_("gl", 6 * j, 5)), c_("om", j * 80, 80), MUL)
-    tt("g0 g1", "g2", g1[2], g1[0], g1[1], ADD)
-    for j, d in enumerate(order):
-        ts1("g2 lm", "zp", T.zp[:, :, j * 20:j * 20 + 20], g1[2], c_("lm", d, 1), MUL)
-    mms("B0", c_("B0", 0, 80), [("Z zp", c_("Z", 96 - 32 * c, 128), T.zp[:, c, :]) for c in range(4)])
-    u2 = [c_("u2", j * 80, 80) for j in range(7)]
-    u3 = [c_("u3", j * 80, 80) for j in range(2)]
-    ts2("g2", "e0", u2[4], g1[2], 1.0 / 32, -0.484375, MUL, ADD)
-    ts1("g2", "c2", u3[1], g1[2], 0.0, EQ)
-    ts1("e0", "a3", u2[5], u2[4], 127, AND)
-    ts1("e0", "a4", u2[6], u2[4], 12, SHR)
-    ts1("a3", "c3", c_("ub", 0, 80), u2[5], 4.0, MUL)
-    tt("a4 c2", "c4b", c_("ub", 80, 80), u2[6], u3[1], SUB)
-    for d in range(4):
-        for h in range(2):
-            mms("B2", c_("B2", d * 40 + 32 + 4 * h, 4), [("Cp s10 s11", c_("Cp", 2 * d, 128), c_("s1", h * 136 + 32, 97, 32)),
-                                                        ("Cn", c_("Cn", 2 * d, 128), c_("s1", h * 136, 97, 32))])
-    for d in range(4):
-        mms("B2", c_("B2", d * 40, 32), [("Pm c3 c4b ub0", c_("ub", h * 80, 128), c_("Pm", d * 32, 32)) for h in range(2)])
+        act("Gb%d Ge%d gl%d0" % (h, h, h), "Fg" + b[0], c_("Fg", h * 80, 80), c_("Gb", h * 144, 144).indirect(c_("gl", 12 * h, 5)))
+
+    def beyond(h, b):
+        mm("one rA", "B3", c_("B3", 256, 160), T.one[0:1, 0:128], T.rA[0:1, :], True, False)
+        for j, (nm, r) in enumerate((("I480", "out"), ("I480", "out"), ("In", "Fg"), ("I1", "Fg"))):
+            mm("%s %s%d" % (nm, r, h), "B3", c_("B3", 256 + (j & 1) * 80, 80), T[nm][:], c_(r, h * 80, 80), False, j == 3)
+
+    def under(h, b):
+        act("B3", "om" + b[0], c_("om", h * 160, 160), c_("B3", 256, 160), F_.Relu, bias=-1.0)
+
+    def close(h, b):
+        tt("GW%d GWp gl%d0 gl%d1 om%d" % (h, h, h, h), "g%d0 g%d1" % (h, h), c_("g1", h * 240, 160),
+           c_("GW", h * 136, 136).indirect(c_("gl", 12 * h, 10)), c_("om", h * 160, 160), MUL)
+
+    def join(h, b):
+        tt("g%d0 g%d1" % (h, h), "g%d2" % h, c_("g1", h * 240 + 160, 80), c_("g1", h * 240, 80), c_("g1", h * 240 + 80, 80), ADD)
+
+    def move(h, b):
+        for j in range(2):
+            ts1("lm g%d2" % h, "zp" + b[0], T.zp[:, 4 * h:4 * h + 4, j * 20:j * 20 + 20], c_("g1", h * 240 + 160, 80),
+                c_("lm", order[2 * h + j] & 1, 1), MUL)
+        for c in range(4):
+            mm("Z zp" + b[0], "B7", T.B7[32 * c:32 * c + 32, h * 64:h * 64 + 40], T.Z[:], T.zp[:, 4 * h + c, :], True, True)
+
+    def name(h, b, x):
+        u, g2, r = [c_("u2", h * 240 + j * 80, 80) for j in range(3)], c_("g1", h * 240 + 160, 80), "g%d2" % h
+        if x == 0:
+            ts2(r, "e0" + b[0], u[0], g2, 1.0 / 32, -0.484375, MUL, ADD)
+            ts1(r, "c2" + b[0], c_("u3", h * 80, 80), g2, 0.0, EQ)
+        elif x == 1:
+            ts1("e0" + b[0], "a3" + b[0], u[1], u[0], 127, AND)
+            ts1("e0" + b[0], "a4" + b[0], u[2], u[0], 12, SHR)
+        else:
+            ts1("a3" + b[0], "ub" + b[0] * 2, c_("ub", h * 208, 80), u[1], 4.0, MUL)
+            tt("a4%d c2%d" % (h, h), "ub" + b[0] * 2, c_("ub", h * 208 + 80, 80), u[2], c_("u3", h * 80, 80), SUB)
+
+    def turn(h, b):
+        for d in order[2 * h:2 * h + 2]:
+            for x in range(2):
+                a = 4 * (d & 1) + 2 * x
+                mms("B0", c_("B0", d * 40 + 32 + 4 * x, 4), [("Cp s1" + b[0], c_("Cp", a, 128), c_("s1", h * 136 + 32, 97, 32)),
+                                                           ("Cn", c_("Cn", a, 128), c_("s1", h * 136, 97, 32))])
+            mms("B0", c_("B0", d * 40, 32), [("one", T.one[0:1, 0:128], T.one[0:1, 0:32])] +
+                [("Pm ub0 ub" + b[0] * 2, c_("ub", h * 208 + x * 80, 128), c_("Pm", (d & 1) * 32, 32)) for x in range(2)])
+
+    def seconds(h, b):
+        ts2("B7", "ll0" + b[0], c_("ll", h * 40, 40), c_("B7", h * 64, 40), 1.0 / 32, -0.484375, MUL, ADD)
+
+    def firsts(h, b, x):
+        u, word = [c_("u2", 480 + h * 160 + j * 40, 40) for j in range(4)], c_("B7", h * 64, 40)
+        if x == 0:
+            ts2("B7", "a0" + b[0], u[0], word, 1.0 / 32, -0.484375, MUL, ADD)
+            ts1("B7", "u1" + b[0], u[1], word, 128.0, MUL)
+        elif x == 1:
+            ts1("a0" + b[0], "a2" + b[0], u[2], u[0], 0x307F, AND)
+            ts1("u1" + b[0], "a1" + b[0], u[3], u[1], 0xF80, AND)
+        elif x == 2:
+            tt("a1%d a2%d" % (h, h), "c1" + b[0], c_("u3", 160 + h * 40, 40), u[2], u[3], ADD)
+        else:
+            cp("c1" + b[0], "ll1" + b[0], c_("ll", 80 + h * 40, 40), c_("u3", 160 + h * 40, 40))
     lw = c_("win", 0, 16384)
-    word = c_("B0", 0, 80)
-    banks = {}
 
     def look(f, j, h):
-        f("ll%d lk" % h, "LK%d%d" % (j, h), c_("LK", j * 640 + h * 320, 320), lw.indirect(c_("ll", h * 80 + j * 20, 20)))
+        f("ll%d%d lk" % (h, j >> 1), "LK%d%d" % (j, h), c_("LK", j * 640 + h * 320, 320), lw.indirect(c_("ll", h * 80 + j * 20, 20)))
 
     def wrap(j, hs):
-        b = banks[j, hs[0]] = "B%d" % (3 + len(banks) % 5)
-        a, n = j * 640 + hs[0] * 320, 320 * len(hs)
-        mms(b, c_(b, 0, n // 16), [("Hm " + " ".join("LK%d%d" % (j, h) for h in hs), c_("Hm", 15 - x, 128), c_("LK", a + x, n - x, 16))
-                                   for x in range(16)])
+        b, a, n = ("B1", "B5", "B6", "B4")[j], j * 640 + hs[0] * 320, 320 * len(hs)
+        mms(b, c_(b, hs[0] * 20, n // 16), [("Hm " + " ".join("LK%d%d" % (j, h) for h in hs), c_("Hm", 15 - x, 128), c_("LK", a + x, n - x, 16))
+                                            for x in range(16)])
 
     def lst(j, hs):
-        b = banks[j, hs[0]]
-        ts1(b, " ".join("lo%d%d" % (j, h) for h in hs), c_("lo", j * 40 + hs[0] * 20, 20 * len(hs)), c_(b, 0, 20 * len(hs)), -64.0, ADD)
+        b = ("B1", "B5", "B6", "B4")[j]
+        ts1(b, " ".join("lo%d%d" % (j, h) for h in hs), c_("lo", j * 40 + hs[0] * 20, 20 * len(hs)), c_(b, hs[0] * 20, 20 * len(hs)), -64.0, ADD)
 
-    def second(j):
+    def second(j, b):
         act("lo%d0 lown lwin" % j, "t2%d" % j, c_("t2", j * 320, 320), T.vw[:].indirect(c_("lo", j * 40, 20)))
 
-    def first(j):
+    def first(j, b):
         d = order[j]
         tt("lo%d1 lown lwin t2%d" % (j, j), "Y%d" % d, c_("Y", j * 320, 320), T.vw[:].indirect(c_("lo", j * 40 + 20, 20)),
            c_("t2", j * 320, 320), SUB)
         if d != k:
             send("sy%d" % d, "ay%d" % k, "Y%d" % d, [(d, c_("Y", j * 320, 320), c_("YL", k * 320, 320), 0, 16)])
 
-    def entities():
-        act("B2", "wS", T.wS[:], c_("B2", 0, 160))
-        send("swho", "awho", "wS", [(d, c_("wS", d * 40, 40), c_("wL", k * 40, 40), 4 * j, 4 * j + 4) for j, d in enumerate(far_first)])
+    def entities(h, b):
+        act("B0", "wS", T.wS[:], c_("B0", 0, 160))
+        send("swho", "awho", "wS", [(d, c_("wS", d * 40, 40), c_("wL", k * 40, 40), 4 * j, 4 * j + 4) for j, d in enumerate(others)])
         arrives("awho", 12, "wL")
-        for s, nm, ks in (("who1", "wS", [k]), ("who2", "wL", others)):
-            dmas(s, nm, "", [it for kk in ks for c0 in [kk * 40]
-                             for it in (("y", T.who[2 * kk:2 * kk + 1, :], T[nm][0:80, c0:c0 + 16]),
-                                        ("y", T.who[2 * kk + 1:2 * kk + 2, :], T[nm][0:80, c0 + 16:c0 + 32]),
-                                        ("y", T.cnt[2 * kk:2 * kk + 2, :], T[nm][0:2, c0 + 32:c0 + 40]))])
-    ts2("B0", "ll0", c_("ll", 0, 80), word, 1.0 / 32, -0.484375, MUL, ADD)
-    ts2("B0", "a0", u2[0], word, 1.0 / 32, -0.484375, MUL, ADD)
-    ts1("B0", "u1", u2[1], word, 128.0, MUL)
-    ts1("a0", "a2", u2[2], u2[0], 0x307F, AND)
-    ts1("u1", "a1", u2[3], u2[1], 0xF80, AND)
-    tt("a1 a2", "c1", u3[0], u2[2], u2[3], ADD)
-    cp("c1", "ll1", c_("ll", 80, 80), u3[0])
-    for st in TAIL.split():
-        j, hs = int(st[1:2] or 0), [int(x) for x in st[2:]]
-        {"S": lambda: look(act, j, hs[0]), "V": lambda: look(cp, j, hs[0]), "w": lambda: wrap(j, hs), "l": lambda: lst(j, hs),
-         "s": lambda: second(j), "f": lambda: first(j), "W": entities}[st[0]]()
-    for r in others:
-        arrives("ay%d" % r, 16, "YL%d" % r)
-    for r in far_first[:2] + [k] + far_first[2:]:
+
+    def told(h, b):
+        nm = ("wS", "wL")[h]
+        dmas("who%d" % (h + 1), nm, "", [it for kk in ([k], others)[h] for c0 in [kk * 40]
+                                         for it in (("y", T.who[2 * kk:2 * kk + 1, :], T[nm][0:80, c0:c0 + 16]),
+                                                    ("y", T.who[2 * kk + 1:2 * kk + 2, :], T[nm][0:80, c0 + 16:c0 + 32]),
+                                                    ("y", T.cnt[2 * kk:2 * kk + 2, :], T[nm][0:2, c0 + 32:c0 + 40]))])
+
+    def store(j, b):
+        r = order[j]
         nm, c0 = ("Y", 960) if r == k else ("YL", r * 320)
+        if r != k:
+            arrives("ay%d" % r, 16, "YL%d" % r)
         dmas("st%d" % r, nm + str(r), "", [("ys"[c & 1], T.y[32 * r:32 * r + 32, c * 320:c * 320 + 320],
                                             T[nm][c * 32:c * 32 + 32, c0:c0 + 320]) for c in range(4)])
+    named = {"both": both, "number": number, "floor": floor, "rows": rows, "kept": kept, "count": count_, "step": step, "steps": steps,
+             "signs": signs, "excess": excess, "again": again, "spread": spread_, "carry": carry, "lists": lists, "over": over, "junk": junk,
+             "keep": keep, "held": held, "anew": anew, "scale": scale, "merge": merge, "evac": evac, "table": table, "wipe": wipe, "open": open_,
+             "tally": lambda h, b: count_(h, b, (0, 1)), "total": total, "outside": outside, "close": close, "move": move, "turn": turn,
+             "seconds": seconds, "second": second, "flag": flag, "beyond": beyond, "under": under, "told": told, "join": join, "first": first,
+             "entities": entities, "store": store}
+    for nm, f in (("pick", pick), ("round", round_), ("test", test), ("name", name), ("first", firsts)):
+        for x, c in enumerate("abcd"):
+            named[nm + c] = lambda h, b, f=f, x=x: f(h, b, x)
+    for nm, f in (("wrap", wrap), ("list", lst)):
+        for c, hs in (("", [0, 1]), ("a", [1]), ("b", [0])):
+            named[nm + c] = lambda j, b, f=f, hs=hs: f(j, hs)
+    for nm, f in (("S", act), ("V", cp)):
+        for c, x in (("a", 1), ("b", 0)):
+            named[nm + c] = lambda j, b, f=f, x=x: look(f, j, x)
+    for st in STEPS.split():
+        h = int(st[-1])
+        named[st[:-1]](h, (str(h), "B%d" % (1 + h), "B%d" % (4 + 2 * h), "B%d" % (5 - h), "B%d" % (3 + 2 * h)))
     for s in count:
         wait("g", s, count[s])

import math
from concourse.bass import DstId, RemoteDMATransfer
from concourse.mybir import AluOpType, ActivationFunctionType

A_ = AluOpType
F_ = ActivationFunctionType
SH = 15360
SPENT = ("pay:2048 vs:1536 pt:1024 ht:1024 lt:1024 clr:2048 sg:512 FW:512 FG:512 Fe:512 fb:512 FS:528 MW:144 "
         "ME:176 c4:128 GT:128 NW:128 LT:128 RW:128 I4k:128 I512:128 I32:128 I15:128 N1:128 one8:64 zt:128 Rb:128 ph:256 tt:256 tl:256")
AT = {}
for _e in SPENT.split():
    AT[_e.split(":")[0]] = (sum(n for _, n in AT.values()), int(_e.split(":")[1]))
AT["rest"] = (sum(n for _, n in AT.values()), SH - sum(n for _, n in AT.values()))
LN2 = math.log(2.0)
Z0 = 480.0 * 6144 + 32.0 * 24576 - 4096 - 15.5
EVEN = 1.5 * 2 ** 24
STEPS = ("pickb0 open0 picka1 picka0 scale1 merge2 roundb0 scale0 pickb1 open1 wipe0 rounda0 rounda1 merge1 merge0 merge3 testb0 roundb1 testa0 "
         "both0 total0 testb1 testa1 flag0 evac0 both1 number0 wipe1 total1 floor0 rows0 flag1 number1 signs0 rows1 floor1 held0 junk0 again0 "
         "count0 step0 kept0 step1 steps0 tally0 table0 excess0 held1 signs1 steps1 junk1 anew0 kept1 tally1 count1 lists0 spread0 outside0 "
         "keep0 over0 excess1 beyond0 keep1 lists1 outside1 again1 anew1 under0 carry0 spread1 over1 close0 beyond1 join0 carry1 move0 under1 "
         "namea0 close1 nameb0 wipe2 join1 seconds0 firsta0 move1 firstb0 namec0 namea1 firstc0 Sb0 Sb1 firsta1 firstd0 turn0 Sa1 nameb1 "
         "firstb1 namec1 Sa0 firstc1 wrapb0 seconds1 turn1 firstd1 Vb2 Va2 wrap1 Sa3 wrapa0 wrap2 entities0 list1 Vb3 told0 listb0 lista0 "
         "second1 list2 second0 first1 wrap3 second2 list3 second3 told1 first0 store1 first2 first3 store3 store0 store2")

SCRATCH = {"vl": ("dram", [4, 128, 512], "bfloat16"), "zp": ("sbuf", [128, 8, 40], "float32"), "fi": ("sbuf", [128, 8, 16], "int32"),
           "f12": ("sbuf", [128, 32, 2, 4], "int32"), "SG": ("sbuf", [128, 96, 16], "bfloat16")}
for _d, _l in (
        ("bfloat16", "win:31744 vw:8192 one:256 I1:128 In:128 I480:128 pw:16 Hm:144 P1:144 E1:144 P2:144 E2:144 P2k:144 E2k:144 Ta:128 Tb:128 "
                     "nA:128 nB:128 Cp:144 Cn:144 mg:512 pres:272 Gs:768 Gb:288 out:160 Fg:160 keep:256 iE:128 rA:160 junk:1536 LK:2560 "
                     "t2:1280 Y:1280 YL:1280 ub:416 Pm:64"),
        ("int32", "ei:128 ai:128 ct:32 pi:8 pb:16 u2:800"),
        ("float32", "cf:32 cT:32 k5:32 pf:16 pc:32 J:176 iA:128 iB:128 iX:16 iC:144 i3:128 wS:160 i4:8 m3:4 lm:4 q1:128 q2:128 Q:128 "
                    "bb:16 Z:32 TB:16 rr:768 bt:256 Jb:256 GW:272 Of:128 tot:2 acc:24 om:320 g1:480 u3:240 wL:160"),
        ("float16", "s1:272 r4:256 r16:256 U:2048 V:2048"),
        ("uint16", "ks:32 ka:96 ke:96 kl:96 ls:32 lr:32 gl:24 ll:160 lo:160")):
    for _e in _l.split():
        SCRATCH[_e.split(":")[0]] = ("sbuf", [128, int(_e.split(":")[1])], _d)
for _j in range(8):
    SCRATCH["B%d" % _j] = ("psum", [128, 512], "float32")
SEMAPHORES = ("pv ps pe pg lkey lkown lcls lform zero lval lown wrp wrh unw lwin alist akey aform aval awho ay0 ay1 ay2 ay3 "
              "slist skey sform sval swho sy0 sy1 sy2 sy3 who1 who2 st0 st1 st2 st3").split()


def rank_program(g, core, T, topo):
    k = T.rank_of(core)
    if k is None:
        return
    cores = T.cores
    others = [(k + 1) % 4, (k + 2) % 4, (k + 3) % 4]
    order = sorted(range(4), key=lambda d: (d >> 1 == k >> 1, d == k))
    Q = {"v": g.vector, "s": g.scalar, "t": g.tensor, "g": g, "y": g.sync}
    count, wrote, read = {}, {}, {}
    seen = {q: {} for q in Q}

    def wait(q, s, n):
        if seen[q].get(s, 0) < n:
            Q[q].wait_ge(T.sem[s], n)
            seen[q][s] = n

    def deps(q, r, w, own):
        toks = []
        for key in r:
            toks += wrote.get(key, [])
            if key[0] == "B":
                toks += [t for t in read.get(key, []) if t[0] != own]
        for key in w:
            toks += [t for t in wrote.get(key, []) + read.get(key, []) if t[0] != own]
        for s in sorted(set(t[0] for t in toks)):
            wait(q, s, max(t[1] for t in toks if t[0] == s))

    def note(s, r, w):
        for key in r:
            read.setdefault(key, []).append((s, count[s]))
        for key in w:
            wrote.setdefault(key, []).append((s, count[s]))

    def op(q, r, w, f, *a, **kw):
        s = {"v": "pv", "s": "ps", "t": "pe", "g": "pg"}[q]
        deps(q, r.split(), w.split(), s)
        count[s] = count.get(s, 0) + 1
        f(*a, **kw).then_inc(T.sem[s], 1)
        note(s, r.split(), w.split())

    def dmas(s, r, w, items):
        for q in sorted(set(it[0] for it in items)):
            deps(q, r.split(), w.split(), None)
        for q, o, i in items:
            Q[q].dma_start(o, i).then_inc(T.sem[s], 16)
        count[s] = 16 * len(items)
        note(s, r.split(), w.split())

    def send(s, rsem, r, items):
        deps("g", r.split(), [], None)
        trs = []
        for d, src, dst, lo, hi in items:
            rid, pid, _ = topo.addr(cores[d])
            m = sum(1 << e for e in topo.engines(core, cores[d])[lo:hi])
            sides = dict(srcs=src, dsts=[dst], alu_op=1) if isinstance(src, list) else dict(src=src, dst=dst)
            trs.append(RemoteDMATransfer(dst_ids=[DstId(rid=rid, pnc=pid)], dma_engine_mask=m, remote_sem=T.sem[rsem], **sides))
            count[s] = count.get(s, 0) + hi - lo
        g.remote_dma_fused(trs, local_sem=T.sem[s])
        note(s, r.split(), [])

    def arrives(s, n, w):
        count[s] = n
        note(s, [], [w])

    V, S = g.vector, g.scalar

    def ts1(r, w, o, i, s, o0):
        op("v", r, w, V.tensor_scalar, o, i, s, None, o0)

    def ts2(r, w, *a):
        op("v", r, w, V.tensor_scalar, *a)

    def tt(r, w, *a):
        op("v", r, w, V.tensor_tensor, *a)

    def cp(r, w, *a):
        op("v", r, w, V.tensor_copy, *a)

    def tr(r, w, *a):
        op("v", r, w, V.transpose, *a)

    def scan(r, w, *a):
        op("v", r, w, V.tensor_tensor_scan, *a)

    def fill(w, o, c=0.0):
        op("v", "", w, V.memset, o, c)

    def act(r, w, o, i, f=F_.Copy, **kw):
        op("s", r, w, S.activation, o, i, f, **kw)

    def scaled(r, w, c):
        act(r, w, c_(w), c_(r), F_.Identity, scale=c)

    def mm(r, w, *a):
        op("t", r, w, g.tensor.matmul, *a)

    def mms(w, o, terms, start=True, stop=True):
        for j, (r, a, b) in enumerate(terms):
            mm(r, w, o, a, b, start and j == 0, stop and j == len(terms) - 1)

    def iota(w, o, pat, base=0):
        op("g", "", w, g.iota, o, pat, base, 0, allow_small_or_imprecise_dtypes=True)

    def sel(r, w, *a):
        op("g", r, w, g.affine_select, *a)

    def c_(name, a=0, n=None, step=1):
        a0, width = AT[name] if name in AT else (0, SCRATCH[name][1][1])
        return T["win" if name in AT else name][:, a0 + a:a0 + (width if n is None else a + n):step]

    win = T.win
    AND, SHR, MUL, ADD, SUB, EQ, MAX, LT_, GE = (A_.bitwise_and, A_.logical_shift_right, A_.mult, A_.add, A_.subtract, A_.is_equal,
                                                 A_.max, A_.is_lt, A_.is_ge)
    E3 = ((0, 4), (4, 8), (8, 16))
    for s, w, ks in (("lkey", "ei ai", others), ("lkown", "eo ao", [k])):
        dmas(s, "", w, [it for kk in ks for j in [(kk - k - 1) % 4] for it in (("y", c_("ei", j * 32, 32), T.ent[2 * kk:2 * kk + 2, :]),
                                                                              ("s", c_("ai", j * 32, 32), T.att[2 * kk:2 * kk + 2, :]))])
    dmas("lform", "", "fi", [("ys"[kk & 1], T.fi[:, 2 * kk:2 * kk + 2, :], T.form[2 * kk:2 * kk + 2, :]) for kk in range(4)])
    dmas("lcls", "", "ct", [("ys"[j & 1], T.ct[(j >> 1) * 32 + (j & 1):(j >> 1) * 32 + 32:2, :], T.cls[(j >> 2)::2, :]) for j in range(8)])

    p0 = c_("pi", 0, 1)
    op("g", "", "pi", g.iota, p0, [[0, 1]], 0, 1)
    iota("iB", T.iB[:], [[0, 4], [1, 32]], 32)
    iota("iA", T.iA[:], [[2048, 4], [0, 32]], 32)
    iota("iX", T.iX[:], [[32, 16]])
    iota("one8", c_("one8"), [[0, 4], [-1, 2], [0, 8]], 1)
    iota("FS", c_("FS", 0, 16), [[0, 16]])

    def formula_matrices(js):
        for j in js:
            sel("one8", "FS", c_("FS", 16 + j * 64, 64), c_("one8"), [[-16, 2], [0, 2], [-1, 16]], EQ, 0.0,
                -64 * (j & 1) - 32 * (j >> 2) - 8 * ((j >> 1) & 1), 1)
    formula_matrices(range(4))
    fill("wz0", c_("win", SH, 1024))
    dmas("zero", "wz0", "wrow", [("y", win[x::16, 16384:16384 + SH], c_("win", SH, SH // 16)) for x in range(3)])
    pb = [c_("pb", j, 1) for j in range(10)]
    pf = [c_("pf", j, 1) for j in range(10)]
    pc = [c_("pc", j, 1) for j in range(24)]

    def bits(a, fields):
        for j, (sh, m) in enumerate(fields):
            ts2("pi", "pb%d" % a, pb[a + j], p0, sh, m, SHR, AND)
        cp("pb%d" % a, "pf%d" % a, c_("pf", a, len(fields)), c_("pb", a, len(fields)))
    fill("one", T.one[:], 1.0)
    bits(0, ((0, 15), (4, 3), (0, 1)))
    ts2("iB pf0", "m3", c_("m3", 0, 3), c_("iB", 0, 3), -32.0, pf[0], ADD, EQ)
    ts1("pf0", "pc0", pc[0], pf[1], 512.0, MUL)
    ts2("pf0", "pc1", pc[1], pf[2], 256.0, 64.0 * k, MUL, ADD)
    m0, m1, m2 = c_("m3", 0, 1), c_("m3", 1, 1), c_("m3", 2, 1)
    ts1("m3", "pc2", pc[2], m2, 32.0, MUL)
    ts2("iA m3 pc0", "q1", T.q1[:], T.iA[:], pc[0], m0, ADD, MUL)
    ts2("iB m3 pc2", "q2", T.q2[:], T.iB[:], m1, pc[2], MUL, ADD)
    act("iX m3", "bb", T.bb[:], T.iX[:], F_.Identity, scale=m0)
    tt("q1 q2", "Q", T.Q[:], T.q1[:], T.q2[:], ADD)
    bits(3, ((5, 1), (0, 64), (0, 3), (2, 3)))
    for x in range(16):
        act("Q bb", "pay", c_("pay", x, None, 16), T.Q[:], F_.Identity, bias=c_("bb", x, 1))

    ts1("ai", "ka", T.ka[:], c_("ai", 0, 96), 512.0, MUL)
    cp("ei", "ke", T.ke[:], c_("ei", 0, 96))
    send("skey", "akey", "ka ke", [(d, [c_("ka", j * 32, 32), c_("ke", j * 32, 32)], c_("kl", j * 32, 32), 4 * j, 4 * j + 4)
                                   for j, d in enumerate(others)])
    arrives("akey", 12, "kl")
    for f, (n, o) in enumerate(((31, AND), (5, SHR))):
        for kk in (0, 2):
            for h in range(2):
                ts1("fi", "f12", T.f12[:, f * 16 + kk * 4:f * 16 + kk * 4 + 8, h, :], T.fi[:, 2 * kk + (h ^ 1 ^ kk >> 1):2 * kk + 4:2, :], n, o)
    ts1("ct pc1", "cf", T.cf[:], T.ct[:], pc[1], ADD)
    ts1("ao", "B7", c_("B7", 0, 32), c_("ai", 96, 32), 512.0, MUL)
    cp("f12", "ph", c_("ph"), T.f12[:])
    tr("ph", "tt", c_("tt"), c_("ph"))
    send("sform", "aform", "tt", [(d, c_("tt", f * 128 + d * 32, 32), c_("tl", f * 128 + k * 32, 32), 4 * j + 2 * f, 4 * j + 2 * f + 2)
                                  for j, d in enumerate(others) for f in range(2)])
    arrives("aform", 12, "tlrem")
    tt("B7 eo", "k5", T.k5[:], c_("B7", 0, 32), c_("ei", 96, 32), ADD)
    tr("cf", "cT", T.cT[:], T.cf[:])
    cp("k5", "ks", T.ks[:], T.k5[:])
    cp("cT", "ls", T.ls[:], T.cT[:])
    cp("cT", "lrown", c_("lr", k * 8, 8), c_("cT", k * 8, 8))
    send("slist", "alist", "ls", [(d, c_("ls", d * 8, 8), c_("lr", k * 8, 8)) + E3[j] for j, d in enumerate(others)])
    arrives("alist", 16, "lr")
    formula_matrices(range(4, 8))
    act("pf0", "pw", c_("pw", 0, 1), pf[0], F_.Exp, scale=LN2, bias=-4 * LN2)
    act("pw", "pc9", pc[9], c_("pw", 0, 1))
    for f in range(2):
        act("tt", "tlown", c_("tl", f * 128 + k * 32, 32), c_("tt", f * 128 + k * 32, 32))
    act("pf0 pf3", "pf7", pf[7], pf[1], F_.Identity, scale=16.0, bias=pf[4])
    act("pf0 pf3", "pf9", pf[9], pf[3], F_.Identity, scale=-2.0, bias=pf[1])
    act("pf3 pf7", "pf8", pf[8], pf[6], F_.Identity, scale=4.0, bias=pf[7])
    for j, (a, sc, b) in enumerate((
            (6, 32.0, 0.0), (5, 32.0, 0.0),
            (8, 1.0, 3.0), (7, 1.0, pf[5]),
            (4, 1.0, pf[0]), (7, 1.0, 15.0),
            (4, 0.25, pf[0]), (3, 32.0, pf[0]),
            (0, -1.0 / 16, 160 + 15.0 / 16 - 0.46875), (5, 1.0, -2.0), (4, 1.0 / 128, pf[1]))):
        act("pf0 pf3 pf7 pf8", "pcs", pc[11 + j], pf[a], F_.Relu if j == 9 else F_.Identity, scale=sc, bias=b)
    act("pcs", "pc20", pc[20], pc[20], F_.Identity, scale=-1024.0, bias=1024.0)
    act("pcs", "pc22", pc[22], pc[21], F_.Identity, scale=2.0, bias=1.0)
    act("pf3 pcs", "pc18", pc[18], pf[4], F_.Identity, scale=0.25, bias=pc[18])
    act("pf9", "pc6", pc[6], pf[9], F_.Identity, scale=-1.0, bias=1.0)
    act("m3", "pc5", pc[5], m0, F_.Identity, bias=m1)
    act("pc22 m3", "pc23", pc[23], pc[22], F_.Identity, scale=m0, bias=-1.0)
    wait("y", "skey", count["skey"])
    dmas("lval", "", "vs", [("y", c_("vs", j * 512, 512), T.val[32 * d:32 * d + 32, :]) for j, d in enumerate(others)])

    for key, a, n in (("ks", 0, 512), ("kl", 512, 1536)):
        op("v", "tab pay " + key, "wz0 wrow tab", V.tensor_copy, c_("win", SH, 16384).indirect(T[key][:]), c_("pay", a, n))
    one = c_("one", 0, 128)
    sel("one", "I1", T.I1[:], one, [[-1, 128]], EQ, 0.0, 0, 1)
    iota("J", T.J[:], [[1, 176]])
    iota("iC", c_("iC", 0, 16), [[0, 16]], 999)
    iota("iC", c_("iC", 16, 128), [[64, 2], [0, 4], [1, 16]])
    sel("one", "N1", c_("N1"), one, [[-16, 8], [0, 16]], GE, 0.0, 0, 1)
    iota("i3", T.i3[:], [[0, 32], [1, 4]])
    sel("N1", "NW", c_("NW"), c_("N1"), [[16, 8], [0, 16]], GE, 0.0, 15, -1)
    iota("i4", T.i4[:], [[16, 8]], 1)
    sel("NW", "RW", c_("RW"), c_("NW"), [[-1, 128]], GE, 0.0, 0, 1)
    sel("NW", "LT", c_("LT"), c_("NW"), [[1, 128]], GE, 0.0, -1, -1)
    sel("NW", "GT", c_("GT"), c_("NW"), [[-1, 128]], GE, 0.0, -1, 1)

    def spread(s, names, rows):
        dmas(s, "tab", names, [("y", c_(nm, x * 512, 512), win[row::16, SH + x * 8192:SH + x * 8192 + 8192])
                               for nm, row in zip(names.split(), rows) for x in range(2)])

    def windows(s, r, rs):
        dmas(s, r, s, [("y", T.vw[c * 32:c * 32 + 32, (k - q) % 4 * 2048:(k - q) % 4 * 2048 + 2048],
                        T.val[32 * k:32 * k + 32, :] if q == k else T.vl[q]) for q in rs for c in range(4)])

    def identities(pairs):
        for nm, c in pairs:
            sel("zt", nm, c_(nm), c_("zt"), [[-1, 128]], A_.not_equal, c, 0, 1)

    for j in range(16):
        a, q = ((j & 1) * 2 + (j >> 3)) * 128, (j >> 1) & 3
        mms("B5", c_("B5", j * 32, 32), [("FS tlown tlrem", c_("FS", a + 16 - 8 * f, 128), c_("tl", f * 128 + q * 32, 32)) for f in range(2)])
    act("pay", "SG0", T.SG[:, 0::3, :], c_("pay", 0, 512), F_.Identity, scale=0.0)
    act("pay", "clr", c_("clr", 0, 768), c_("pay", 0, 768), F_.Identity, scale=0.0)
    act("B5", "FW", c_("FW"), T.B5[:])
    act("FW lrown lr", "FG", c_("FG"), c_("FW").indirect(T.lr[:]))
    spread("wrp", "pt", [2])
    spread("wrh", "ht lt", [0, 1])
    iota("zt", c_("zt"), [[0, 128]])
    identities((("I15", -15.5), ("I4k", 4096.0), ("I512", 512.0)))
    deps("g", ["pt"], [], None)
    send("sval", "aval", "vs", [(d, c_("vs", j * 512, 512), T.vl[k]) + E3[j] for j, d in enumerate(others)])
    arrives("aval", 16, "vl")
    identities((("I32", -32.0), ("I480", -480.0), ("In", -1.0)))
    iota("iE", T.iE[:], [[0, 4], [128, 32]])
    iota("rest", c_("rest"), [[0, AT["rest"][1]]])
    for h in range(2):
        iota("ub0", c_("ub", h * 208 + 160, 48), [[0, 48]])
    iota("rA", c_("rA", 80, 80), [[-1, 80]], -160)
    iota("rA", c_("rA", 0, 80), [[1, 80]], 163)
    windows("lown", "pt", [k])
    fill("B0", T.B0[:, 2:96:3])
    fill("Of0", c_("Of", 0, 16))
    fill("GWp", T.GW[:, 0:137:136])
    fill("GWp", T.GW[:, 129:266:136])
    fill("pres0", T.pres[:, 0:137:136])
    ts2("iC pf3 pc9", "MW", c_("MW"), T.iC[:], pf[4], pc[9], EQ, MUL)
    tr("FG", "Fe", c_("Fe"), c_("FG"))
    act("Fe", "SG1", T.SG[:, 1::3, :], c_("Fe"), F_.Sign, bias=-15.5)
    act("Fe", "SG1", T.SG[:, 2::3, :], c_("Fe"), F_.Exp, scale=-LN2, bias=-LN2)
    for j in range(16):
        mm("I1 Fe", "B5", c_("B5", j * 32, 32), T.I1[:], c_("Fe", (j >> 2 & 1) * 8 + (j >> 3) * 4 + (j & 3), None, 16), True, True)
    for j in range(4):
        act("B5 pcs", "fb", c_("fb", j * 128, 128), c_("B5", j * 128, 128), F_.Identity, scale=2.0, bias=pc[11 + (j & 1)])
    act("B5", "sg", c_("sg"), T.B5[:], F_.Sign, bias=-15.5)
    ts2("J pcs", "ME", c_("ME"), c_("J", 0, 176), -48.0, pc[15], ADD, EQ)
    ts2("J pcs", "P2", T.P2[:], c_("J", 0, 144), -12.0, pc[14], ADD, EQ)
    ts1("J pcs", "P1", T.P1[:], c_("J", 0, 144), pc[13], EQ)
    ts2("i3 pf3", "c4", c_("c4"), T.i3[:], pf[5], 128.0, EQ, MUL)
    ts2("i4 pf0", "TB0", c_("TB", 8, 8), T.i4[:], pf[0], 16.0, ADD, MUL)
    tt("P1", "E1", c_("E1", 0, 143), c_("P1", 0, 143), c_("P1", 1, 143), SUB)
    tt("P2", "E2", c_("E2", 0, 140), c_("P2", 0, 140), c_("P2", 4, 140), SUB)
    ts1("TB0", "TB", c_("TB", 0, 8), c_("TB", 8, 8), -0.5, ADD)
    tt("c4 GT", "Ta", T.Ta[:], c_("c4"), c_("GT"), MUL)
    ts1("J pf3", "lm", c_("lm", 0, 2), c_("J", 0, 2), pf[3], EQ)
    ts1("J pcs", "Z", T.Z[:], c_("J", 0, 32), pc[17], EQ)
    ts1("J pc23", "Cp", T.Cp[:], c_("J", 0, 144), pc[23], EQ)
    ts1("J pc18", "Pm", T.Pm[:], c_("J", 0, 64), pc[18], EQ)
    ts2("J pcs pc5", "Hm", T.Hm[:], c_("J", 0, 144), pc[16], pc[5], EQ, MUL)

    mms("B0", T.B0[:, 1:192:3], [("one", T.one[0:1, 0:128], T.one[0:1, 0:64])] +
        [("MW pt", c_("MW", 16 - x, 128), c_("pt", x, None, 16)) for x in range(16)])
    mm("one SG0", "B7", T.B7[:], T.one[0:1, 0:128], T.SG[0:1, 0::3, :], True, False)
    ts2("B0", "B0 M", T.B0[:, 0:96:3], T.B0[:, 97:192:3], 131072.0, 65536.0, ADD, MUL)

    def merge(j, b):
        nm = ("ht", "lt")[j >> 1]
        for x in range((j & 1) * 8, (j & 1) * 8 + 8):
            mm("ME " + nm, "B7", T.B7[:, (j >> 1) * 256 + (x >> 2):(j >> 1) * 256 + 256:4], c_("ME", 48 - 16 * (x & 3), 128), c_(nm, x, None, 16),
               False, j == 3 and x == 15)

    def wipe(j, b):
        if j == 2:
            return scaled("Cp", "Cn", -1.0)
        act("pay", "clr", c_("clr", 768 + j * 640, 640), c_("pay", 0, 640), F_.Identity, scale=0.0)

    def evac(h, b):
        act("B7", "mg", T.mg[:], T.B7[:])

    def table(h, b):
        dmas("unw", "mg", "tab lk tlown tlrem " + " ".join(AT), [("y", win[c * 32 + x:c * 32 + 32:16, 0:16384], c_("mg", x * 256, 256))
                                                                 for c in range(4) for x in range(2)])
        windows("lwin", "vl", others)

    def scale(h, b):
        if h == 0:
            act("NW pc6", "Of", c_("Of", 16, 112), c_("NW", 0, 112), F_.Identity, scale=pc[6])
            return act("NW m3", "Rb", c_("Rb"), c_("NW"), F_.Identity, scale=m0)
        scaled("P2", "P2k", 4096.0)
        act("E2", "E2k", c_("E2k", 0, 140), c_("E2", 0, 140), F_.Identity, scale=4096.0)
        for nm, c in (("Tb", 4096.0), ("nA", -1.0), ("nB", -4096.0)):
            scaled("Ta", nm, c)

    def open_(h, b):
        mms(b[2], c_(b[2], 0, 256), [("I1 fb", T.I1[:], c_("fb", h * 256, 256)), ("I15 sg", c_("I15"), c_("sg", h * 256, 256))], stop=False)

    def pick(h, b, f):
        for j in range(4):
            scan("SG0 SG1 M B0", b[1 + 3 * f], c_(b[1 + 3 * f], j * 96, 96), T.SG[:, :, f * 8 + h * 4 + j], c_("B0", 0, 96), 0.0, MUL, MAX)

    def round_(h, b, f):
        x, a = b[1 + 3 * f], h * 256 + f * 128
        if h == 0:
            return ts2(x, "rr0%d" % f, c_("rr", a, 128), c_(x, 2, 382, 3), EVEN, -EVEN, ADD, ADD)
        act(x, "rq%d" % f, c_("rr", 512 + f * 128, 128), c_(x, 2, 382, 3), F_.Identity, bias=EVEN)
        act("rq%d" % f, "rr1%d" % f, c_("rr", a, 128), c_("rr", 512 + f * 128, 128), F_.Identity, bias=-EVEN)

    def test(h, b, f):
        x = b[1 + 3 * f]
        tt("rr%d%d %s" % (h, f, x), "bt" + b[0] if f else x, c_("bt", h * 128, 128) if f else c_(x, 384, 128), c_(x, 2, 382, 3),
           c_("rr", h * 256 + f * 128, 128), LT_)

    def both(h, b):
        tt(b[1] + " bt" + b[0], "pres" + b[0] * 2, c_("pres", 1 + h * 136, 128), c_(b[1], 384, 128), c_("bt", h * 128, 128), MUL)
        r = " pres0 pres" + b[0] * 2
        act(r, "tot" + b[0], c_("junk", 1280 + h * 128, 128), c_("pres", h * 136 + 1, 128), accum_out=c_("tot", h, 1))
        mm("RW" + r, b[1], c_(b[1], 128, 129), c_("RW"), c_("pres", h * 136, 129), True, False)
        mm("LT" + r, b[1], c_(b[1], 128, 128), c_("LT"), c_("pres", h * 136 + 1, 128), False, True)

    def flag(h, b):
        for f in range(2):
            mm("I4k pres" + b[0] * 2, b[2], c_(b[2], f * 128, 128), c_("I4k"), c_("pres", h * 136 + 1, 128), False, False)

    def total(h, b):
        mm("Of Of0 tot" + b[0], b[1], c_(b[1], 260, 1), T.Of[:], c_("tot", h, 1), True, True)

    def route(h, b, nm, r, a):
        for f in range(2):
            mm("%s %s%d" % (nm, r, h), b[2], c_(b[2], f * 128, 128), c_(nm), c_(r, a, 128), False, r == "r4" and f == 1)

    def number(h, b):
        scan("one " + b[1], "s1" + b[0], c_("s1", h * 136, 129), c_("one", 0, 129), c_(b[1], 128, 129), c_(b[1], 260, 1), MUL, ADD)
        route(h, b, "I512", "s1", h * 136)

    def floor(h, b):
        for nm, r, c in (("I32", "r16", 24576 - 7.5), ("I480", "r4", 6144 - 1.5)):
            ts1("s1" + b[0], r + b[0], c_(r, h * 128, 128), c_("s1", h * 136, 128), c, ADD)
            route(h, b, nm, r, h * 128)

    def rows(h, b):
        mm("Rb s1" + b[0], "B0", c_("B0", 128 + h * 136, 129), c_("Rb"), c_("s1", h * 136, 129), True, True)

    def held(h, b):
        act("B0 pcs", "Gb" + b[0], c_("Gb", h * 144, 129), c_("B0", 128 + h * 136, 129), F_.Identity, scale=1.0 / 16, bias=pc[19])

    def kept(h, b):
        mms(b[2], c_(b[2], 256, 128), [("I1 Gb" + b[0], T.I1[:], c_("Gb", h * 144 + 1, 128)), ("In", T.In[:], c_("Gb", h * 144, 128))])

    def keep(h, b):
        act(b[2], "keep" + b[0], c_("keep", h * 128, 128), c_(b[2], 256, 128), F_.Identity, scale=-1.0, bias=1.0)

    def count_(h, b, js=(2, 3, 4)):
        for j in js:
            act("B0 TB", "acc" + b[0], c_("junk", j * 256 + h * 128, 128), c_("B0", 129 + h * 136, 128), F_.Sign, scale=-1.0, bias=c_("TB", j, 1),
                accum_out=c_("acc", h * 8 + j, 1))

    def stage1(h, b, j):
        mm("P1 E1 U%d%d" % (h, j), b[1], c_(b[1], 0, 256), c_("E1" if j else "P1", 3 - j, 128), c_("U", h * 1024 + j * 256, 256), j == 0, j == 3)

    def step(h, b):
        ts2(b[2], "U%d0" % h, c_("U", h * 1024, 256), c_(b[2], 0, 256), Z0, 0.0, ADD, MAX)
        stage1(h, b, 0)

    def steps(h, b):
        for j in range(1, 4):
            ts2("U%d0" % h, "U%d%d" % (h, j), c_("U", h * 1024 + j * 256, 256), c_("U", h * 1024, 256), -512.0 * j, 0.0, ADD, MAX)
            stage1(h, b, j)

    def signs(h, b):
        for j in range(3):
            act(b[2], "Gs%d%d" % (h, j), c_("Gs", h * 384 + j * 128, 128), c_(b[2], 0, 128), F_.Sign, bias=Z0 + 0.5 - 512.0 * (j + 1))

    def junk(h, b):
        mms("B3", c_("B3", h * 128, 128), [("P1 Gs%d%d" % (h, j), c_("P1", 3 - j, 128), c_("Gs", h * 384 + j * 128, 128)) for j in range(3)])

    def excess(h, b):
        ts2("B3 pc20", "Jb" + b[0], c_("Jb", h * 128, 128), c_("B3", h * 128, 128), 256.0, pc[20], MUL, ADD)

    def again(h, b):
        mms(b[3], c_(b[3], 0, 128), [("one iE", T.one[0:1, 0:128], T.iE[0:1, :])] +
            [("Gb%d %s" % (h, nm), T[nm][:], c_("Gb", h * 144 + x, 128)) for x, nm in ((0, "Ta"), (0, "Tb"), (1, "nA"), (1, "nB"))], stop=False)

    def anew(h, b):
        for f in range(2):
            tt("%s Jb%d" % (b[1], h), "V%d0%d" % (h, f), c_("V", h * 1024 + f * 128, 128), c_(b[1], f * 128, 128), c_("Jb", h * 128, 128), SUB)
            mm("P2 P2k V%d0%d" % (h, f), b[3], c_(b[3], 0, 128), c_(("P2", "P2k")[f], 12, 128), c_("V", h * 1024 + f * 128, 128), False, False)

    def spread_(h, b):
        for j in range(1, 4):
            ts2("V%d00 V%d01" % (h, h), "V%d%d" % (h, j), c_("V", h * 1024 + j * 256, 256), c_("V", h * 1024, 256), -128.0 * j, 0.0, ADD, MAX)
            for f in range(2):
                mm("E2 E2k V%d%d" % (h, j), b[3], c_(b[3], 0, 128), c_(("E2", "E2k")[f], 12 - 4 * j, 128), c_("V", h * 1024 + j * 256 + f * 128, 128),
                   False, j + f == 4)

    def carry(h, b):
        scan("keep%d %s" % (h, b[3]), "GW" + b[0], c_("GW", 1 + h * 136, 128), c_("keep", h * 128, 128), c_(b[3], 0, 128), 0.0, MUL, MAX)

    def lists(h, b):
        for j in range(2):
            ts2("acc" + b[0], "gl%d%d" % (h, j), c_("gl", 12 * h + 5 * j, 5), c_("acc", 8 * h, 5), 0.5, 65.0 - j, MUL, ADD)

    def outside(h, b):
        act("Gb" + b[0], "Ge" + b[0], c_("Gb", h * 144 + 129, 1), c_("Gb", h * 144 + 128, 1), F_.Identity, bias=1.0)
        act("rA Gb" + b[0], "out" + b[0], c_("out", h * 80, 80), c_("rA", 80, 80), F_.Relu, bias=c_("Gb", h * 144, 1))

    def over(h, b):
        act("Gb%d Ge%d gl%d0" % (h, h, h), "Fg" + b[0], c_("Fg", h * 80, 80), c_("Gb", h * 144, 144).indirect(c_("gl", 12 * h, 5)))

    def beyond(h, b):
        mm("one rA", "B3", c_("B3", 256, 160), T.one[0:1, 0:128], T.rA[0:1, :], True, False)
        for j, (nm, r) in enumerate((("I480", "out"), ("I480", "out"), ("In", "Fg"), ("I1", "Fg"))):
            mm("%s %s%d" % (nm, r, h), "B3", c_("B3", 256 + (j & 1) * 80, 80), T[nm][:], c_(r, h * 80, 80), False, j == 3)

    def under(h, b):
        act("B3", "om" + b[0], c_("om", h * 160, 160), c_("B3", 256, 160), F_.Relu, bias=-1.0)

    def close(h, b):
        tt("GW%d GWp gl%d0 gl%d1 om%d" % (h, h, h, h), "g%d0 g%d1" % (h, h), c_("g1", h * 240, 160),
           c_("GW", h * 136, 136).indirect(c_("gl", 12 * h, 10)), c_("om", h * 160, 160), MUL)

    def join(h, b):
        tt("g%d0 g%d1" % (h, h), "g%d2" % h, c_("g1", h * 240 + 160, 80), c_("g1", h * 240, 80), c_("g1", h * 240 + 80, 80), ADD)

    def move(h, b):
        for j in range(2):
            ts1("lm g%d2" % h, "zp" + b[0], T.zp[:, 4 * h:4 * h + 4, j * 20:j * 20 + 20], c_("g1", h * 240 + 160, 80),
                c_("lm", order[2 * h + j] & 1, 1), MUL)
        for c in range(4):
            mm("Z zp" + b[0], "B7", T.B7[32 * c:32 * c + 32, h * 64:h * 64 + 40], T.Z[:], T.zp[:, 4 * h + c, :], True, True)

    def name(h, b, x):
        u, g2, r = [c_("u2", h * 240 + j * 80, 80) for j in range(3)], c_("g1", h * 240 + 160, 80), "g%d2" % h
        if x == 0:
            ts2(r, "e0" + b[0], u[0], g2, 1.0 / 32, -0.484375, MUL, ADD)
            ts1(r, "c2" + b[0], c_("u3", h * 80, 80), g2, 0.0, EQ)
        elif x == 1:
            ts1("e0" + b[0], "a3" + b[0], u[1], u[0], 127, AND)
            ts1("e0" + b[0], "a4" + b[0], u[2], u[0], 12, SHR)
        else:
            ts1("a3" + b[0], "ub" + b[0] * 2, c_("ub", h * 208, 80), u[1], 4.0, MUL)
            tt("a4%d c2%d" % (h, h), "ub" + b[0] * 2, c_("ub", h * 208 + 80, 80), u[2], c_("u3", h * 80, 80), SUB)

    def turn(h, b):
        for d in order[2 * h:2 * h + 2]:
            for x in range(2):
                a = 4 * (d & 1) + 2 * x
                mms("B0", c_("B0", d * 40 + 32 + 4 * x, 4), [("Cp s1" + b[0], c_("Cp", a, 128), c_("s1", h * 136 + 32, 97, 32)),
                                                           ("Cn", c_("Cn", a, 128), c_("s1", h * 136, 97, 32))])
            mms("B0", c_("B0", d * 40, 32), [("one", T.one[0:1, 0:128], T.one[0:1, 0:32])] +
                [("Pm ub0 ub" + b[0] * 2, c_("ub", h * 208 + x * 80, 128), c_("Pm", (d & 1) * 32, 32)) for x in range(2)])

    def seconds(h, b):
        ts2("B7", "ll0" + b[0], c_("ll", h * 40, 40), c_("B7", h * 64, 40), 1.0 / 32, -0.484375, MUL, ADD)

    def firsts(h, b, x):
        u, word = [c_("u2", 480 + h * 160 + j * 40, 40) for j in range(4)], c_("B7", h * 64, 40)
        if x == 0:
            ts2("B7", "a0" + b[0], u[0], word, 1.0 / 32, -0.484375, MUL, ADD)
            ts1("B7", "u1" + b[0], u[1], word, 128.0, MUL)
        elif x == 1:
            ts1("a0" + b[0], "a2" + b[0], u[2], u[0], 0x307F, AND)
            ts1("u1" + b[0], "a1" + b[0], u[3], u[1], 0xF80, AND)
        elif x == 2:
            tt("a1%d a2%d" % (h, h), "c1" + b[0], c_("u3", 160 + h * 40, 40), u[2], u[3], ADD)
        else:
            cp("c1" + b[0], "ll1" + b[0], c_("ll", 80 + h * 40, 40), c_("u3", 160 + h * 40, 40))
    lw = c_("win", 0, 16384)

    def look(f, j, h):
        f("ll%d%d lk" % (h, j >> 1), "LK%d%d" % (j, h), c_("LK", j * 640 + h * 320, 320), lw.indirect(c_("ll", h * 80 + j * 20, 20)))

    def wrap(j, hs):
        b, a, n = ("B1", "B5", "B6", "B4")[j], j * 640 + hs[0] * 320, 320 * len(hs)
        mms(b, c_(b, hs[0] * 20, n // 16), [("Hm " + " ".join("LK%d%d" % (j, h) for h in hs), c_("Hm", 15 - x, 128), c_("LK", a + x, n - x, 16))
                                            for x in range(16)])

    def lst(j, hs):
        b = ("B1", "B5", "B6", "B4")[j]
        ts1(b, " ".join("lo%d%d" % (j, h) for h in hs), c_("lo", j * 40 + hs[0] * 20, 20 * len(hs)), c_(b, hs[0] * 20, 20 * len(hs)), -64.0, ADD)

    def second(j, b):
        act("lo%d0 lown lwin" % j, "t2%d" % j, c_("t2", j * 320, 320), T.vw[:].indirect(c_("lo", j * 40, 20)))

    def first(j, b):
        d = order[j]
        tt("lo%d1 lown lwin t2%d" % (j, j), "Y%d" % d, c_("Y", j * 320, 320), T.vw[:].indirect(c_("lo", j * 40 + 20, 20)),
           c_("t2", j * 320, 320), SUB)
        if d != k:
            send("sy%d" % d, "ay%d" % k, "Y%d" % d, [(d, c_("Y", j * 320, 320), c_("YL", k * 320, 320), 0, 16)])

    def entities(h, b):
        act("B0", "wS", T.wS[:], c_("B0", 0, 160))
        send("swho", "awho", "wS", [(d, c_("wS", d * 40, 40), c_("wL", k * 40, 40), 4 * j, 4 * j + 4) for j, d in enumerate(others)])
        arrives("awho", 12, "wL")

    def told(h, b):
        nm = ("wS", "wL")[h]
        dmas("who%d" % (h + 1), nm, "", [it for kk in ([k], others)[h] for c0 in [kk * 40]
                                         for it in (("y", T.who[2 * kk:2 * kk + 1, :], T[nm][0:80, c0:c0 + 16]),
                                                    ("y", T.who[2 * kk + 1:2 * kk + 2, :], T[nm][0:80, c0 + 16:c0 + 32]),
                                                    ("y", T.cnt[2 * kk:2 * kk + 2, :], T[nm][0:2, c0 + 32:c0 + 40]))])

    def store(j, b):
        r = order[j]
        nm, c0 = ("Y", 960) if r == k else ("YL", r * 320)
        if r != k:
            arrives("ay%d" % r, 16, "YL%d" % r)
        dmas("st%d" % r, nm + str(r), "", [("ys"[c & 1], T.y[32 * r:32 * r + 32, c * 320:c * 320 + 320],
                                            T[nm][c * 32:c * 32 + 32, c0:c0 + 320]) for c in range(4)])
    named = {"both": both, "number": number, "floor": floor, "rows": rows, "kept": kept, "count": count_, "step": step, "steps": steps,
             "signs": signs, "excess": excess, "again": again, "spread": spread_, "carry": carry, "lists": lists, "over": over, "junk": junk,
             "keep": keep, "held": held, "anew": anew, "scale": scale, "merge": merge, "evac": evac, "table": table, "wipe": wipe, "open": open_,
             "tally": lambda h, b: count_(h, b, (0, 1)), "total": total, "outside": outside, "close": close, "move": move, "turn": turn,
             "seconds": seconds, "second": second, "flag": flag, "beyond": beyond, "under": under, "told": told, "join": join, "first": first,
             "entities": entities, "store": store}
    for nm, f in (("pick", pick), ("round", round_), ("test", test), ("name", name), ("first", firsts)):
        for x, c in enumerate("abcd"):
            named[nm + c] = lambda h, b, f=f, x=x: f(h, b, x)
    for nm, f in (("wrap", wrap), ("list", lst)):
        for c, hs in (("", [0, 1]), ("a", [1]), ("b", [0])):
            named[nm + c] = lambda j, b, f=f, hs=hs: f(j, hs)
    for nm, f in (("S", act), ("V", cp)):
        for c, x in (("a", 1), ("b", 0)):
            named[nm + c] = lambda j, b, f=f, x=x: look(f, j, x)
    for st in STEPS.split():
        h = int(st[-1])
        named[st[:-1]](h, (str(h), "B%d" % (1 + h), "B%d" % (4 + 2 * h), "B%d" % (5 - h), "B%d" % (3 + 2 * h)))
    for s in count:
        wait("g", s, count[s])
